import numpy as np, ml_dtypes
CORES = [3,11,19,27,35,43,51,59]
N = 8
BF = ml_dtypes.bfloat16
def gentries(a):
    return np.ascontiguousarray(a.reshape(8, 16, -1).transpose(0, 2, 1)).reshape(8, -1)
def gtable(e):
    e = np.asarray(e); return np.ascontiguousarray(e.reshape(8, -1, 16).transpose(0, 2, 1)).reshape(128, -1).astype(np.int32)
GW, GH, M, RO, HP = 128, 32, 1024, 2, 3
W, D = GW * GH, 511
def parts(rng):
    s = np.exp2(rng.permutation(np.arange(16) % 3 - 1)).astype(np.float32).reshape(1, 1, 16, 1)
    x = s * np.exp2(2 * rng.random((N, 8, 16, W), dtype=np.float32) - 1)
    eps = s * (0.17 + 0.34 * rng.random((N, 8, 16, 1)))
    fl = np.where(rng.random((N, 8, 1, W)) < 0.6, rng.integers(-48, 49, (N, 8, 4, W)), rng.integers(-D, D + 1, (N, 8, 4, W)))
    cor = rng.integers(0, W, (N, 8, 4, W))
    ms = np.ascontiguousarray(np.argsort(rng.random((N, 8, W)), axis=-1)[..., :M])
    return x, eps, fl, cor, ms
def pack(x, eps, fl, cor, ms):
    return {"x": np.clip(x, 2.0 ** -20, 4.0).astype(BF).reshape(N, 128, W), "eps": np.ascontiguousarray(eps).astype(np.float32).reshape(N, 128, 1),
            "fl": np.ascontiguousarray(fl.transpose(0, 2, 1, 3)).astype(np.int32).reshape(N, 32, W),
            "cor": np.stack([gtable(a.reshape(8, -1)) for a in cor]), "ms": np.stack([gtable(a) for a in ms])}
def setup_inputs(rng):
    return pack(*parts(rng))
def setup_inputs_calm(rng):
    x, eps, fl, cor, ms = parts(rng)
    v = (np.arange(N).reshape(N, 1, 1, 1) + np.arange(8).reshape(1, 8, 1, 1) + np.arange(4).reshape(1, 1, 4, 1)) % 4
    fl = v * np.where(rng.random((N, 8, 4, W)) < 0.5, 1, -1) * (rng.random((N, 8, 1, W)) < 0.8)
    return pack(x, eps, fl, cor, ms)
def setup_inputs_corners(rng):
    x, eps, fl, cor, ms = parts(rng); sh = int(rng.integers(0, 6)); clear = int(rng.integers(0, 8)); own = np.arange(W)
    for q in range(N):
        o = rng.permutation(8); u = [int(v) for v in rng.permutation(8)]
        j = u.index(2 + q % 3); u[j], u[clear] = u[clear], u[j]
        for g in range(8):
            k = 0 if g == clear else (q + g + sh) % 6
            if k in (1, 4):
                m = ms[q, g]; ms[q, g] = rng.permutation(np.concatenate([np.array([0, W - 1]), m[(m != 0) & (m != W - 1)]])[:M])
            m = ms[q, g]; there = np.ones(W, bool); there[m] = False; kno = np.flatnonzero(there)
            if k == 0: cor[q, g] = rng.choice(kno, (4, W))
            if k == 1:
                c = rng.choice(kno, (4, W)); c[rng.integers(0, 4, W), own] = rng.choice(m, W); cor[q, g] = c
            if k == 2: cor[q, g] = own
            if k == 3: cor[q, g] = rng.choice(np.array([0, W - 1]), (4, W))
            if k == 4: cor[q, g] = rng.choice(m, (4, W))
            if o[g] == 0: fl[q, g] = 0
            if o[g] == 1: fl[q, g] = rng.choice(np.array([-D, D]), (4, W))
            if o[g] == 2: fl[q, g] = rng.choice(np.array([-D, 0, D]), (4, W))
            n = (0, 8, 9, 15, 16, -1, -1, -1)[u[g]]
            if n >= 0: eps[q, g, :, 0] = rng.permutation(np.where(np.arange(16) < n, 4.0, 0.0))
    return pack(x, eps, fl, cor, ms)
def setup_inputs_ends(rng):
    x, eps, fl, cor, ms = parts(rng); h = M // 2; tips = np.array([0, GW - 1, W - GW, W - 1])
    x = np.where(rng.random(x.shape) < 0.5, np.float32(4), np.float32(2.0 ** -20))
    m = rng.random((N, 8, 1, W)) < 0.8; m[..., tips] = True
    fl = np.where(m, np.where(rng.random(fl.shape) < 0.5, D, -D), fl)
    cor = np.where(rng.random((N, 8, 1, W)) < 0.75, np.where(rng.random(cor.shape) < 0.5, 0, W - 1), cor)
    top = np.where(np.arange(16) % 2 == 0, 4.0, 4.0 - 2.0 ** -20)
    for q in range(N):
        o = rng.permutation(8)
        for g in range(8):
            lo, hi = (1, 1, 1, 1, 0, 1, 0, 0)[g], (1, 1, 1, 1, 0, 0, 1, 0)[g]
            s = np.concatenate([np.arange(lo, lo + h), np.arange(W - hi - h, W - hi)])
            ms[q, g] = np.concatenate([s[:1], rng.permutation(s[1:-1]), s[-1:]])
            if g >= 4 and q % 2 == 1: cor[q, g][:, tips[[0, 3]]] = rng.integers(h + 1, W - 1 - h, (4, 2))
            n = (16, 9, 8, 9, 8, 7, 12, 0)[int(o[g])]
            eps[q, g, :, 0] = rng.permutation(np.where(np.arange(16) < n, top, 0.0))
    return pack(x, eps, fl, cor, ms)
def setup_inputs_spread(rng):
    x, eps, fl, cor, ms = parts(rng)
    x = np.exp2(2 * rng.random((N, 8, 16, W), dtype=np.float32) - 1) * np.exp2(rng.integers(-1, 2, (N, 8, 1, W))).astype(np.float32)
    eps = np.exp2(4 * rng.random((N, 8, 16, 1)) - 2.5)
    fl = rng.integers(-D, D + 1, (N, 8, 4, W))
    v = np.minimum(np.exp2(rng.random((N, 4, 4, W)) * np.log2(D)).astype(np.int64), D)
    fl[:, 1::2] = v * np.where(rng.random((N, 4, 4, W)) < 0.5, 1, -1)
    cor[:, ::2] = np.minimum((W * rng.random((N, 4, 4, W)) ** 3).astype(np.int64), W - 1)
    return pack(x, eps, fl, cor, ms)
def setup_inputs_ties(rng):
    x, eps, fl, cor, ms = parts(rng)
    x = rng.integers(1, 9, (N, 8, 16, W)).astype(np.float32) * np.float32(0.5)
    eps = rng.choice(np.array([0.0, 1.0 - 2.0 ** -24, 1.0, 1.5, 2.0]), (N, 8, 16, 1))
    fl = np.where(rng.random((N, 8, 1, W)) < 0.8, np.maximum(fl // 4 * 4, 3 - D), fl)
    own = np.arange(W); pool = np.flatnonzero((own % GW % 2 == 0) & (own // GW % 2 == 0))
    for i, g in enumerate([int(v) for v in rng.permutation(8)[:3]]):
        pix = rng.permutation(pool)[:M]; kno = np.setdiff1d(own, pix); fx, fy = [int(v) for v in rng.integers(1, 4, 2)]
        x[:, g] = (128 + rng.integers(0, 128, (16, W))) * np.exp2(np.where(rng.random((16, W)) < 0.5, rng.integers(-8, -5, (16, W)), rng.integers(-27, -24, (16, W))))
        eps[:, g] = 0; t = rng.choice(kno, (4, W)); v = fl[:, g]
        v[:] = np.array([fx, fy, fx, fy + 4]).reshape(4, 1)
        if i == 0:
            n = M // 3; a, b, c = pix[:n], pix[n:2 * n], pix[2 * n:3 * n]
            t[:, a + GW] = t[:, a]; t[:, b + GW] = t[:, a]; t[:, c + GW] = t[:, a]
            t[:, b] = a; t[:, c] = b
        else:
            v[:, :, pix + (1, GW)[i - 1]] = np.array([fx + 4, fy, fx + 4, fy]).reshape(4, 1)
        cor[:, g] = t
        for q in range(N): ms[q, g] = rng.permutation(pix)
    return pack(x, eps, fl, cor, ms)
def check_ranges(d):
    bad = []
    for k, lo, hi in (("x", 2.0 ** -20, 4), ("eps", 0, 4), ("fl", -D, D), ("cor", 0, W - 1), ("ms", 0, W - 1)):
        v = np.asarray(d[k]).astype(np.float64)
        if not np.all((v >= lo) & (v <= hi)): bad.append("range of " + k)
    s = np.sort(np.stack([gentries(np.asarray(a)) for a in d["ms"]]), axis=-1)
    if np.any(s[..., 1:] == s[..., :-1]): bad.append("a number twice in a group of ms")
    return bad
def chase(a, way, xs, kn, fw, taps, mis, home):
    sg = 1 - 2 * way; lim = np.array([4 * GW - 1, 4 * GH - 1]).reshape(1, 2, 1)
    z = np.zeros((8, 16, M), np.float32); got = np.zeros((8, M), np.int64); end = np.zeros((8, 2, M), np.int64)
    pos = home[a]; step = np.take_along_axis(fw[a][:, 2 * way:2 * way + 2], mis[a][:, None, :], 2)
    for h in range(1, HP + 1):
        q = (a + sg * h) % N; gi = (np.arange(8) + sg * (h - 1)) % 8
        pos = np.minimum(np.maximum(pos + step, 0), lim)
        cell = (pos[:, 1] >> 2) * GW + (pos[:, 0] >> 2); part = (pos & 3).astype(np.float32) * np.float32(0.25)
        t = np.take_along_axis(taps[q][gi], cell[:, None, :], 2).reshape(8, 4 * M)
        ok = np.all(np.take_along_axis(kn[q][gi], t, 1).reshape(8, 4, M), axis=1)
        v = np.take_along_axis(xs[q][gi], t[:, None, :], 2).reshape(8, 16, 4, M)
        u0 = part[:, 0][:, None, :]; u1 = part[:, 1][:, None, :]
        up = v[:, :, 0] + u0 * (v[:, :, 1] - v[:, :, 0]); dn = v[:, :, 2] + u0 * (v[:, :, 3] - v[:, :, 2])
        w = up + u1 * (dn - up)
        new = ok & (got == 0)
        z = np.where(new[:, None, :], w, z); end = np.where(new[:, None, :], pos, end); got = np.where(new, h, got)
        step = np.take_along_axis(fw[q][:, 2 * way:2 * way + 2][gi], cell[:, None, :], 2)
    return z, got, end
def reference(x, eps, fl, cor, ms):
    xs = x.astype(np.float32).reshape(N, 8, 16, W); ep = eps.astype(np.float32).reshape(N, 8, 16, 1)
    fw = np.ascontiguousarray(fl.astype(np.int64).reshape(N, 4, 8, W).transpose(0, 2, 1, 3))
    taps = np.stack([gentries(a) for a in cor]).astype(np.int64).reshape(N, 8, 4, W); mis = np.stack([gentries(a) for a in ms]).astype(np.int64)
    kn = np.ones((N, 8, W), bool); np.put_along_axis(kn, mis, False, 2)
    mx = mis % GW; my = mis // GW; home = np.stack([4 * mx, 4 * my], axis=2)
    done = np.zeros((N, 8, M), bool); val = np.zeros((N, 8, 16, M), np.float32); ex = np.zeros((N, 8, 16, M), np.float64)
    for rnd in range(RO):
        ends = [(chase(a, 0, xs, kn, fw, taps, mis, home), chase(a, 1, xs, kn, fw, taps, mis, home)) for a in range(N)]
        nb = ((my + (0, 1, 0)[rnd]) % GH) * GW + (mx + (1, 0, GW - 1)[rnd]) % GW
        for a in range(N):
            (zf, gf, pf), (zb, gb, pb) = ends[a]
            both = (gf > 0) & (gb > 0); open_ = ~done[a]; dif = zf - zb; gap = np.abs(dif)
            agree = np.add.reduce((gap <= ep[a]).astype(np.int64), axis=1)
            won = both & open_ & (agree >= 9)
            ex[a] = np.where(open_[:, None, :], np.where(both[:, None, :], np.exp(-gap.astype(np.float64)), 0.0), ex[a])
            val[a] = np.where(won[:, None, :], zb + np.float32(0.5) * dif, val[a])
            cur = np.take_along_axis(fw[a], mis[a][:, None, :], 2); near = np.take_along_axis(fw[a], nb[a][:, None, :], 2)
            own = np.concatenate([(pf - home[a]) >> np.maximum(gf - 1, 0)[:, None, :], (pb - home[a]) >> np.maximum(gb - 1, 0)[:, None, :]], axis=1)
            new = np.where(won[:, None, :], own, np.where(open_[:, None, :], near, cur))
            done[a] = done[a] | won
            np.put_along_axis(fw[a], np.broadcast_to(mis[a][:, None, :], (8, 4, M)), new, 2)
            np.put_along_axis(kn[a], mis[a], done[a], 1)
            np.put_along_axis(xs[a], np.broadcast_to(mis[a][:, None, :], (8, 16, M)), val[a], 2)
    last = np.stack([np.take_along_axis(fw[a], mis[a][:, None, :], 2) for a in range(N)])
    yf = np.concatenate([last.transpose(0, 2, 1, 3).reshape(N, 32, M), done.astype(np.int64)], axis=1)
    return {"y": val.reshape(N, 128, M), "ye": ex.reshape(N, 128, M).astype(np.float32), "yf": yf.astype(np.float32)}

def check_inputs(d):
    bad = list(check_ranges(d))
    if not bad:
        for name, y in reference(**d).items():
            for q in range(N):
                v = np.abs(np.asarray(y[q], np.float64)); s = np.sqrt(np.mean(v * v))
                if v.max() > 8 * s or s < 2.0 ** -3: bad.append('%s of rank %d is uneven or too small' % (name, q))
    return bad

@@ -1,0 +1,892 @@
+from concourse.bass import DstId, RemoteDMATransfer
+from concourse.mybir import AluOpType as AL, ActivationFunctionType as AF
+
+F32, BF, I32, U16 = "float32", "bfloat16", "int32", "uint16"
+NF = 26
+ZF0, SN2, SN1 = 15360, 17408, 12288
+SCRATCH = {
+    "W1": ("sbuf", [128, 12288], BF), "W2": ("sbuf", [128, 13312], BF), "KB": ("sbuf", [128, 4096], BF),
+    "GB": ("sbuf", [128, 4096], BF), "XB": ("sbuf", [128, 12304], BF), "XF": ("sbuf", [128, 17416], F32),
+    "CL": ("sbuf", [128, 1024], U16),
+    "A0": ("sbuf", [128, 1024], F32), "A2": ("sbuf", [128, 1024], F32), "D0": ("sbuf", [128, 1024], F32),
+    "D2": ("sbuf", [128, 1024], F32), "SS": ("sbuf", [128, 1024], F32), "ZI0": ("sbuf", [128, 1024], F32),
+    "ZI1": ("sbuf", [128, 1024], F32), "DF": ("sbuf", [128, 1024], F32), "GP": ("sbuf", [128, 1024], F32),
+    "UU": ("sbuf", [128, 1024], BF), "VV": ("sbuf", [128, 1024], BF), "O0": ("sbuf", [128, 1024], BF),
+    "O1": ("sbuf", [128, 1024], BF), "NR": ("sbuf", [128, 1024], BF),
+    "CT": ("sbuf", [128, 1024], BF), "ZM": ("sbuf", [128, 7 * 144], BF), "MM": ("sbuf", [128, 8 * 128], BF),
+    "UC": ("sbuf", [128, 16], BF), "SL": ("sbuf", [128, 128], BF),
+    "IN": ("sbuf", [128, 144], F32), "CO": ("sbuf", [128, NF * 16], F32), "PC": ("sbuf", [128, 8], F32),
+    "PI": ("sbuf", [128, 8], I32), "EP": ("sbuf", [128, 4], F32), "LE": ("dram", [8, 128, 1], F32), "SE": ("dram", [2, 128, 1], F32),
+    "ED": ("sbuf", [128, 4], F32),
+    "MI": ("sbuf", [128, 64], I32), "HM": ("sbuf", [128, 256], I32), "JT": ("sbuf", [128, 64], I32),
+    "TI": ("sbuf", [128, 2048], I32), "TF": ("sbuf", [128, 256], F32),
+    "UL": ("sbuf", [128, 1344], U16),
+    "MS0": ("sbuf", [128, 192], I32), "MS1": ("sbuf", [128, 192], I32),
+    "EM0": ("sbuf", [128, 192], I32), "EM1": ("sbuf", [128, 192], I32),
+    "ST": ("sbuf", [128, 640], I32), "EN": ("sbuf", [128, 384], I32),
+    "SM": ("dram", [8, 128, 8], I32), "LM": ("dram", [8, 128, 8], I32),
+    "SC0": ("dram", [8, 128, 64], U16), "LC0": ("dram", [8, 128, 64], U16),
+    "SC1": ("dram", [8, 128, 64], U16), "LC1": ("dram", [8, 128, 64], U16),
+    "SF": ("dram", [16, 128, 128], BF), "LF": ("dram", [16, 128, 128], BF),
+    "SX": ("dram", [16, 128, 256], BF), "LX": ("dram", [8, 128, 256], BF),
+    "SH": ("dram", [8, 128, 64], F32), "LH": ("dram", [8, 128, 64], F32),
+    "SZ0": ("dram", [8, 128, 64], F32), "LZ0": ("dram", [8, 128, 64], F32),
+    "SZ1": ("dram", [8, 128, 64], F32), "LZ1": ("dram", [8, 128, 64], F32),
+    "SZ2": ("dram", [8, 128, 64], F32), "LZ2": ("dram", [8, 128, 64], F32),
+    "SZ3": ("dram", [8, 128, 32], F32), "LZ3": ("dram", [8, 128, 32], F32),
+    "SZ4": ("dram", [8, 128, 32], F32), "LZ4": ("dram", [8, 128, 32], F32),
+    "P0": ("psum", [128, 512], F32), "P1": ("psum", [128, 512], F32), "P2": ("psum", [128, 512], F32),
+    "P3": ("psum", [128, 512], F32), "P4": ("psum", [128, 512], F32), "P5": ("psum", [128, 512], F32),
+    "P6": ("psum", [128, 512], F32), "P7": ("psum", [128, 512], F32),
+}
+ARR = ["a_ms", "a_c0", "a_c1", "a_w1", "a_w2", "a_xb", "h_in", "h_z", "h_x", "h_fl", "h_f0", "h_f1", "h_f2", "h_f3", "h_f4", "h_f5", "a_fl", "a_eps", "a_st00", "a_st01", "a_st10", "a_st11", "a_en00", "a_en01",
+       "a_en10", "a_en11", "a_mh"] + ["a_z%d" % i for i in range(5)] + ["a_f%d" % i for i in range(5)]
+SEMAPHORES = ARR + ["e_v", "e_a", "e_p", "e_g"] + ["d%d" % i for i in range(100)]
+IO = {"x": [128, 4096], "eps": [128, 1], "fl": [32, 4096], "cor": [128, 1024], "ms": [128, 64],
+      "y": [128, 1024], "ye": [128, 1024], "yf": [40, 1024]}
+ALL = slice(None)
+CH = [(1, 0, 512), (1, 512, 1024), (0, 0, 512), (0, 512, 768), (0, 768, 1024)]
+
+
+def diag_ring(T, topo):
+    n = len(T.cores)
+    ch = [topo.chip(c) for c in T.cores]
+    best = [-1, list(range(n))]
+
+    def go(path, score):
+        if len(path) == n:
+            a, b = ch[path[-1]], ch[path[0]]
+            if topo.mates(a, b) or topo.same_plane(a, b):
+                s = score + (1 if topo.mates(a, b) else 0)
+                if s > best[0]:
+                    best[0], best[1] = s, list(path)
+            return
+        for r in range(n):
+            if r not in path:
+                a, b = ch[path[-1]], ch[r]
+                if topo.mates(a, b) or topo.same_plane(a, b):
+                    go(path + [r], score + (1 if topo.mates(a, b) else 0))
+    go([0], 0)
+    return best[1]
+
+
+def V(name, p=ALL, c=None, e=None):
+    return (name, (p,) if c is None else ((p, c) if e is None else (p, c, e)))
+
+
+def C(name, a, b, step=1):
+    return (name, (ALL, slice(a, b, step) if step != 1 else slice(a, b)))
+
+
+def IND(win, off):
+    return ("*", win, off)
+
+
+def region(v):
+    name, idx = v
+    shp = IO[name] if name in IO else SCRATCH[name][1]
+    p = idx[0]
+    ps = frozenset(range(*p.indices(shp[0]))) if isinstance(p, slice) else frozenset([p])
+    if name not in IO and SCRATCH[name][0] == "psum":
+        return (name, frozenset(range(128)), 0, 512, True)
+    if len(idx) > 1:
+        r = range(*idx[1].indices(shp[1]))
+        return (name, ps, r[0], r[-1] + 1, False)
+    return (name, ps, 0, shp[1], False)
+
+
+def dst_id(topo, c):
+    return DstId(rid=topo.addr(c)[0], pnc=topo.addr(c)[1])
+
+
+def helpers(T, topo, c):
+    mine = [o for o in topo.cores_of(c) if o != c]
+    near = [o for o in mine if topo.die(o) == topo.die(c)]
+    far = [o for o in mine if topo.die(o) != topo.die(c) and all(topo.may_write(o, t) for t in T.cores)]
+    return near, far[:2]
+
+
+def carriers(T, topo, c):
+    near, far = helpers(T, topo, c)
+    wide = far + [o for o in near if all(topo.may_write(o, t) for t in T.cores)]
+    return [wide[0], wide[1], c, wide[2], c, wide[0]]
+
+
+def input_plan(T, ring, rank):
+    return [(T.cores[ring[(v - rank) % 8]], v, (rank + 2 * ((v - rank) % 8) - 2) % 8) for v in range(8)]
+
+
+def final_plan(T, k, s):
+    rs = [(gm - 2 * k + (0, 4, 2)[s]) % 8 for gm in range(8)]
+    return [(T.cores[r], gm, (r + k + (1, -1, 0)[s]) % 8) for gm, r in enumerate(rs)]
+
+
+def helper_program(g, core, T, topo):
+    boss = [c for c in T.cores if topo.chip(c) == topo.chip(core)]
+    if not boss:
+        return
+    boss = boss[0]
+    near, far = helpers(T, topo, boss)
+    S = T.sem
+    rank, ring = T.rank_of(boss), diag_ring(T, topo)
+    n = len(topo.engines(boss, core))
+
+    def deal(plan, src, dst, sem):
+        g.remote_dma_fused([RemoteDMATransfer(dst_ids=[dst_id(topo, c)], dma_engine_mask=1 << topo.engines(core, c)[e],
+                                              remote_sem=S[sem], src=T[src][i], dst=T[dst][j])
+                            for e, (c, i, j) in enumerate(plan)], local_sem=S["d0"])
+
+    def blends():
+        mine = [c for c, o in enumerate(carriers(T, topo, boss)) if o == core]
+        for c in mine:
+            if c == len(CH):
+                g.wait_ge(S["h_f%d" % c], n)
+                deal(final_plan(T, ring.index(rank), 2), "SH", "LH", "a_mh")
+                continue
+            s, a, b = CH[c]
+            g.sync.wait_ge(S["h_f%d" % c], n)
+            g.sync.dma_start(T["SZ%d" % c][:], T["ZI%d" % s][:, a:b]).then_inc(S["d%d" % (10 + c)], 16)
+            g.wait_ge(S["d%d" % (10 + c)], 16)
+            deal(final_plan(T, ring.index(rank), s), "SZ%d" % c, "LZ%d" % c, "a_f%d" % c)
+        return 8 * len(mine)
+
+    if core in far:
+        hf = far.index(core)
+        plan = input_plan(T, ring, rank)
+        g.wait_ge(S["h_fl"], n)
+        deal([(c, 2 * i + hf, 2 * j + hf) for c, i, j in plan], "SF", "LF", "a_fl")
+        g.wait_ge(S["h_in"], n)
+        deal([(helpers(T, topo, c)[0][1 + hf], i, j) for c, i, j in plan], "SX", "LX", "h_x")
+        g.wait_ge(S["d0"], 16 + blends())
+    if core in near:
+        i = near.index(core)
+        m, n = topo.mask(core, boss), len(topo.engines(core, boss))
+        rid, pid, _ = topo.addr(boss)
+        sent = 0
+
+        def spread(dsts, cores, sem):
+            g.remote_dma_fused([RemoteDMATransfer(dst_ids=[dst_id(topo, c) for c in cores], dma_engine_mask=m, remote_sem=S[sem],
+                                                  src=T["O0"][:, 0:512], dsts=dsts)], local_sem=S["d0"])
+        g.wait_ge(S["h_z"], n)
+        if i == 0:
+            spread([T["O0"][:, 0:512]] * 2, near[1:], "h_z")
+            sent += n
+        spread([T["W1"][:, 512 * j:512 * j + 512] for j in range(8 * i, 8 * i + 8)], [boss] * 8, "a_w1")
+        js = range(8 + (0, 6, 11)[i], 8 + (6, 11, 16)[i])
+        spread([T["W2"][:, 512 * j:512 * j + 512] for j in js], [boss] * len(js), "a_w2")
+        sent += 2 * n
+        if i:
+            a = 2048 * (i - 1)
+            XB, LX = T["XB"], T["LX"]
+            g.sync.wait_ge(S["h_x"], 8)
+            g.sync.dma_start(XB[0:112, 8192 + a:10240 + a], LX[1:8]).then_inc(S["d3"], 16)
+            g.sync.dma_start(XB[112:128, 8192 + a:10240 + a], LX[0]).then_inc(S["d3"], 16)
+            g.sync.dma_start(XB[:, a:a + 2048], LX[:]).then_inc(S["d1"], 16)
+            g.sync.dma_start(XB[16:128, 4096 + a:6144 + a], LX[0:7]).then_inc(S["d2"], 16)
+            g.sync.dma_start(XB[0:16, 4096 + a:6144 + a], LX[7]).then_inc(S["d2"], 16)
+            for sl, cnt in ((2, 32), (0, 16), (1, 32)):
+                g.wait_ge(S["d%d" % (sl + 1)], cnt)
+                blk = XB[:, 4096 * sl + a:4096 * sl + a + 2048]
+                g.remote_dma(blk, blk, S["a_xb"], S["d0"], pid, rid, m)
+            sent += 3 * n
+        g.wait_ge(S["d0"], sent + blends())
+
+
+def rank_program(g, core, T, topo):
+    rank = T.rank_of(core)
+    if rank is None:
+        helper_program(g, core, T, topo)
+        return
+    ring = diag_ring(T, topo)
+    k = ring.index(rank)
+    dcore = [T.cores[ring[d]] for d in range(8)]
+    ops = []
+
+    def ap(v):
+        if v[0] == "*":
+            return ap(v[1]).indirect(ap(v[2]))
+        return T[v[0]][v[1]]
+
+    def sc(s):
+        return ap(s) if isinstance(s, tuple) else s
+
+    def rec(q, fn, outs, ins, grp=None, n=1):
+        rd, wr = [], []
+        for v in ins:
+            if isinstance(v, tuple):
+                rd += [region(v[1]), region(v[2])] if v[0] == "*" else [region(v)]
+        for v in outs:
+            if v[0] == "*":
+                wr.append(region(v[1]))
+                rd.append(region(v[2]))
+            else:
+                wr.append(region(v))
+        ops.append({"q": q, "fn": fn, "rd": rd, "wr": wr, "grp": grp, "n": n})
+
+    def tt(o, a, b, op):
+        rec("v", lambda: g.vector.tensor_tensor(ap(o), ap(a), ap(b), op), [o], [a, b])
+
+    def ts(o, a, s1, op0, s2=None, op1=None):
+        if op1 is None:
+            rec("v", lambda: g.vector.tensor_scalar(ap(o), ap(a), sc(s1), None, op0), [o], [a, s1])
+        else:
+            rec("v", lambda: g.vector.tensor_scalar(ap(o), ap(a), sc(s1), sc(s2), op0, op1), [o], [a, s1, s2])
+
+    def cp(o, a):
+        rec("v", lambda: g.vector.tensor_copy(ap(o), ap(a)), [o], [a])
+
+    def fill(o, val):
+        rec("v", lambda: g.vector.memset(ap(o), val), [o], [])
+
+    def act(o, a, f=AF.Identity, bias=0.0, scale=1.0):
+        rec("a", lambda: g.scalar.activation(ap(o), ap(a), f, bias=sc(bias), scale=sc(scale)), [o], [a, bias, scale])
+
+    def mm(o, l, r, st, sp):
+        rec("p", lambda: g.tensor.matmul(ap(o), ap(l), ap(r), st, sp), [o], [l, r])
+
+    def dma(q, o, a, grp, slow=False, after=None):
+        eng = {"s": g.sync, "a": g.scalar, "g": g}[q]
+        if slow:
+            rec(q, lambda: eng.dma_start(ap(o), ap(a), allow_slow_non_contiguous=True), [o], [a], grp, 16)
+        else:
+            rec(q, lambda: eng.dma_start(ap(o), ap(a)), [o], [a, after], grp, 16)
+
+    def iota(o, pat, base, cm, small=False):
+        if small:
+            rec("g", lambda: g.iota(ap(o), pat, base, cm, allow_small_or_imprecise_dtypes=True), [o], [])
+        else:
+            rec("g", lambda: g.iota(ap(o), pat, base, cm), [o], [])
+
+    def arrive(name, outs, n):
+        rec(None, None, outs, [], name, n)
+
+    def send(dst, o, a, name):
+        rid, pid, _ = topo.addr(dst)
+        m = topo.mask(core, dst)
+        n = len(topo.engines(core, dst))
+        rec("r", lambda ls: g.remote_dma(ap(o), ap(a), T.sem[name], ls, pid, rid, m), [], [a], "t" + name, n)
+        return n
+
+    def deal(name, src, dst, plan, q="s", stage=None, own_src=None, after=None):
+        tr, rd = [], [after] if after else []
+        if stage:
+            dma(q, V(src), stage, "s" + name)
+        for c, i, j in plan:
+            if c == core:
+                dma(q, V(dst, j), own_src(i) if own_src else V(src, i), "l" + name)
+                own = j
+            else:
+                rid, pid, _ = topo.addr(c)
+                tr.append((rid, pid, 1 << topo.engines(core, c)[len(tr)], i, j))
+                rd.append(V(src, i))
+        rec("r", lambda ls: g.remote_dma_fused(
+            [RemoteDMATransfer(dst_ids=[DstId(rid=a, pnc=b)], dma_engine_mask=m, remote_sem=T.sem[name],
+                               src=ap(V(src, i)), dst=ap(V(dst, j))) for a, b, m, i, j in tr], local_sem=ls),
+            [], rd, "t" + name, len(tr))
+        st = len(SCRATCH[dst][1]) and SCRATCH[dst][1][0] // 8
+        arrive(name, [V(dst, j) for j in range(own % st, 8 * st, st) if j != own], len(tr))
+
+    def col(f):
+        return C("CO", 16 * f + 15, 16 * f + 16)
+
+    def wrap(out, f, src, first=True, last=True):
+        for q in range(16):
+            mm(out, C("ZM", 144 * f + 15 - q, 144 * f + 143 - q), C(src[0], src[1] + q, src[1] + 1024, 16),
+               first and q == 0, last and q == 15)
+
+    def mat(i, m=128):
+        return C("MM", 128 * i, 128 * i + m)
+    I1, I1024, ONES, DH, DHN, EO, EN_, C40 = range(8)
+
+    def grp(gm, a, b):
+        return slice(16 * (gm % 8) + a, 16 * (gm % 8) + b)
+
+    def rows_to_slots(q, dst, r1, src, r0, name, mid=True, side=True):
+        if side:
+            dma(q, V(dst, slice(16 + r1, 128, 16), slice(4096, 8192)), V(src, slice(r0, 112, 16), slice(0, 4096)), name)
+            dma(q, V(dst, slice(r1, 112, 16), slice(8192, 12288)), V(src, slice(16 + r0, 128, 16), slice(0, 4096)), name)
+            dma(q, V(dst, slice(r1, r1 + 1), slice(4096, 8192)), V(src, slice(112 + r0, 113 + r0), slice(0, 4096)), name)
+            dma(q, V(dst, slice(112 + r1, 113 + r1), slice(8192, 12288)), V(src, slice(r0, r0 + 1), slice(0, 4096)), name)
+        if mid:
+            dma(q, V(dst, slice(r1, 128, 16), slice(0, 4096)), V(src, slice(r0, 128, 16), slice(0, 4096)), name)
+
+    in_plan = input_plan(T, ring, rank)
+    nb = [dcore[(k - 1) % 8], dcore[(k + 1) % 8]]
+    src_nb = [nb[1], nb[0]]
+
+    def nin(c):
+        return len(topo.engines(c, core))
+
+    dma("a", V("SM"), V("ms"), "sm")
+    dma("s", C("TI", 0, 512), C("cor", 0, 512), "ci0")
+    dma("s", C("TI", 1024, 2048), V("fl"), "fi")
+    near, far = helpers(T, topo, core)
+
+    carry = carriers(T, topo, core)
+
+    def hand(buf, src, dst, c, sem):
+        es = topo.engines(core, c)
+        rec("r", lambda ls: g.remote_dma_fused(
+            [RemoteDMATransfer(dst_ids=[dst_id(topo, c)], dma_engine_mask=sum(1 << e for e in es[v::8]), remote_sem=T.sem[sem],
+                               src=ap(V(buf, src[v])), dst=ap(V(buf, dst[v]))) for v in range(8)], local_sem=ls),
+            [], [V(buf, i) for i in src], "t%s%d" % (buf, c), len(es))
+
+    wt = [(0, 3, 7, 2, 1), (0, 9, 13, 2, 1), (7, 2, 6, 2, 64), (7, 1, 2, 1, 1), (8, 1, 2, 1, 1), (8, 4, 6, 1, 1),
+          (9, 2, 9, 6, 1), (9, 3, 10, 6, 1), (9, 4, 11, 6, 2), (9, 5, 12, 6, 2),
+          (10, 0, 16, 2, -16),
+          (11, 0, 21, 20, 32), (11, 1, 22, 20, 1), (11, 2, 23, 20, 32768), (11, 3, 24, 20, 1024),
+          (11, 9, 11, 1, 2 ** 21), (12, 9, 11, 1, 2 ** 21),
+          (13, 1, 64, 16, 32768), (13, 7, 64, 16, 32768),
+          (13, 2, 21, 18, 64), (13, 3, 22, 18, 1), (15, 8, 27, 18, 64), (15, 9, 28, 18, 1),
+          (14, 2, 41, 38, -64), (14, 3, 42, 38, -1),
+          (17, 0, 55, 18, 1), (17, 1, 56, 18, 1), (21, 0, 8, 1, 1), (22, 8, 9, 1, 1), (23, 0, 9, 1, 1),
+          (24, 0, 8, 2, 16), (24, 1, 8, 2, 0.5), (25, 1, 16, 2, 1)]
+    wt += [(1 + i, 0, 16, 2, 2 ** i) for i in range(6)]
+
+    def weights(f0, f1):
+        fill(C("GP", 16 * f0, 16 * f1), 0.0)
+        for f, x0, x1, s, val in wt:
+            if f0 <= f < f1:
+                fill(C("GP", 16 * f + x0, 16 * f + x1, s), float(val))
+
+    def columns(f0, f1):
+        a, b = 16 * f0, 16 * f1
+        if f0 == 0:
+            ts(C("PI", 1, 2), C("PI", 0, 1), 15, AL.bitwise_and)
+            cp(C("PC", 0, 2), C("PI", 0, 2))
+        ts(C("A2", a, b), C("DF", a, b), 0.0, AL.is_gt)
+        ts(C("A0", a, b), C("DF", a, b), C("PC", 1, 2), AL.is_equal)
+        tt(C("A0", a, b), C("A0", a, b), C("GP", a, b), AL.mult)
+        rec("v", lambda: g.vector.tensor_tensor_scan(ap(C("CO", a, b)), ap(C("A2", a, b)), ap(C("A0", a, b)), 0.0,
+                                                     AL.mult, AL.add), [C("CO", a, b)], [C("A2", a, b), C("A0", a, b)])
+
+    iota(C("PI", 0, 1), [[1, 1]], 0, 1)
+    iota(C("DF", 0, 160), [[0, 10], [1, 16]], 0, 0, True)
+    iota(V("IN"), [[1, 144]], 0, 0, True)
+    fill(C("O0", 0, 512), 0.0)
+    send(near[0], C("O0", 0, 512), C("O0", 0, 512), "h_z")
+    iota(C("DF", 160, 16 * NF), [[0, NF - 10], [1, 16]], 0, 0, True)
+    deal("a_ms", "SM", "LM", in_plan, "a", own_src=lambda i: V("ms", grp(i, 0, 16)))
+    weights(0, 10)
+    columns(0, 10)
+    act(C("KB", 0, 64), C("IN", 0, 64), scale=col(0))
+    for i in range(6):
+        act(C("KB", 64 << i, 128 << i), C("KB", 0, 64 << i), bias=col(1 + i))
+    cp(C("CL", 0, 512), C("TI", 0, 512))
+    deal("a_c0", "SC0", "LC0", in_plan, stage=C("CL", 0, 512), own_src=lambda i: V("CL", grp(i, 0, 16), slice(0, 512)))
+    dma("s", C("TI", 512, 1024), C("cor", 512, 1024), "ci1")
+    dma("s", V("MI"), V("LM"), "mi")
+    iota(V("JT"), [[16, 64]], 12288, 1)
+    weights(10, NF)
+    columns(10, NF)
+    act(C("GB", 2048, 3072), C("KB", 0, 1024), bias=col(7))
+    act(C("W2", 12288, 13312), C("KB", 0, 1024), scale=col(9))
+    for h in range(2):
+        fi = C("TI", 1024 + 512 * h, 1536 + 512 * h)
+        ts(C("TI", 0, 512), fi, 5, AL.arith_shift_right)
+        ts(fi, fi, 31, AL.bitwise_and)
+        cp(C("GB", 512 * h, 512 * h + 512), C("TI", 0, 512))
+        cp(C("GB", 1024 + 512 * h, 1536 + 512 * h), fi)
+        if h == 0:
+            cp(C("CL", 512, 1024), C("TI", 512, 1024))
+            deal("a_c1", "SC1", "LC1", in_plan, stage=C("CL", 512, 1024),
+                 own_src=lambda i: V("CL", grp(i, 0, 16), slice(512, 1024)))
+    dma("a", C("CL", 0, 512), V("LC0"), "cl0")
+    for i in range(8):
+        dma("s", V("SF", slice(i // 4, 16, 2), slice(32 * (i % 4), 32 * (i % 4) + 32)),
+            V("GB", slice(32 * (i // 2), 32 * (i // 2) + 32), slice(1024 * (i % 2), 1024 * (i % 2) + 1024)), "sf%d" % (i // 4))
+    MSL, NB1, NB2, LS, UVL, TL, OWL = 0, 64, 128, 192, 320, 576, 1088
+    cp(C("UL", MSL, MSL + 64), V("MI"))
+    cp(IND(V("KB"), C("UL", MSL, MSL + 64)), C("GB", 2048, 3072))
+    for hf in range(2):
+        hand("SF", range(hf, 16, 2), range(hf, 16, 2), far[hf], "h_fl")
+    arrive("a_fl", [V("LF")], 16)
+    dma("s", V("SX", slice(8, 16)), C("x", 2048, 4096), "sx1", after=V("SF"))
+    dma("s", C("CL", 512, 1024), V("LC1"), "cl1")
+    dma("s", V("SX", slice(0, 8)), C("x", 0, 2048), "sx0")
+    hand("SX", range(8, 16), range(8), far[1], "h_in")
+    hand("SX", range(8), range(8), far[0], "h_in")
+    dma("g", V("SE", 0), V("eps"), "se", True)
+    dma("g", C("EP", 0, 1), V("eps"), "ep", True)
+    oth = [c for c in T.cores if c != core]
+    em = 1 << topo.engines(core, oth[0])[-1]
+    rec("r", lambda ls: g.remote_dma_fused(
+        [RemoteDMATransfer(dst_ids=[dst_id(topo, c) for c in oth], dma_engine_mask=em,
+                           remote_sem=T.sem["a_eps"], src=ap(V("SE", 0)), dsts=[ap(V("LE", rank)) for c in oth])],
+        local_sem=ls), [], [V("SE", 0)], "ta_eps", 1)
+    arrive("a_eps", [V("LE")], len(oth))
+    arrive("a_w1", [V("W1")], 24 * nin(near[0]))
+    arrive("a_w2", [C("W2", 4096, 12288)], 16 * nin(near[0]))
+    arrive("a_xb", [C("XB", 0, 12288)], 6 * nin(near[0]))
+    for gm in range(8):
+        dma("s", V("W1", grp(gm, 0, 8), slice(0, 4096)), V("LF", slice(2 * gm, 2 * gm + 2)), "f1")
+    for gm in range(8):
+        for sl, o in ((1, 2 * ((gm - 1) % 8)), (2, 2 * ((gm + 1) % 8))):
+            dma("s", V("W1", grp(gm, 0, 8), slice(4096 * sl, 4096 * sl + 4096)), V("LF", slice(o, o + 2)), "f2")
+    ts(C("PI", 2, 3), C("PI", 1, 2), 1, AL.arith_shift_right)
+    ts(C("PI", 3, 4), C("PI", 0, 1), 4, AL.arith_shift_right)
+    tt(C("PC", 2, 3), C("PC", 0, 1), C("PC", 1, 2), AL.subtract)
+    cp(C("PC", 6, 8), C("PI", 2, 4))
+    ts(C("PC", 3, 4), C("PC", 2, 3), 15.0, AL.add)
+    tt(C("PC", 4, 5), C("PC", 2, 3), C("PC", 6, 7), AL.add)
+    ts(C("PC", 5, 6), C("PC", 4, 5), 4.0, AL.add)
+    for f in range(6):
+        ts(C("ZM", 144 * f, 144 * f + 144), V("IN"), C("PC", 3, 4), AL.is_equal, col(11 + f), AL.mult)
+    ts(C("TI", 0, 64), V("MI"), 127, AL.bitwise_and)
+    ts(C("TI", 64, 128), V("MI"), 7, AL.arith_shift_right)
+    ts(V("JT"), V("JT"), C("PC", 2, 3), AL.subtract)
+    for i in range(4):
+        ts(C("HM", 64 * i, 64 * i + 64), C("TI", 64 * (i // 2), 64 * (i // 2) + 64), 4.0, AL.mult, -512.0, AL.add)
+
+    def late_constants():
+        ts(C("ZM", 144 * 6, 144 * 7), V("IN"), C("PC", 3, 4), AL.is_equal)
+        n128 = C("IN", 0, 128)
+        ts(mat(I1), n128, C("PC", 0, 1), AL.is_equal)
+        ts(mat(I1024), n128, C("PC", 0, 1), AL.is_equal, 1024.0, AL.mult)
+        ts(C("TF", 0, 128), n128, C("PC", 2, 3), AL.is_ge)
+        ts(C("TF", 128, 256), n128, C("PC", 3, 4), AL.is_le)
+        ts(mat(DH), n128, C("PC", 0, 1), AL.is_equal, col(23), AL.mult)
+        tt(mat(ONES), C("TF", 0, 128), C("TF", 128, 256), AL.mult)
+        ts(mat(DHN), mat(DH), -1.0, AL.mult)
+        ts(C("TF", 0, 128), n128, C("PC", 4, 5), AL.is_equal, col(24), AL.mult)
+        ts(C("TF", 128, 256), n128, C("PC", 5, 6), AL.is_equal, col(24), AL.mult)
+        ts(V("UC"), C("IN", 0, 16), 0.25, AL.mult)
+        tt(mat(EO), C("TF", 0, 128), C("TF", 128, 256), AL.add)
+        tt(mat(EN_), C("TF", 0, 128), C("TF", 128, 256), AL.subtract)
+        for i in range(5):
+            ts(C("MM", 128 * C40 + 8 * i, 128 * C40 + 8 * i + 8), C("IN", 0, 8), C("PC", 7, 8), AL.is_equal)
+        ts(C("TI", 0, 64), V("MI"), 1.0, AL.add)
+        ts(C("TI", 64, 128), V("MI"), 128.0, AL.add)
+        ts(C("TI", 128, 192), V("MI"), 4096 - 128, AL.bitwise_and)
+        ts(C("TI", 0, 64), C("TI", 0, 64), 127, AL.bitwise_and)
+        ts(C("TI", 64, 128), C("TI", 64, 128), 4095, AL.bitwise_and)
+        tt(C("TI", 0, 64), C("TI", 0, 64), C("TI", 128, 192), AL.add)
+        cp(C("UL", NB1, NB1 + 128), C("TI", 0, 128))
+        fill(C("XB", SN1, SN1 + 1), 1024.0)
+        fill(C("XB", SN1 + 1, SN1 + 2), -1024.0)
+        fill(C("XF", SN2, SN2 + 1), 1024.0)
+        fill(C("XF", SN2 + 1, SN2 + 2), -1024.0)
+
+    CQ = float(512 + 512 * 1024)
+    FB = C("W1", 0, 4096)
+
+    def starts(rnd):
+        ts(C("TI", 0, 128), C("P0", 0, 128), CQ, AL.add)
+        if rnd:
+            ts(C("MS0", 128, 192), C("P0", 128, 192), 8.5, AL.is_ge)
+            ts(C("MS1", 128, 192), C("P0", 128, 192), 8.5, AL.is_ge)
+        ts(C("TI", 128, 256), C("TI", 0, 128), 1023, AL.bitwise_and)
+        ts(C("TI", 256, 384), C("TI", 0, 128), 10, AL.arith_shift_right)
+        tt(C("TI", 128, 384), C("TI", 128, 384), V("HM"), AL.add)
+        w = 192 if rnd else 128
+        for s in (1, 0):
+            ts(C("MS%d" % s, 0, 64), C("TI", 128 + 64 * s, 192 + 64 * s), 0.0, AL.max, 511.0, AL.min)
+            ts(C("MS%d" % s, 64, 128), C("TI", 256 + 64 * s, 320 + 64 * s), 0.0, AL.max, 127.0, AL.min)
+            send(nb[s], st_ap(rnd, s, 0, w), C("MS%d" % s, 0, w), "a_st%d%d" % (rnd, s))
+        for s in (1, 0):
+            arrive("a_st%d%d" % (rnd, s), [st_ap(rnd, s, 0, w)], nin(src_nb[s]))
+
+    def st_ap(rnd, s, a, b):
+        o = 128 * s if rnd == 0 else 256 + 192 * s
+        return C("ST", o + a, o + b)
+
+    SO0, INC = (4096, 8192), ((-4096, 8192), (-8192, 4096))
+
+    def tmp(s, i, n=1):
+        o = 384 + 384 * s + 64 * i
+        return C("TI", o, o + 64 * n)
+
+    def cells(s, buf, o, off, so, dn):
+        ts(tmp(s, 0), C(buf, o, o + 64), 2, AL.arith_shift_right)
+        ts(tmp(s, 1), C(buf, o + 64, o + 128), 124, AL.bitwise_and)
+        if so:
+            tt(tmp(s, 0), tmp(s, 0), tmp(s, 4), AL.add)
+        ts(tmp(s, 1), tmp(s, 1), 32.0, AL.mult, float(SO0[s] - off // 4), AL.add)
+        tt(tmp(s, 0), tmp(s, 0), tmp(s, 1), AL.add)
+        if dn:
+            tt(tmp(s, 0), tmp(s, 0), tmp(s, 3), AL.max)
+        cp(C("UL", LS + 64 * s, LS + 64 * s + 64), tmp(s, 0))
+
+    def step(rnd, s, h):
+        Q, em_ = C("P%d" % (1 - s), 0, 64), "EM%d" % s
+        wrap(Q, s, ("O%d" % s, 0))
+        ts(tmp(s, 2), Q, float(2 ** 20), AL.max, CQ, AL.add)
+        ts(tmp(s, 4 + h), Q, float(2 ** 20), AL.is_ge, float(INC[s][h]), AL.mult)
+        ts(tmp(s, 0), tmp(s, 2), 1023, AL.bitwise_and)
+        ts(tmp(s, 1), tmp(s, 2), 10, AL.arith_shift_right, 1023, AL.bitwise_and)
+        if h:
+            ts(tmp(s, 2), tmp(s, 5), -1.0 / INC[s][1], AL.mult, 2.0, AL.add)
+            tt(tmp(s, 4), tmp(s, 4), tmp(s, 5), AL.add)
+        tt(tmp(s, 0, 2), tmp(s, 0, 2), C(em_, 0, 128) if h else st_ap(rnd, s, 0, 128), AL.add)
+        if h:
+            tt(C(em_, 128, 192), C(em_, 128, 192), tmp(s, 2), AL.mult)
+        else:
+            ts(C(em_, 128, 192), tmp(s, 4), -1.0 / INC[s][0], AL.mult, 2.0, AL.add)
+        off = 512 * (h + 1)
+        ts(C(em_, 0, 64), tmp(s, 0), float(off), AL.max, float(off + 511), AL.min)
+        ts(C(em_, 64, 128), tmp(s, 1), float(off), AL.max, float(off + 127), AL.min)
+        cells(s, em_, 0, off, True, rnd and h)
+        if h:
+            send(src_nb[s], C("EN", 192 * s, 192 * s + 192), V(em_), "a_en%d%d" % (rnd, s))
+            sl = C("SL", 64 * s, 64 * s + 64)
+            if rnd:
+                ts(tmp(s, 5), tmp(s, 4), float(SO0[s]), AL.add, 5.0 / 4096, AL.mult)
+                ts(tmp(s, 2), st_ap(1, s, 128, 192), 15.0 + s, AL.mult)
+                tt(sl, tmp(s, 5), tmp(s, 2), AL.max)
+            else:
+                ts(sl, tmp(s, 4), float(SO0[s]), AL.add, 1.0 / 1024, AL.mult)
+            ts(tmp(s, 0, 2), C(em_, 0, 128), 3, AL.bitwise_and)
+            cp(C("UL", UVL + 128 * s, UVL + 128 * s + 128), tmp(s, 0, 2))
+
+    def look(s, win, on_act=True):
+        i = IND(win, C("UL", LS + 64 * s, LS + 64 * s + 64))
+        if on_act:
+            act(V("O%d" % s), i)
+        else:
+            cp(V("O%d" % s), i)
+
+    def taps_mm(s, bank, c0, fields):
+        for n, i in enumerate(fields):
+            o = C(bank, c0 + 64 * n, c0 + 64 * n + 64)
+            mm(o, mat(I1024), C("SL", 64 * s, 64 * s + 64), True, False)
+            wrap(o, 2 + i, ("O%d" % s, 0), False, True)
+
+    def taps_list(rnd, s, bank, fields):
+        a = TL + 256 * s + 64 * fields[0]
+        ts(C("UL", a, a + 64 * len(fields)), C(bank, 0, 64 * len(fields)), float((SN2 if rnd else SN1) + s), AL.min)
+
+    def own_lists(rnd):
+        for s in range(2):
+            arrive("a_en%d%d" % (rnd, s), [C("EN", 192 * s, 192 * s + 192)], nin(nb[s]))
+        for i in range(4):
+            o = 192 * (i // 2) + 64 * (i % 2)
+            tt(C("TI", 64 * i, 64 * i + 64), C("EN", o, o + 64), C("HM", 128 * (i % 2), 128 * (i % 2) + 64), AL.subtract)
+        ts(C("TI", 0, 256), C("TI", 0, 256), -1536.0, AL.add)
+        for i in range(4):
+            o = 192 * (i // 2) + 128
+            tt(C("TI", 64 * i, 64 * i + 64), C("TI", 64 * i, 64 * i + 64), C("EN", o, o + 64), AL.mult)
+        new = C("TI", 1152 + 256 * rnd, 1408 + 256 * rnd)
+        ts(new, C("TI", 0, 256), 0.25, AL.mult, 511.625, AL.add)
+        if rnd:
+            tt(C("TI", 0, 256), C("TI", 1152, 1408), new, AL.subtract)
+            for i in range(4):
+                tt(C("TI", 64 * i, 64 * i + 64), C("TI", 64 * i, 64 * i + 64), C("MS0", 128, 192), AL.mult)
+            tt(new, new, C("TI", 0, 256), AL.add)
+        cp(C("UL", OWL, OWL + 256), new)
+
+    def own_look(i):
+        act(C("GB", 1024 * i, 1024 * i + 1024), IND(V("CT"), C("UL", OWL + 64 * i, OWL + 64 * i + 64)), scale=col(17 + i))
+
+    def own_mm(rnd, last):
+        for h in range(2):
+            if not last:
+                mm(V("P%d" % (6 + h)), mat(EN_ if rnd else DHN), C("NR", 512 * h, 512 * h + 512), True, False)
+            for i in ((3,) if last else (0, 1, 2)):
+                mm(V("P%d" % (6 + h)), mat(EO if rnd else DH), C("GB", 1024 * i + 512 * h, 1024 * i + 512 * h + 512), False, last)
+
+    def widen(i, on_act=True):
+        a = 1024 * i
+        b = 5120 * (i // 4) + 1024 * (i % 4)
+        (act if on_act else cp)(C("XF", b, b + 1024), C("XB", a, a + 1024))
+
+    def hb(n, c, p=ALL):
+        return V(n, p, slice(CH[c][1], CH[c][2]))
+
+    def pb(bank, c):
+        return C("P%d" % bank, 0, CH[c][2] - CH[c][1])
+
+    def pc(bank, c, p=ALL):
+        return V("P%d" % (bank + CH[c][1] // 512), p, slice(CH[c][1] % 512, (CH[c][2] - 1) % 512 + 1))
+
+    def lst(base, c):
+        return C("UL", base + CH[c][1] // 16, base + CH[c][2] // 16)
+
+    for rnd in range(2):
+        win = FB if rnd else V("KB")
+        abuf = "KB" if rnd else "W2"
+        mrow = 8 if rnd else 1
+        for half, buf in enumerate((abuf, "GB")):
+            cuts = [0, 1024, 2048, 3072, 4096] if half else [0, 256, 768, 1792, 2944, 4096]
+            for c in range(len(cuts) - 1):
+                o = C(buf, cuts[c], cuts[c + 1])
+                a, w = 512 * half + 256 + cuts[c] // 16, (cuts[c + 1] - cuts[c]) // 16
+                act(o, IND(win, C("CL", a, a + w)), scale=col(8) if rnd == 0 else 1.0)
+                if rnd == 0 and half == 1 and c == 1:
+                    act(V("NR"), IND(FB, C("UL", MSL, MSL + 64)), scale=col(21))
+                    wrap(C("P0", 0, 64), 0, ("NR", 0))
+                    wrap(C("P0", 64, 128), 1, ("NR", 0))
+                tt(o, IND(win, C("CL", a - 256, a - 256 + w)), o, AL.add)
+                if rnd == 0 and half == 1 and c == 2:
+                    starts(0)
+            if half == 0:
+                rows_to_slots("s", "W1", 9, abuf, mrow, "ma%d" % rnd, mid=False)
+                if rnd == 1:
+                    rows_to_slots("s", "W2", 1, abuf, mrow, "wa2")
+                    starts(1)
+        if rnd:
+            for c in (2, 3, 4):
+                act(pc(4, c), hb("DF", c), scale=0.5)
+            widen(5)
+            widen(6)
+        rows_to_slots("s", "W1", 10, "GB", mrow, "mb%d" % rnd, mid=False)
+        rows_to_slots("a", "W1", 10, "GB", mrow, "mb%d" % rnd, side=False)
+        rows_to_slots("a", "W1", 9, abuf, mrow, "mb%d" % rnd, side=False)
+        if rnd == 0:
+            for gm in range(8):
+                for sl, sh in ((1, -1), (2, 1)):
+                    dma("s", V("W2", grp(gm, 1, 6), slice(4096 * sl, 4096 * sl + 4096)),
+                        V("W2", grp(gm + sh, 1, 6), slice(0, 4096)), "wa")
+                for sl, sh in enumerate((0, -1, 1)):
+                    dma("s", V("W2", grp(gm, 7, 12), slice(4096 * sl, 4096 * sl + 4096)), V("GB", grp(gm + sh, 1, 6)), "wb")
+            act(C("CT", 0, 32), C("IN", 0, 32), scale=col(25), bias=col(10))
+            for i in range(5):
+                act(C("CT", 32 << i, 64 << i), C("CT", 0, 32 << i), bias=col(1 + i))
+            late_constants()
+        else:
+            rows_to_slots("s", "W2", 7, "GB", mrow, "wb2")
+            widen(7)
+            widen(8)
+        for s in (1, 0):
+            o = st_ap(rnd, s, 0, 1)[1][1].start
+            cells(s, "ST", o, 0, False, False)
+            if rnd:
+                tt(tmp(s, 3), st_ap(1, s, 128, 192), V("JT"), AL.mult)
+        if rnd:
+            for h in range(2):
+                tt(C("XF", 4096 + 512 * h, 4608 + 512 * h), hb("ZI1", h), V("P%d" % (4 + h)), AL.add)
+            va = slice(4096, 5120)
+            dma("s", V("XF", slice(16, 128), slice(9216, 10240)), V("XF", slice(0, 112), va), "vs")
+            dma("s", V("XF", slice(0, 112), slice(14336, 15360)), V("XF", slice(16, 128), va), "vs")
+            dma("s", V("XF", slice(0, 16), slice(9216, 10240)), V("XF", slice(112, 128), va), "vs")
+            dma("s", V("XF", slice(112, 128), slice(14336, 15360)), V("XF", slice(0, 16), va), "vs")
+            widen(9, False)
+        look(1, V("W1"))
+        look(0, V("W1"), False)
+        a = NB2 if rnd else NB1
+        act(V("NR"), IND(FB, C("UL", a, a + 64)), scale=col(21), bias=col(22))
+        step(rnd, 1, 0)
+        look(1, V("W1"))
+        step(rnd, 0, 0)
+        look(0, V("W1"))
+        if rnd:
+            widen(4)
+        step(rnd, 1, 1)
+        look(1, V("W2"))
+        if rnd:
+            widen(10)
+            widen(11)
+        step(rnd, 0, 1)
+        taps_mm(1, "P0", 0, [0])
+        taps_list(rnd, 1, "P0", [0])
+        look(0, V("W2"), False)
+        taps_mm(1, "P6", 0, [1])
+        taps_list(rnd, 1, "P6", [1])
+        taps_mm(1, "P7", 0, [2, 3])
+        xw = C("XF", 0, SN2 + 2) if rnd else C("XB", 0, SN1 + 2)
+
+        def fetch(c):
+            s = CH[c][0]
+            act(hb("A0", c), IND(xw, lst(TL + 256 * s, c)))
+            if c == 0:
+                diff(0, 0)
+                taps_list(rnd, 1, "P7", [2, 3])
+            act(hb("UU", c), IND(V("UC"), lst(UVL + 128 * s, c)))
+            mm(pb(2 + c % 2, c), mat(I1), hb("UU", c), True, True)
+            act(hb("A2", c), IND(xw, lst(TL + 256 * s + 128, c)))
+            act(hb("VV", c), IND(V("UC"), lst(UVL + 128 * s + 64, c)))
+
+        def diff(c, i):
+            s = CH[c][0]
+            tt(hb(("D0", "D2")[i], c), IND(xw, lst(TL + 256 * s + 64 + 128 * i, c)), hb(("A0", "A2")[i], c), AL.subtract)
+
+        def zout(c):
+            s, a, b = CH[c]
+            return hb("ZI%d" % s, c) if rnd else C("XF", ZF0 + 1024 * s + a, ZF0 + 1024 * s + b)
+
+        fetch(0)
+        taps_mm(0, "P1", 0, [0, 1, 2, 3])
+        fetch(1)
+        diff(0, 1)
+        for c in range(5):
+            s = CH[c][0]
+            U, M1, M2 = pb(2 + c % 2, c), pb(4, c), pb(5, c)
+            tt(M1, hb("D0", c), U, AL.mult)
+            tt(M2, hb("D2", c), U, AL.mult)
+            tt(hb("SS", c), hb("A0", c), M1, AL.add)
+            tt(M2, hb("A2", c), M2, AL.add)
+            if c == 0:
+                taps_list(rnd, 0, "P1", [0, 1, 2, 3])
+                own_lists(rnd)
+                own_look(0)
+            tt(M2, M2, hb("SS", c), AL.subtract)
+            if c < 4:
+                diff(c + 1, 0)
+            tt(M2, M2, hb("VV", c), AL.mult)
+            if c < 4:
+                diff(c + 1, 1)
+            tt(zout(c), hb("SS", c), M2, AL.add)
+            if rnd == 0:
+                send(src_nb[s], hb("ZI%d" % s, c), zout(c), "a_z%d" % c)
+                arrive("a_z%d" % c, [hb("ZI%d" % s, c)], nin(nb[s]))
+                for gm in range(4 * c, 4 * c + 4) if c < 2 else ():
+                    r = (gm - 2 * k + 2) % 8
+                    s_ = V("eps", grp(r + k, 0, 16)) if r == rank else V("LE", r, grp(r + k, 0, 16))
+                    dma("g", V("ED", grp(gm, 0, 16), slice(0, 1)), s_, "ed", True)
+            elif carry[c] != core:
+                send(carry[c], zout(c), zout(c), "h_f%d" % c)
+                arrive("a_f%d" % c, [V("LZ%d" % c)], 8)
+            else:
+                deal("a_f%d" % c, "SZ%d" % c, "LZ%d" % c, final_plan(T, k, s), stage=zout(c),
+                     own_src=lambda i: hb("ZI%d" % s, c, grp(i, 0, 16)))
+            if c < 3:
+                fetch(c + 2)
+            if c == 0:
+                own_look(1)
+                own_look(2)
+                own_mm(rnd, False)
+            if c == 1:
+                own_look(3)
+            if c == 2:
+                own_mm(rnd, True)
+                if rnd == 0:
+                    act(V("P0"), hb("ZI1", 0))
+                    act(V("P1"), hb("ZI1", 1))
+                else:
+                    dma("s", hb("GP", 0), V("LZ0"), "gb0")
+                    act(C("DF", 0, 512), V("P6"))
+                    act(C("DF", 512, 1024), V("P7"))
+                    for i in range(8):
+                        dma("a", V("SH", ALL, slice(16 * i, 16 * i + 16)), V("DF", slice(i, 128, 16)), "sh")
+            if c == 3 and rnd:
+                hand("SH", range(8), range(8), carry[5], "h_f5")
+                arrive("a_mh", [V("LH")], 8)
+        if rnd == 1:
+            dma("s", hb("GP", 1), V("LZ1"), "gb1")
+        if rnd == 0:
+            def gap(c):
+                tt(hb("DF", c), hb("ZI0", c), pc(0, c), AL.subtract)
+                act(hb("GP", c), hb("DF", c), AF.Abs)
+
+            def vote(c):
+                ts(hb("O0", c), hb("GP", c), C("ED", 0, 1), AL.is_le)
+                mm(pb(2 + c % 2, c), mat(ONES), hb("O0", c), True, True)
+
+            def pick(c):
+                ts(hb("VV", c), pb(2 + c % 2, c), 8.5, AL.is_ge)
+                tt(hb("O1", c), hb("VV", c), pc(6, c), AL.mult)
+
+            def put(c):
+                tt(IND(FB, lst(MSL, c)), hb("NR", c), hb("O1", c), AL.add)
+            widen(0)
+            widen(1)
+            gap(2)
+            vote(2)
+            gap(3)
+            pick(2)
+            widen(2)
+            vote(3)
+            put(2)
+            gap(4)
+            pick(3)
+            vote(4)
+            put(3)
+            pick(4)
+            put(4)
+            widen(3)
+            for gm in range(8):
+                dma("s", V("W1", grp(gm, 0, 8), slice(4096, 8192)), V("W1", grp(gm - 1, 0, 8), slice(0, 4096)), "f3")
+                dma("s", V("W1", grp(gm, 0, 8), slice(8192, 12288)), V("W1", grp(gm + 1, 0, 8), slice(0, 4096)), "f3")
+            wrap(C("P0", 128, 192), 6, ("O0", 0))
+            for s in range(2):
+                wrap(C("P0", 64 * s, 64 * s + 64), s, ("NR", 0), True, False)
+                wrap(C("P0", 64 * s, 64 * s + 64), s, ("O1", 0), False, True)
+
+    p40 = slice(0, 40)
+    fill(V("D0", slice(32, 64)), 0.5)
+    fill(V("D2", slice(32, 64)), 0.5)
+    for c in (2, 3, 4):
+        dma("s", hb("A0", c), V("LZ%d" % c), "zf%d" % c)
+    for h in range(2):
+        act(V("P%d" % (6 + h)), hb("GP", h))
+    for c in (2, 3, 4):
+        cnt, hh = pb(2 + c % 2, c), pb(4 + c % 2, c)
+        tt(hb("A2", c), hb("A0", c), pc(6, c), AL.subtract)
+        act(hb("SS", c), hb("A2", c), AF.Abs)
+        act(hh, hb("A2", c), scale=0.5)
+        ts(hb("O0", c), hb("SS", c), C("EP", 0, 1), AL.is_le)
+        mm(cnt, mat(ONES), hb("O0", c), True, True)
+        mm(pc(0, c, p40), mat(C40, 40), hb("O0", c), True, True)
+        tt(hh, hb("GP", c), hh, AL.add)
+        act(hb("DF", c), hb("SS", c), AF.Exp, scale=-1.0)
+        dma("a", hb("ye", c), hb("DF", c), "oe%d" % c)
+        ts(hb("O1", c), cnt, 8.5, AL.is_ge)
+        act(pc(0, c, p40), pc(0, c, p40), AF.Sign, bias=-8.5)
+        tt(hb("ZI1", c), hh, hb("O1", c), AL.mult)
+        dma("s", hb("y", c), hb("ZI1", c), "oy%d" % c)
+        if c == 2:
+            for i in range(8):
+                dma("s", V(("D0", "D2")[i // 4], slice(8 * (i % 4), 8 * (i % 4) + 8)),
+                    V("LH", ALL, slice(16 * i, 16 * i + 16)), "mh")
+        for b in ((), (2, 3), (4,))[c - 2]:
+            tt(pc(0, b, p40), pc(0, b, p40), hb("D2", b, p40), AL.mult)
+            tt(hb("D0", b, p40), hb("D0", b, p40), pc(0, b, p40), AL.add)
+            dma("s", hb("yf", b), hb("D0", b, p40), "of%d" % b)
+
+    def meets(a, b):
+        return a[0] == b[0] and a[2] < b[3] and b[2] < a[3] and not a[1].isdisjoint(b[1])
+
+    total, semof, free = {}, {}, ["d%d" % i for i in range(100)]
+    for o in ops:
+        if o["grp"]:
+            total[o["grp"]] = total.get(o["grp"], 0) + o["n"]
+            if o["grp"] not in semof:
+                semof[o["grp"]] = o["grp"] if o["q"] is None else free.pop(0)
+    seen, need = {}, set()
+    for i, o in enumerate(ops):
+        dep = set()
+        for kind in ("rd", "wr"):
+            for r in o[kind]:
+                for j, wj, rj in seen.get(r[0], []):
+                    pj = ops[j]
+                    clash = wj or kind == "wr" or (r[4] and pj["q"] != o["q"])
+                    if clash and meets(r, rj) and not (o["q"] == "p" and pj["q"] == "p"):
+                        if not (pj["grp"] and pj["grp"] == o["grp"]):
+                            dep.add(j)
+        last = {}
+        for j in dep:
+            if not ops[j]["grp"]:
+                last[ops[j]["q"]] = max(last.get(ops[j]["q"], -1), j)
+        o["dep"] = (sorted(set(ops[j]["grp"] for j in dep if ops[j]["grp"])), last)
+        if o["q"] is not None:
+            need.update(last.values())
+        for kind in ("rd", "wr"):
+            for r in o[kind]:
+                seen.setdefault(r[0], []).append((i, kind == "wr", r))
+    eng = {"v": g.vector, "a": g.scalar, "p": g.tensor, "s": g.sync, "g": g, "r": g}
+    cnt, idx, waited = {"v": 0, "a": 0, "p": 0, "g": 0}, {}, {}
+    for i, o in enumerate(ops):
+        q = o["q"]
+        if q is None:
+            continue
+        qq = "g" if q == "r" else q
+        ws = [(semof[n], total[n]) for n in o["dep"][0]] + [("e_" + e, idx[j]) for e, j in sorted(o["dep"][1].items())]
+        for s, val in ws:
+            if waited.get((qq, s), 0) < val:
+                waited[(qq, s)] = val
+                eng[q].wait_ge(T.sem[s], val)
+        if q == "r":
+            o["fn"](T.sem[semof[o["grp"]]])
+        elif o["grp"]:
+            o["fn"]().then_inc(T.sem[semof[o["grp"]]], 16)
+        elif i in need:
+            cnt[q] += 1
+            idx[i] = cnt[q]
+            o["fn"]().then_inc(T.sem["e_" + q], 1)
+        else:
+            o["fn"]()
+    for n in sorted(total):
+        if waited.get(("g", semof[n]), 0) < total[n]:
+            g.wait_ge(T.sem[semof[n]], total[n])
+    for e in cnt:
+        if cnt[e]:
+            g.wait_ge(T.sem["e_" + e], cnt[e])

@@ -2,50 +2,53 @@ from concourse.bass import DstId, RemoteDMATransfer
 from concourse.mybir import AluOpType as AL, ActivationFunctionType as AF
 
 F32, BF, I32, U16 = "float32", "bfloat16", "int32", "uint16"
-NF = 26
-ZF0, SN2, SN1 = 15360, 17408, 12288
+SN2, SN1 = 15360, 12288
+EARLY = 2
+CH = [(1, 0, 512), (0, 0, 512), (1, 512, 1024), (0, 512, 768), (0, 768, 1024)]
+NC = len(CH)
+AHEAD = 40
 SCRATCH = {
-    "W1": ("sbuf", [128, 12288], BF), "W2": ("sbuf", [128, 13312], BF), "KB": ("sbuf", [128, 4096], BF),
-    "GB": ("sbuf", [128, 4096], BF), "XB": ("sbuf", [128, 12304], BF), "XF": ("sbuf", [128, 17416], F32),
+    "W1": ("sbuf", [128, 12288], BF), "W2": ("sbuf", [128, 12288], BF), "KB": ("sbuf", [128, 4096], BF),
+    "GB": ("sbuf", [128, 4096], BF), "XB": ("sbuf", [128, 12304], BF), "XF": ("sbuf", [128, 15368], F32),
     "CL": ("sbuf", [128, 1024], U16),
     "A0": ("sbuf", [128, 1024], F32), "A2": ("sbuf", [128, 1024], F32), "D0": ("sbuf", [128, 1024], F32),
     "D2": ("sbuf", [128, 1024], F32), "SS": ("sbuf", [128, 1024], F32), "ZI0": ("sbuf", [128, 1024], F32),
     "ZI1": ("sbuf", [128, 1024], F32), "DF": ("sbuf", [128, 1024], F32), "GP": ("sbuf", [128, 1024], F32),
+    "ZO0": ("sbuf", [128, 1024], F32), "ZO1": ("sbuf", [128, 1024], F32),
     "UU": ("sbuf", [128, 1024], BF), "VV": ("sbuf", [128, 1024], BF), "O0": ("sbuf", [128, 1024], BF),
     "O1": ("sbuf", [128, 1024], BF), "NR": ("sbuf", [128, 1024], BF),
-    "CT": ("sbuf", [128, 1024], BF), "ZM": ("sbuf", [128, 7 * 144], BF), "MM": ("sbuf", [128, 8 * 128], BF),
-    "UC": ("sbuf", [128, 16], BF), "SL": ("sbuf", [128, 128], BF),
-    "IN": ("sbuf", [128, 144], F32), "CO": ("sbuf", [128, NF * 16], F32), "PC": ("sbuf", [128, 8], F32),
-    "PI": ("sbuf", [128, 8], I32), "EP": ("sbuf", [128, 4], F32), "LE": ("dram", [8, 128, 1], F32), "SE": ("dram", [2, 128, 1], F32),
-    "ED": ("sbuf", [128, 4], F32),
-    "MI": ("sbuf", [128, 64], I32), "HM": ("sbuf", [128, 256], I32), "JT": ("sbuf", [128, 64], I32),
-    "TI": ("sbuf", [128, 2048], I32), "TF": ("sbuf", [128, 256], F32),
-    "UL": ("sbuf", [128, 1344], U16),
-    "MS0": ("sbuf", [128, 192], I32), "MS1": ("sbuf", [128, 192], I32),
-    "EM0": ("sbuf", [128, 192], I32), "EM1": ("sbuf", [128, 192], I32),
-    "ST": ("sbuf", [128, 640], I32), "EN": ("sbuf", [128, 384], I32),
+    "CT": ("sbuf", [128, 1024], BF), "ZM": ("sbuf", [128, 7 * 144], BF), "MM": ("sbuf", [128, 9 * 128], BF),
+    "SL": ("sbuf", [128, 2, 64], BF),
+    "IN": ("sbuf", [128, 144], F32), "JB": ("sbuf", [128, 168], F32), "PC": ("sbuf", [128, 24], F32),
+    "EE": ("sbuf", [128, 24], F32), "BC": ("sbuf", [128, 68], F32),
+    "PJ": ("sbuf", [128, 40], I32), "EP": ("sbuf", [128, 4], F32), "EW": ("sbuf", [128, 16], F32), "ED": ("sbuf", [128, 16], F32),
+    "MI": ("sbuf", [128, 64], I32), "HM": ("sbuf", [128, 2, 256], F32),
+    "TI": ("sbuf", [128, 2048], I32), "TF": ("sbuf", [128, 2, 448], F32), "FI": ("sbuf", [128, 2, 256], I32),
+    "UL": ("sbuf", [128, 704], U16), "LS": ("sbuf", [128, 2, 64], U16), "UV": ("sbuf", [128, 2, 64], U16),
+    "OW": ("sbuf", [128, 2, 128], U16),
+    "MS": ("sbuf", [128, 2, 192], F32), "EM": ("sbuf", [128, 2, 192], F32), "EN": ("sbuf", [128, 2, 192], F32),
+    "ST0": ("sbuf", [128, 2, 192], F32), "ST1": ("sbuf", [128, 2, 192], F32),
+    "SE": ("dram", [8, 128, 2], F32), "LE": ("dram", [8, 128, 2], F32),
     "SM": ("dram", [8, 128, 8], I32), "LM": ("dram", [8, 128, 8], I32),
     "SC0": ("dram", [8, 128, 64], U16), "LC0": ("dram", [8, 128, 64], U16),
     "SC1": ("dram", [8, 128, 64], U16), "LC1": ("dram", [8, 128, 64], U16),
     "SF": ("dram", [16, 128, 128], BF), "LF": ("dram", [16, 128, 128], BF),
-    "SX": ("dram", [16, 128, 256], BF), "LX": ("dram", [8, 128, 256], BF),
+    "SX": ("dram", [32, 128, 128], BF), "LX": ("dram", [8, 128, 128], BF),
     "SH": ("dram", [8, 128, 64], F32), "LH": ("dram", [8, 128, 64], F32),
-    "SZ0": ("dram", [8, 128, 64], F32), "LZ0": ("dram", [8, 128, 64], F32),
-    "SZ1": ("dram", [8, 128, 64], F32), "LZ1": ("dram", [8, 128, 64], F32),
-    "SZ2": ("dram", [8, 128, 64], F32), "LZ2": ("dram", [8, 128, 64], F32),
-    "SZ3": ("dram", [8, 128, 32], F32), "LZ3": ("dram", [8, 128, 32], F32),
-    "SZ4": ("dram", [8, 128, 32], F32), "LZ4": ("dram", [8, 128, 32], F32),
-    "P0": ("psum", [128, 512], F32), "P1": ("psum", [128, 512], F32), "P2": ("psum", [128, 512], F32),
-    "P3": ("psum", [128, 512], F32), "P4": ("psum", [128, 512], F32), "P5": ("psum", [128, 512], F32),
-    "P6": ("psum", [128, 512], F32), "P7": ("psum", [128, 512], F32),
 }
-ARR = ["a_ms", "a_c0", "a_c1", "a_w1", "a_w2", "a_xb", "h_in", "h_z", "h_x", "h_fl", "h_f0", "h_f1", "h_f2", "h_f3", "h_f4", "h_f5", "a_fl", "a_eps", "a_st00", "a_st01", "a_st10", "a_st11", "a_en00", "a_en01",
-       "a_en10", "a_en11", "a_mh"] + ["a_z%d" % i for i in range(5)] + ["a_f%d" % i for i in range(5)]
-SEMAPHORES = ARR + ["e_v", "e_a", "e_p", "e_g"] + ["d%d" % i for i in range(100)]
+for _c, (_s, _a, _b) in enumerate(CH):
+    SCRATCH["SZ%d" % _c] = ("dram", [8, 128, (_b - _a) // 8], F32)
+    SCRATCH["LZ%d" % _c] = ("dram", [8, 128, (_b - _a) // 8], F32)
+for _c in range(8):
+    SCRATCH["P%d" % _c] = ("psum", [128, 2, 256] if _c == 1 else [128, 512], F32)
+ARR = (["a_ms", "a_c0", "a_c1", "a_w1", "a_w2", "a_xb", "h_in", "h_z", "h_x", "h_c1", "h_fl", "a_fl", "a_eps", "a_mh"]
+       + ["h_r%d" % i for i in range(NC - 1)]
+       + ["a_%s%d%d" % (n, r, s) for n in ("st", "en") for r in range(2) for s in range(2)]
+       + ["a_z%d" % i for i in range(NC)] + ["a_f%d" % i for i in range(NC)] + ["h_f%d" % i for i in range(NC + 1)])
+SEMAPHORES = ARR + ["e_v", "e_a", "e_p", "e_g"] + ["d%d" % i for i in range(95)]
 IO = {"x": [128, 4096], "eps": [128, 1], "fl": [32, 4096], "cor": [128, 1024], "ms": [128, 64],
       "y": [128, 1024], "ye": [128, 1024], "yf": [40, 1024]}
 ALL = slice(None)
-CH = [(1, 0, 512), (1, 512, 1024), (0, 0, 512), (0, 512, 768), (0, 768, 1024)]
 
 
 def diag_ring(T, topo):
@@ -78,6 +81,14 @@ def C(name, a, b, step=1):
     return (name, (ALL, slice(a, b, step) if step != 1 else slice(a, b)))
 
 
+def one(name, s, i, n=1, p=ALL):
+    return (name, (p, s, slice(64 * i, 64 * (i + n))))
+
+
+def two(name, i, n=1):
+    return (name, (ALL, ALL, slice(64 * i, 64 * (i + n))))
+
+
 def IND(win, off):
     return ("*", win, off)
 
@@ -87,12 +98,18 @@ def region(v):
     shp = IO[name] if name in IO else SCRATCH[name][1]
     p = idx[0]
     ps = frozenset(range(*p.indices(shp[0]))) if isinstance(p, slice) else frozenset([p])
-    if name not in IO and SCRATCH[name][0] == "psum":
-        return (name, frozenset(range(128)), 0, 512, True)
+    bank = name not in IO and SCRATCH[name][0] == "psum"
+    if len(idx) == 3 and SCRATCH[name][0] != "dram":
+        a, b, _ = idx[2].indices(shp[2])
+        if idx[1] != ALL:
+            ps = frozenset((q, idx[1]) for q in ps)
+        else:
+            ps = frozenset((q, s) for q in ps for s in range(2))
+        return (name, ps, a, b, bank)
     if len(idx) > 1:
         r = range(*idx[1].indices(shp[1]))
-        return (name, ps, r[0], r[-1] + 1, False)
-    return (name, ps, 0, shp[1], False)
+        return (name, ps, r[0], r[-1] + 1, bank)
+    return (name, ps, 0, shp[1], bank)
 
 
 def dst_id(topo, c):
@@ -101,15 +118,40 @@ def dst_id(topo, c):
 
 def helpers(T, topo, c):
     mine = [o for o in topo.cores_of(c) if o != c]
-    near = [o for o in mine if topo.die(o) == topo.die(c)]
-    far = [o for o in mine if topo.die(o) != topo.die(c) and all(topo.may_write(o, t) for t in T.cores)]
-    return near, far[:2]
+    out = []
+    for same in (False, True):
+        die = [o for o in mine if (topo.die(o) == topo.die(c)) == same]
+        wide = [o for o in die if all(topo.may_write(o, t) for t in T.cores)]
+        out.append((wide, [o for o in die if o not in wide]))
+    return out
 
 
 def carriers(T, topo, c):
-    near, far = helpers(T, topo, c)
-    wide = far + [o for o in near if all(topo.may_write(o, t) for t in T.cores)]
-    return [wide[0], wide[1], c, wide[2], c, wide[0]]
+    far, near = helpers(T, topo, c)
+    two = [(far[1][0], far[0][0]), (far[1][1], far[0][1]), (near[1][0], near[0][0])]
+    return [two[0], (), (), (), (), two[1]]
+
+
+def relays(T, topo, c, dst, i):
+    out = []
+    for wide, narrow in helpers(T, topo, c):
+        can = narrow if topo.may_write(narrow[0], dst) else wide
+        out.append(can[i % len(can)])
+    return out
+
+
+def routes(T, topo, boss, dies):
+    out = []
+    for h, d in enumerate(dies):
+        wide, narrow = helpers(T, topo, boss)[d]
+        for c, v, gm in input_plan(T, diag_ring(T, topo), T.rank_of(boss)):
+            can = narrow if topo.may_write(narrow[0], c) else wide
+            load = [len([r for r in out if r[0] == o]) for o in can]
+            out.append((boss if c == boss else can[load.index(min(load))], c, len(dies) * v + h, len(dies) * gm + h))
+    return out
+
+
+RELAYED = (("c1", "SC1", "LC1", (0,)), ("fl", "SF", "LF", (0, 1)))
 
 
 def input_plan(T, ring, rank):
@@ -121,75 +163,108 @@ def final_plan(T, k, s):
     return [(T.cores[r], gm, (r + k + (1, -1, 0)[s]) % 8) for gm, r in enumerate(rs)]
 
 
+def x_routes(T, topo, boss):
+    out = []
+    for q in range(4):
+        wide, narrow = helpers(T, topo, boss)[q // 2]
+        for c, v, gm in input_plan(T, diag_ring(T, topo), T.rank_of(boss)):
+            lay = helpers(T, topo, c)[q // 2][1][q % 2]
+            who = boss if c == boss else (narrow[q % 2] if topo.may_write(narrow[q % 2], lay) else wide[q % len(wide)])
+            out.append((who, lay, 8 * q + v, gm))
+    return out
+
+
+def x_width(routes, who, boss):
+    n = len([r for r in routes if r[0] == who])
+    return 1 if who == boss or n > 4 else (2 if n > 2 else 4)
+
+
 def helper_program(g, core, T, topo):
     boss = [c for c in T.cores if topo.chip(c) == topo.chip(core)]
     if not boss:
         return
     boss = boss[0]
-    near, far = helpers(T, topo, boss)
+    far, near = helpers(T, topo, boss)
+    near = near[1] + near[0]
     S = T.sem
     rank, ring = T.rank_of(boss), diag_ring(T, topo)
-    n = len(topo.engines(boss, core))
+    m, n = topo.mask(core, boss), len(topo.engines(core, boss))
+    rid, pid, _ = topo.addr(boss)
+    sent = [0]
 
-    def deal(plan, src, dst, sem):
-        g.remote_dma_fused([RemoteDMATransfer(dst_ids=[dst_id(topo, c)], dma_engine_mask=1 << topo.engines(core, c)[e],
-                                              remote_sem=S[sem], src=T[src][i], dst=T[dst][j])
+    def deal(plan, src, dst, sem, w=1):
+        g.remote_dma_fused([RemoteDMATransfer(dst_ids=[dst_id(topo, c)], remote_sem=S[sem], src=T[src][i], dst=T[dst][j],
+                                              dma_engine_mask=sum(1 << x for x in topo.engines(core, c)[w * e:w * e + w]))
                             for e, (c, i, j) in enumerate(plan)], local_sem=S["d0"])
+        sent[0] += w * len(plan)
 
-    def blends():
-        mine = [c for c, o in enumerate(carriers(T, topo, boss)) if o == core]
-        for c in mine:
-            if c == len(CH):
-                g.wait_ge(S["h_f%d" % c], n)
-                deal(final_plan(T, ring.index(rank), 2), "SH", "LH", "a_mh")
-                continue
-            s, a, b = CH[c]
-            g.sync.wait_ge(S["h_f%d" % c], n)
-            g.sync.dma_start(T["SZ%d" % c][:], T["ZI%d" % s][:, a:b]).then_inc(S["d%d" % (10 + c)], 16)
-            g.wait_ge(S["d%d" % (10 + c)], 16)
-            deal(final_plan(T, ring.index(rank), s), "SZ%d" % c, "LZ%d" % c, "a_f%d" % c)
-        return 8 * len(mine)
+    def zeros(buf, js, sem):
+        g.remote_dma_fused([RemoteDMATransfer(dst_ids=[dst_id(topo, boss)] * len(js), dma_engine_mask=m, remote_sem=S[sem],
+                                              src=T["O0"][:, 0:512], dsts=[T[buf][:, 512 * j:512 * j + 512] for j in js])],
+                           local_sem=S["d0"])
+        sent[0] += n
 
-    if core in far:
-        hf = far.index(core)
-        plan = input_plan(T, ring, rank)
-        g.wait_ge(S["h_fl"], n)
-        deal([(c, 2 * i + hf, 2 * j + hf) for c, i, j in plan], "SF", "LF", "a_fl")
-        g.wait_ge(S["h_in"], n)
-        deal([(helpers(T, topo, c)[0][1 + hf], i, j) for c, i, j in plan], "SX", "LX", "h_x")
-        g.wait_ge(S["d0"], 16 + blends())
     if core in near:
         i = near.index(core)
-        m, n = topo.mask(core, boss), len(topo.engines(core, boss))
-        rid, pid, _ = topo.addr(boss)
-        sent = 0
-
-        def spread(dsts, cores, sem):
-            g.remote_dma_fused([RemoteDMATransfer(dst_ids=[dst_id(topo, c) for c in cores], dma_engine_mask=m, remote_sem=S[sem],
-                                                  src=T["O0"][:, 0:512], dsts=dsts)], local_sem=S["d0"])
         g.wait_ge(S["h_z"], n)
-        if i == 0:
-            spread([T["O0"][:, 0:512]] * 2, near[1:], "h_z")
-            sent += n
-        spread([T["W1"][:, 512 * j:512 * j + 512] for j in range(8 * i, 8 * i + 8)], [boss] * 8, "a_w1")
-        js = range(8 + (0, 6, 11)[i], 8 + (6, 11, 16)[i])
-        spread([T["W2"][:, 512 * j:512 * j + 512] for j in js], [boss] * len(js), "a_w2")
-        sent += 2 * n
-        if i:
-            a = 2048 * (i - 1)
-            XB, LX = T["XB"], T["LX"]
-            g.sync.wait_ge(S["h_x"], 8)
-            g.sync.dma_start(XB[0:112, 8192 + a:10240 + a], LX[1:8]).then_inc(S["d3"], 16)
-            g.sync.dma_start(XB[112:128, 8192 + a:10240 + a], LX[0]).then_inc(S["d3"], 16)
-            g.sync.dma_start(XB[:, a:a + 2048], LX[:]).then_inc(S["d1"], 16)
-            g.sync.dma_start(XB[16:128, 4096 + a:6144 + a], LX[0:7]).then_inc(S["d2"], 16)
-            g.sync.dma_start(XB[0:16, 4096 + a:6144 + a], LX[7]).then_inc(S["d2"], 16)
-            for sl, cnt in ((2, 32), (0, 16), (1, 32)):
-                g.wait_ge(S["d%d" % (sl + 1)], cnt)
-                blk = XB[:, 4096 * sl + a:4096 * sl + a + 2048]
-                g.remote_dma(blk, blk, S["a_xb"], S["d0"], pid, rid, m)
-            sent += 3 * n
-        g.wait_ge(S["d0"], sent + blends())
+        zeros("W1", range(8 * i, 8 * i + 8), "a_w1")
+    for name, src, dst, dies in RELAYED:
+        way = routes(T, topo, boss, dies)
+        mine = [(c, i, j) for who, c, i, j in way if who == core]
+        if mine:
+            g.wait_ge(S["h_" + name], len(mine))
+            deal(mine, src, dst, "a_" + name, x_width(way, core, boss))
+    if core in near:
+        zeros("W2", (list(range(8)) + list(range(16, 24)))[near.index(core)::3], "a_w2")
+    way = x_routes(T, topo, boss)
+    mine = [(lay, i, j) for who, lay, i, j in way if who == core]
+    if mine:
+        g.wait_ge(S["h_in"], len(mine))
+        deal(mine, "SX", "LX", "h_x", x_width(way, core, boss))
+    comes = [(i // 8, x_width(x_routes(T, topo, c), who, c)) for c in T.cores
+             for who, lay, i, j in x_routes(T, topo, c) if lay == core]
+    if comes:
+        a = 1024 * comes[0][0]
+        XB, LX = T["XB"], T["LX"]
+        g.sync.wait_ge(S["h_x"], sum(w for q, w in comes))
+        g.scalar.wait_ge(S["h_x"], sum(w for q, w in comes))
+        g.sync.dma_start(XB[16:128, a:a + 1024], LX[0:7]).then_inc(S["d1"], 16)
+        g.scalar.dma_start(XB[0:16, a:a + 1024], LX[7]).then_inc(S["d1"], 16)
+        g.sync.dma_start(XB[0:112, 8192 + a:9216 + a], LX[1:8]).then_inc(S["d3"], 16)
+        g.scalar.dma_start(XB[112:128, 8192 + a:9216 + a], LX[0]).then_inc(S["d3"], 16)
+        g.sync.dma_start(XB[:, 4096 + a:5120 + a], LX[:]).then_inc(S["d2"], 16)
+        for sl, cnt in ((0, 32), (2, 32), (1, 16)):
+            g.wait_ge(S["d%d" % (sl + 1)], cnt)
+            blk = XB[:, 4096 * sl + a:4096 * sl + a + 1024]
+            g.remote_dma(blk, blk, S["a_xb"], S["d0"], pid, rid, m)
+            sent[0] += n
+    k = ring.index(rank)
+    for c in range(EARLY):
+        s, a, b = CH[c]
+        dst = T.cores[ring[(k + 1 - 2 * s) % 8]]
+        who = relays(T, topo, boss, dst, c)
+        if core in who:
+            a, b = ((a, (a + b) // 2), ((a + b) // 2, b))[who.index(core)]
+            g.wait_ge(S["h_r%d" % c], n // 2)
+            g.remote_dma(T["ZI%d" % s][:, a:b], T["ZO%d" % s][:, a:b], S["a_z%d" % c], S["d0"], topo.addr(dst)[1], topo.addr(dst)[0],
+                         topo.mask(core, dst))
+            sent[0] += len(topo.engines(core, dst))
+    carry = carriers(T, topo, boss)
+    for c in [0, 1, 2, NC] + list(range(3, NC)):
+        if core not in carry[c]:
+            continue
+        s = CH[c][0] if c < NC else 2
+        plan = [p for p in final_plan(T, k, s) if topo.may_write(carry[c][0], p[0]) == (core == carry[c][0])]
+        if c == NC:
+            g.wait_ge(S["h_f%d" % c], 2 * len(plan))
+            deal(plan, "SH", "LH", "a_mh", 2)
+            continue
+        s, a, b = CH[c]
+        g.sync.wait_ge(S["h_f%d" % c], n)
+        g.sync.dma_start(T["SZ%d" % c][:], T["ZO%d" % s][:, a:b]).then_inc(S["d%d" % (10 + c)], 16)
+        g.wait_ge(S["d%d" % (10 + c)], 16)
+        deal(plan, "SZ%d" % c, "LZ%d" % c, "a_f%d" % c, 2)
+    g.wait_ge(S["d0"], sent[0])
 
 
 def rank_program(g, core, T, topo):
@@ -244,12 +319,12 @@ def rank_program(g, core, T, topo):
     def mm(o, l, r, st, sp):
         rec("p", lambda: g.tensor.matmul(ap(o), ap(l), ap(r), st, sp), [o], [l, r])
 
-    def dma(q, o, a, grp, slow=False, after=None):
+    def dma(q, o, a, grp, slow=False):
         eng = {"s": g.sync, "a": g.scalar, "g": g}[q]
         if slow:
             rec(q, lambda: eng.dma_start(ap(o), ap(a), allow_slow_non_contiguous=True), [o], [a], grp, 16)
         else:
-            rec(q, lambda: eng.dma_start(ap(o), ap(a)), [o], [a, after], grp, 16)
+            rec(q, lambda: eng.dma_start(ap(o), ap(a)), [o], [a], grp, 16)
 
     def iota(o, pat, base, cm, small=False):
         if small:
@@ -267,8 +342,14 @@ def rank_program(g, core, T, topo):
         rec("r", lambda ls: g.remote_dma(ap(o), ap(a), T.sem[name], ls, pid, rid, m), [], [a], "t" + name, n)
         return n
 
-    def deal(name, src, dst, plan, q="s", stage=None, own_src=None, after=None):
-        tr, rd = [], [after] if after else []
+    def fused(name, tr):
+        rec("r", lambda ls: g.remote_dma_fused(
+            [RemoteDMATransfer(dst_ids=[dst_id(topo, c)], dma_engine_mask=sum(1 << e for e in es), remote_sem=T.sem[sem],
+                               src=ap(a), dst=ap(o)) for c, es, sem, a, o in tr], local_sem=ls),
+            [], [t[3] for t in tr], "t" + name, sum(len(t[1]) for t in tr))
+
+    def deal(name, src, dst, plan, q="s", stage=None, own_src=None):
+        tr = []
         if stage:
             dma(q, V(src), stage, "s" + name)
         for c, i, j in plan:
@@ -276,582 +357,663 @@ def rank_program(g, core, T, topo):
                 dma(q, V(dst, j), own_src(i) if own_src else V(src, i), "l" + name)
                 own = j
             else:
-                rid, pid, _ = topo.addr(c)
-                tr.append((rid, pid, 1 << topo.engines(core, c)[len(tr)], i, j))
-                rd.append(V(src, i))
-        rec("r", lambda ls: g.remote_dma_fused(
-            [RemoteDMATransfer(dst_ids=[DstId(rid=a, pnc=b)], dma_engine_mask=m, remote_sem=T.sem[name],
-                               src=ap(V(src, i)), dst=ap(V(dst, j))) for a, b, m, i, j in tr], local_sem=ls),
-            [], rd, "t" + name, len(tr))
-        st = len(SCRATCH[dst][1]) and SCRATCH[dst][1][0] // 8
-        arrive(name, [V(dst, j) for j in range(own % st, 8 * st, st) if j != own], len(tr))
+                tr.append((c, [topo.engines(core, c)[len(tr)]], name, V(src, i), V(dst, j)))
+        fused(name, tr)
+        arrive(name, [V(dst, j) for j in range(8) if j != own], len(tr))
 
-    def col(f):
-        return C("CO", 16 * f + 15, 16 * f + 16)
+    def relay(name, src, dst, dies):
+        way = routes(T, topo, core, dies)
+        fused(name, [(who, [topo.engines(core, who)[e]], "h_" + name, V(src, i), V(src, i))
+                     for e, (who, c, i, j) in enumerate(way) if who != core])
+        own = [(i, j) for who, c, i, j in way if who == core]
+        for i, j in own:
+            dma("s", V(dst, j), V(src, i), "l" + name)
+        arrive("a_" + name, [V(dst, j) for j in range(len(way)) if j not in [o[1] for o in own]],
+               sum(x_width(routes(T, topo, o, dies), who, o) for o in T.cores if o != core
+                   for who, c, i, j in routes(T, topo, o, dies) if c == core))
+
+    def spread(name, cores, a):
+        rec("r", lambda ls: g.remote_dma_fused(
+            [RemoteDMATransfer(dst_ids=[dst_id(topo, c) for c in cores], dma_engine_mask=topo.mask(core, cores[0]),
+                               remote_sem=T.sem[name], src=ap(a), dsts=[ap(a)] * len(cores))], local_sem=ls),
+            [], [a], "t" + name, len(topo.engines(core, cores[0])))
+
+    folds = []
+
+    def fold(name):
+        tr = list(folds)
+        del folds[:]
+        rec("r", lambda ls: g.remote_dma_fused(
+            [RemoteDMATransfer(dst_ids=[dst_id(topo, c) for c in cs], dma_engine_mask=sum(1 << e for e in es), remote_sem=T.sem[name],
+                               srcs=[ap(a) for a in srcs], dsts=[ap(o)] * len(cs), alu_op=1) for cs, es, srcs, o in tr], local_sem=ls),
+            [], [a for t in tr for a in t[2]], "t" + name, sum(len(t[1]) for t in tr))
+
+    (PP, G16, GG, LT8, ODD, EVN, CTB, SRB, F21, WF, WB, T0, T1, T3, SMK, LE8, NLE8, HF8, SU, SV, C4, C5) = range(22)
+
+    def col(f, n=1):
+        return C("PC", f, f + n)
+
+    def row(i):
+        return C("EE", i, i + 1)
+
+    def pair(i):
+        return C("EE", 16 + i, 17 + i)
 
     def wrap(out, f, src, first=True, last=True):
         for q in range(16):
-            mm(out, C("ZM", 144 * f + 15 - q, 144 * f + 143 - q), C(src[0], src[1] + q, src[1] + 1024, 16),
-               first and q == 0, last and q == 15)
+            mm(out, C("ZM", 144 * f + 15 - q, 144 * f + 143 - q), C(src, q, 1024, 16), first and q == 0, last and q == 15)
 
     def mat(i, m=128):
         return C("MM", 128 * i, 128 * i + m)
-    I1, I1024, ONES, DH, DHN, EO, EN_, C40 = range(8)
+    I1, ONES, SELU, SELV, DH, DHN, EO, EN_, C40 = range(9)
 
     def grp(gm, a, b):
         return slice(16 * (gm % 8) + a, 16 * (gm % 8) + b)
 
-    def rows_to_slots(q, dst, r1, src, r0, name, mid=True, side=True):
+    def rows_to_slots(q, dst, r1, src, r0, name, mid=True, side=True, c0=0, d0=0):
+        cs = slice(c0, c0 + 4096 - d0)
         if side:
-            dma(q, V(dst, slice(16 + r1, 128, 16), slice(4096, 8192)), V(src, slice(r0, 112, 16), slice(0, 4096)), name)
-            dma(q, V(dst, slice(r1, 112, 16), slice(8192, 12288)), V(src, slice(16 + r0, 128, 16), slice(0, 4096)), name)
-            dma(q, V(dst, slice(r1, r1 + 1), slice(4096, 8192)), V(src, slice(112 + r0, 113 + r0), slice(0, 4096)), name)
-            dma(q, V(dst, slice(112 + r1, 113 + r1), slice(8192, 12288)), V(src, slice(r0, r0 + 1), slice(0, 4096)), name)
+            dma(q, V(dst, slice(16 + r1, 128, 16), slice(d0, 4096)), V(src, slice(r0, 112, 16), cs), name)
+            dma(q, V(dst, slice(r1, 112, 16), slice(8192 + d0, 12288)), V(src, slice(16 + r0, 128, 16), cs), name)
+            dma(q, V(dst, slice(r1, r1 + 1), slice(d0, 4096)), V(src, slice(112 + r0, 113 + r0), cs), name)
+            dma(q, V(dst, slice(112 + r1, 113 + r1), slice(8192 + d0, 12288)), V(src, slice(r0, r0 + 1), cs), name)
         if mid:
-            dma(q, V(dst, slice(r1, 128, 16), slice(0, 4096)), V(src, slice(r0, 128, 16), slice(0, 4096)), name)
+            dma(q, V(dst, slice(r1, 128, 16), slice(4096 + d0, 8192)), V(src, slice(r0, 128, 16), cs), name)
 
     in_plan = input_plan(T, ring, rank)
     nb = [dcore[(k - 1) % 8], dcore[(k + 1) % 8]]
     src_nb = [nb[1], nb[0]]
+    near = helpers(T, topo, core)[1]
+    near = near[1] + near[0]
+    carry = carriers(T, topo, core)
+    wide = len(topo.engines(core, near[0]))
 
     def nin(c):
         return len(topo.engines(c, core))
 
+    MSL, NB1, NB2, TL = 0, 64, 128, 192
+    CQ = float(512 + 512 * 1024)
+    FB = C("W1", 4096, 8192)
+    BIG = float(2 ** 21)
+    MOVE = 16384.0
+    R1 = 1.5 * 2 ** 23
+    pm = C("PJ", 16, 17)
+    n128 = C("IN", 0, 128)
+
     dma("a", V("SM"), V("ms"), "sm")
     dma("s", C("TI", 0, 512), C("cor", 0, 512), "ci0")
-    dma("s", C("TI", 1024, 2048), V("fl"), "fi")
-    near, far = helpers(T, topo, core)
-
-    carry = carriers(T, topo, core)
-
-    def hand(buf, src, dst, c, sem):
-        es = topo.engines(core, c)
-        rec("r", lambda ls: g.remote_dma_fused(
-            [RemoteDMATransfer(dst_ids=[dst_id(topo, c)], dma_engine_mask=sum(1 << e for e in es[v::8]), remote_sem=T.sem[sem],
-                               src=ap(V(buf, src[v])), dst=ap(V(buf, dst[v]))) for v in range(8)], local_sem=ls),
-            [], [V(buf, i) for i in src], "t%s%d" % (buf, c), len(es))
-
-    wt = [(0, 3, 7, 2, 1), (0, 9, 13, 2, 1), (7, 2, 6, 2, 64), (7, 1, 2, 1, 1), (8, 1, 2, 1, 1), (8, 4, 6, 1, 1),
-          (9, 2, 9, 6, 1), (9, 3, 10, 6, 1), (9, 4, 11, 6, 2), (9, 5, 12, 6, 2),
-          (10, 0, 16, 2, -16),
-          (11, 0, 21, 20, 32), (11, 1, 22, 20, 1), (11, 2, 23, 20, 32768), (11, 3, 24, 20, 1024),
-          (11, 9, 11, 1, 2 ** 21), (12, 9, 11, 1, 2 ** 21),
-          (13, 1, 64, 16, 32768), (13, 7, 64, 16, 32768),
-          (13, 2, 21, 18, 64), (13, 3, 22, 18, 1), (15, 8, 27, 18, 64), (15, 9, 28, 18, 1),
-          (14, 2, 41, 38, -64), (14, 3, 42, 38, -1),
-          (17, 0, 55, 18, 1), (17, 1, 56, 18, 1), (21, 0, 8, 1, 1), (22, 8, 9, 1, 1), (23, 0, 9, 1, 1),
-          (24, 0, 8, 2, 16), (24, 1, 8, 2, 0.5), (25, 1, 16, 2, 1)]
-    wt += [(1 + i, 0, 16, 2, 2 ** i) for i in range(6)]
-
-    def weights(f0, f1):
-        fill(C("GP", 16 * f0, 16 * f1), 0.0)
-        for f, x0, x1, s, val in wt:
-            if f0 <= f < f1:
-                fill(C("GP", 16 * f + x0, 16 * f + x1, s), float(val))
-
-    def columns(f0, f1):
-        a, b = 16 * f0, 16 * f1
-        if f0 == 0:
-            ts(C("PI", 1, 2), C("PI", 0, 1), 15, AL.bitwise_and)
-            cp(C("PC", 0, 2), C("PI", 0, 2))
-        ts(C("A2", a, b), C("DF", a, b), 0.0, AL.is_gt)
-        ts(C("A0", a, b), C("DF", a, b), C("PC", 1, 2), AL.is_equal)
-        tt(C("A0", a, b), C("A0", a, b), C("GP", a, b), AL.mult)
-        rec("v", lambda: g.vector.tensor_tensor_scan(ap(C("CO", a, b)), ap(C("A2", a, b)), ap(C("A0", a, b)), 0.0,
-                                                     AL.mult, AL.add), [C("CO", a, b)], [C("A2", a, b), C("A0", a, b)])
-
-    iota(C("PI", 0, 1), [[1, 1]], 0, 1)
-    iota(C("DF", 0, 160), [[0, 10], [1, 16]], 0, 0, True)
-    iota(V("IN"), [[1, 144]], 0, 0, True)
+    dma("a", C("TI", 1024, 2048), V("fl"), "fi")
+    dma("s", C("TI", 512, 1024), C("cor", 512, 1024), "ci1")
     fill(C("O0", 0, 512), 0.0)
-    send(near[0], C("O0", 0, 512), C("O0", 0, 512), "h_z")
-    iota(C("DF", 160, 16 * NF), [[0, NF - 10], [1, 16]], 0, 0, True)
+    iota(C("PJ", 0, 16), [[-1, 16]], 16, 1)
+    iota(V("IN"), [[1, 144]], 0, 0, True)
+    spread("h_z", near, C("O0", 0, 512))
     deal("a_ms", "SM", "LM", in_plan, "a", own_src=lambda i: V("ms", grp(i, 0, 16)))
-    weights(0, 10)
-    columns(0, 10)
-    act(C("KB", 0, 64), C("IN", 0, 64), scale=col(0))
-    for i in range(6):
-        act(C("KB", 64 << i, 128 << i), C("KB", 0, 64 << i), bias=col(1 + i))
+    ts(C("PJ", 16, 32), C("PJ", 0, 16), 15, AL.bitwise_and)
+    ts(C("PJ", 32, 33), C("PJ", 0, 1), 1, AL.bitwise_and)
+    ts(col(LT8), pm, 8.0, AL.is_lt)
+    ts(C("EE", 0, 16), C("PJ", 16, 32), 0.0, AL.is_equal)
+    ts(col(ODD), C("PJ", 32, 33), col(LT8), AL.mult)
+    tt(col(EVN), col(LT8), col(ODD), AL.subtract)
+    ts(C("KB", 0, 64), C("IN", 0, 64), col(ODD), AL.mult)
+    ts(C("BC", 0, 65), C("IN", 0, 65), col(EVN), AL.mult, 64.0, AL.mult)
+    for i in range(4):
+        ts(C("KB", 64 << i, 128 << i), C("KB", 0, 64 << i), C("BC", 1 << i, (1 << i) + 1), AL.add)
+    ts(col(F21), row(8), BIG, AL.mult)
+    ts(col(SRB), row(8), BIG, AL.mult, C("BC", 64, 65), AL.add)
+    ts(col(CTB), col(EVN), -512.0, AL.mult)
+    ts(C("KB", 1024, 2048), C("KB", 0, 1024), C("BC", 16, 17), AL.add)
+    act(C("KB", 2048, 4096), C("KB", 0, 2048), bias=C("BC", 32, 33))
     cp(C("CL", 0, 512), C("TI", 0, 512))
     deal("a_c0", "SC0", "LC0", in_plan, stage=C("CL", 0, 512), own_src=lambda i: V("CL", grp(i, 0, 16), slice(0, 512)))
-    dma("s", C("TI", 512, 1024), C("cor", 512, 1024), "ci1")
-    dma("s", V("MI"), V("LM"), "mi")
-    iota(V("JT"), [[16, 64]], 12288, 1)
-    weights(10, NF)
-    columns(10, NF)
-    act(C("GB", 2048, 3072), C("KB", 0, 1024), bias=col(7))
-    act(C("W2", 12288, 13312), C("KB", 0, 1024), scale=col(9))
+    cp(C("CL", 512, 1024), C("TI", 512, 1024))
+    dma("s", V("SC1"), C("CL", 512, 1024), "sc1")
+    relay(*RELAYED[0])
+    iota(C("JB", 0, 128), [[1, 8], [0, 16]], 0, 0, True)
+    iota(C("JB", 128, 168), [[0, 5], [1, 8]], 0, 0, True)
     for h in range(2):
         fi = C("TI", 1024 + 512 * h, 1536 + 512 * h)
-        ts(C("TI", 0, 512), fi, 5, AL.arith_shift_right)
-        ts(fi, fi, 31, AL.bitwise_and)
-        cp(C("GB", 512 * h, 512 * h + 512), C("TI", 0, 512))
-        cp(C("GB", 1024 + 512 * h, 1536 + 512 * h), fi)
-        if h == 0:
-            cp(C("CL", 512, 1024), C("TI", 512, 1024))
-            deal("a_c1", "SC1", "LC1", in_plan, stage=C("CL", 512, 1024),
-                 own_src=lambda i: V("CL", grp(i, 0, 16), slice(512, 1024)))
-    dma("a", C("CL", 0, 512), V("LC0"), "cl0")
+        ts(V("P%d" % (2 + h)), fi, 32 * R1, AL.add, 32 * R1, AL.subtract)
+        tt(C("GB", 1024 + 512 * h, 1536 + 512 * h), fi, V("P%d" % (2 + h)), AL.subtract)
+        act(C("GB", 512 * h, 512 * h + 512), V("P%d" % (2 + h)))
     for i in range(8):
-        dma("s", V("SF", slice(i // 4, 16, 2), slice(32 * (i % 4), 32 * (i % 4) + 32)),
-            V("GB", slice(32 * (i // 2), 32 * (i // 2) + 32), slice(1024 * (i % 2), 1024 * (i % 2) + 1024)), "sf%d" % (i // 4))
-    MSL, NB1, NB2, LS, UVL, TL, OWL = 0, 64, 128, 192, 320, 576, 1088
+        dma("sa"[i % 2], V("SF", slice(i // 4, 16, 2), slice(32 * (i % 4), 32 * (i % 4) + 32)),
+            V("GB", slice(32 * (i // 2), 32 * (i // 2) + 32), slice(1024 * (i % 2), 1024 * (i % 2) + 1024)), "sf")
+    dma("s", V("MI"), V("LM"), "mi")
+    dma("s", C("CL", 0, 512), V("LC0"), "cl0")
+    act(C("GB", 2048, 3072), C("KB", 0, 1024), bias=col(SRB))
+    act(V("CT"), C("KB", 0, 1024), bias=col(CTB))
+    relay(*RELAYED[1])
+    tt(C("EE", 16, 24), C("EE", 0, 16, 2), C("EE", 1, 16, 2), AL.add)
+    ts(C("PJ", 33, 34), C("PJ", 0, 1), 4, AL.arith_shift_right)
+    ts(col(PP), C("PJ", 0, 1), -16.0, AL.add)
+    ts(col(G16), C("PJ", 33, 34), 16.0, AL.mult, -1.0, AL.add)
+    ts(col(GG), C("PJ", 33, 34), -1.0, AL.add)
+    ts(col(SMK), pair(3), pair(4), AL.add)
+    ts(col(C4), pair(5), pair(6), AL.add)
+    ts(col(WF, 2), C("EE", 17, 20, 2), 1024.0, AL.mult, col(C4), AL.add)
+    tt(col(WF, 2), col(WF, 2), C("EE", 16, 19, 2), AL.add)
+    ts(C("ZM", 144 * 6, 144 * 7), V("IN"), col(G16), AL.is_equal)
+    for buf in ("MS", "ST0"):
+        fill(one(buf, 0, 0), 0.0)
+        fill(one(buf, 1, 0), 2 * MOVE)
+    ts(col(T0), pair(2), pair(4), AL.add, pair(7), AL.add)
+    tt(col(T1, 2), C("EE", 19, 23, 3), C("EE", 18, 22, 3), AL.subtract)
+    for f, w in enumerate((col(WF), col(WB), col(T0), col(T1), pair(5), col(T3))):
+        act(C("ZM", 144 * f, 144 * f + 144), C("ZM", 144 * 6, 144 * 7), scale=w)
+    ts(col(LE8), pm, 8.0, AL.is_le)
+    ts(col(SU), row(1), 0.25, AL.mult)
+    ts(col(SV), row(0), 1.0 / 512, AL.mult)
+    ts(mat(I1), n128, col(PP), AL.is_equal)
+    ts(mat(DH), mat(I1), col(LE8), AL.mult)
+    ts(mat(DHN), mat(I1), col(LE8), AL.mult, -1.0, AL.mult)
+    for buf, a, lo, hi in (("XB", SN1, 2.0 ** 12, 2.0 ** 17), ("XF", SN2, 2.0 ** 20, 2.0 ** 26)):
+        fill(C(buf, a, a + 1), lo)
+        fill(C(buf, a + 1, a + 2), hi)
+    ts(C("PJ", 34, 35), pm, 1, AL.arith_shift_right)
+    ts(col(HF8), col(LT8), 0.5, AL.mult)
+    ts(col(C4), C("PJ", 34, 35), col(G16), AL.add, -15.0, AL.add)
+    ts(col(C5), C("PJ", 34, 35), col(G16), AL.add, -11.0, AL.add)
+    ts(C("P7", 0, 128), n128, col(C4), AL.is_equal, col(HF8), AL.mult)
+    ts(C("GP", 0, 128), n128, col(C5), AL.is_equal, col(LT8), AL.mult)
+    ts(mat(ONES), C("JB", 0, 128), col(GG), AL.is_equal)
+    ts(mat(C40, 40), C("JB", 128, 168), col(GG), AL.is_equal)
+    tt(mat(EO), C("P7", 0, 128), C("GP", 0, 128), AL.add)
+    tt(mat(EN_), C("P7", 0, 128), C("GP", 0, 128), AL.subtract)
+    act(mat(SELU), mat(ONES), scale=col(SU))
+    act(mat(SELV), mat(ONES), scale=col(SV))
     cp(C("UL", MSL, MSL + 64), V("MI"))
     cp(IND(V("KB"), C("UL", MSL, MSL + 64)), C("GB", 2048, 3072))
-    for hf in range(2):
-        hand("SF", range(hf, 16, 2), range(hf, 16, 2), far[hf], "h_fl")
-    arrive("a_fl", [V("LF")], 16)
-    dma("s", V("SX", slice(8, 16)), C("x", 2048, 4096), "sx1", after=V("SF"))
+    for q in range(4):
+        dma("s", V("SX", slice(8 * q, 8 * q + 8)), C("x", 1024 * q, 1024 * q + 1024), "sx%d" % (q // 2))
     dma("s", C("CL", 512, 1024), V("LC1"), "cl1")
-    dma("s", V("SX", slice(0, 8)), C("x", 0, 2048), "sx0")
-    hand("SX", range(8, 16), range(8), far[1], "h_in")
-    hand("SX", range(8), range(8), far[0], "h_in")
-    dma("g", V("SE", 0), V("eps"), "se", True)
-    dma("g", C("EP", 0, 1), V("eps"), "ep", True)
-    oth = [c for c in T.cores if c != core]
-    em = 1 << topo.engines(core, oth[0])[-1]
-    rec("r", lambda ls: g.remote_dma_fused(
-        [RemoteDMATransfer(dst_ids=[dst_id(topo, c) for c in oth], dma_engine_mask=em,
-                           remote_sem=T.sem["a_eps"], src=ap(V("SE", 0)), dsts=[ap(V("LE", rank)) for c in oth])],
-        local_sem=ls), [], [V("SE", 0)], "ta_eps", 1)
-    arrive("a_eps", [V("LE")], len(oth))
-    arrive("a_w1", [V("W1")], 24 * nin(near[0]))
-    arrive("a_w2", [C("W2", 4096, 12288)], 16 * nin(near[0]))
-    arrive("a_xb", [C("XB", 0, 12288)], 6 * nin(near[0]))
+    way = x_routes(T, topo, core)
+    for h in range(2):
+        fused("x%d" % h, [(lay, [topo.engines(core, lay)[e]], "h_x", V("SX", i), V("LX", j)) if who == core else
+                          (who, [topo.engines(core, who)[e]], "h_in", V("SX", i), V("SX", i))
+                          for e, (who, lay, i, j) in enumerate(way[16 * h:16 * h + 16])])
+    arrive("a_w1", [V("W1")], 24 * wide)
+    arrive("a_w2", [C("W2", 0, 4096), C("W2", 8192, 12288)], 16 * wide)
+    arrive("a_xb", [C("XB", 0, 12288)], 12 * wide)
     for gm in range(8):
-        dma("s", V("W1", grp(gm, 0, 8), slice(0, 4096)), V("LF", slice(2 * gm, 2 * gm + 2)), "f1")
+        dma("s", V("W1", grp(gm, 0, 8), slice(4096, 8192)), V("LF", slice(2 * gm, 2 * gm + 2)), "f1")
     for gm in range(8):
-        for sl, o in ((1, 2 * ((gm - 1) % 8)), (2, 2 * ((gm + 1) % 8))):
-            dma("s", V("W1", grp(gm, 0, 8), slice(4096 * sl, 4096 * sl + 4096)), V("LF", slice(o, o + 2)), "f2")
-    ts(C("PI", 2, 3), C("PI", 1, 2), 1, AL.arith_shift_right)
-    ts(C("PI", 3, 4), C("PI", 0, 1), 4, AL.arith_shift_right)
-    tt(C("PC", 2, 3), C("PC", 0, 1), C("PC", 1, 2), AL.subtract)
-    cp(C("PC", 6, 8), C("PI", 2, 4))
-    ts(C("PC", 3, 4), C("PC", 2, 3), 15.0, AL.add)
-    tt(C("PC", 4, 5), C("PC", 2, 3), C("PC", 6, 7), AL.add)
-    ts(C("PC", 5, 6), C("PC", 4, 5), 4.0, AL.add)
-    for f in range(6):
-        ts(C("ZM", 144 * f, 144 * f + 144), V("IN"), C("PC", 3, 4), AL.is_equal, col(11 + f), AL.mult)
-    ts(C("TI", 0, 64), V("MI"), 127, AL.bitwise_and)
-    ts(C("TI", 64, 128), V("MI"), 7, AL.arith_shift_right)
-    ts(V("JT"), V("JT"), C("PC", 2, 3), AL.subtract)
-    for i in range(4):
-        ts(C("HM", 64 * i, 64 * i + 64), C("TI", 64 * (i // 2), 64 * (i // 2) + 64), 4.0, AL.mult, -512.0, AL.add)
+        for sl in (0, 2):
+            dma("s", V("W1", grp(gm, 2 * sl, 2 * sl + 4), slice(4096 * sl, 4096 * sl + 4096)),
+                V("LF", 2 * ((gm + sl - 1) % 8) + sl // 2), "f2")
+
+    def homes():
+        ts(C("TI", 0, 64), V("MI"), 7, AL.arith_shift_right)
+        ts(C("TI", 64, 128), V("MI"), 127, AL.bitwise_and)
+        ts(one("HM", 0, 0), C("TI", 0, 64), 512.0, AL.mult, -192.0, AL.add)
+        ts(one("HM", 0, 1), C("TI", 64, 128), 4.0, AL.mult, -1.5, AL.add)
 
     def late_constants():
-        ts(C("ZM", 144 * 6, 144 * 7), V("IN"), C("PC", 3, 4), AL.is_equal)
-        n128 = C("IN", 0, 128)
-        ts(mat(I1), n128, C("PC", 0, 1), AL.is_equal)
-        ts(mat(I1024), n128, C("PC", 0, 1), AL.is_equal, 1024.0, AL.mult)
-        ts(C("TF", 0, 128), n128, C("PC", 2, 3), AL.is_ge)
-        ts(C("TF", 128, 256), n128, C("PC", 3, 4), AL.is_le)
-        ts(mat(DH), n128, C("PC", 0, 1), AL.is_equal, col(23), AL.mult)
-        tt(mat(ONES), C("TF", 0, 128), C("TF", 128, 256), AL.mult)
-        ts(mat(DHN), mat(DH), -1.0, AL.mult)
-        ts(C("TF", 0, 128), n128, C("PC", 4, 5), AL.is_equal, col(24), AL.mult)
-        ts(C("TF", 128, 256), n128, C("PC", 5, 6), AL.is_equal, col(24), AL.mult)
-        ts(V("UC"), C("IN", 0, 16), 0.25, AL.mult)
-        tt(mat(EO), C("TF", 0, 128), C("TF", 128, 256), AL.add)
-        tt(mat(EN_), C("TF", 0, 128), C("TF", 128, 256), AL.subtract)
-        for i in range(5):
-            ts(C("MM", 128 * C40 + 8 * i, 128 * C40 + 8 * i + 8), C("IN", 0, 8), C("PC", 7, 8), AL.is_equal)
-        ts(C("TI", 0, 64), V("MI"), 1.0, AL.add)
-        ts(C("TI", 64, 128), V("MI"), 128.0, AL.add)
-        ts(C("TI", 128, 192), V("MI"), 4096 - 128, AL.bitwise_and)
-        ts(C("TI", 0, 64), C("TI", 0, 64), 127, AL.bitwise_and)
-        ts(C("TI", 64, 128), C("TI", 64, 128), 4095, AL.bitwise_and)
-        tt(C("TI", 0, 64), C("TI", 0, 64), C("TI", 128, 192), AL.add)
-        cp(C("UL", NB1, NB1 + 128), C("TI", 0, 128))
-        fill(C("XB", SN1, SN1 + 1), 1024.0)
-        fill(C("XB", SN1 + 1, SN1 + 2), -1024.0)
-        fill(C("XF", SN2, SN2 + 1), 1024.0)
-        fill(C("XF", SN2 + 1, SN2 + 2), -1024.0)
+        act(two("HM", 2), two("HM", 0), bias=131072.0)
+        act(two("HM", 3), two("HM", 1), bias=1024.0)
+        for i, (edge, back, on) in enumerate(((506.5, -128.0, 1.0), (128 * 122.5, -4096.0, 128.0))):
+            ts(C("TI", 64 * i, 64 * i + 64), one("HM", 0, 1 - i), edge, AL.is_equal, back, AL.mult)
+            tt(C("TI", 64 * i, 64 * i + 64), C("TI", 64 * i, 64 * i + 64), V("MI"), AL.add)
+            ts(C("UL", NB1 + 64 * i, NB1 + 64 * i + 64), C("TI", 64 * i, 64 * i + 64), on, AL.add)
 
-    CQ = float(512 + 512 * 1024)
-    FB = C("W1", 0, 4096)
+    def blk(buf, o, i, n=1):
+        return C(buf, o + 64 * i, o + 64 * (i + n))
+    TMP, DL, DXY, PR, BASE = 0, 1, 2, 4, 6
+
+    def clip(x, y, off):
+        ts(x, x, off - 1.5, AL.max, off + 509.5, AL.min)
+        ts(y, y, 128 * (off - 1.5), AL.max, 128 * (off + 125.5), AL.min)
 
     def starts(rnd):
-        ts(C("TI", 0, 128), C("P0", 0, 128), CQ, AL.add)
+        t, fy, done, next_door = two("P1", 1), two("TF", TMP), two("P1", 2), two("P1", 3)
         if rnd:
-            ts(C("MS0", 128, 192), C("P0", 128, 192), 8.5, AL.is_ge)
-            ts(C("MS1", 128, 192), C("P0", 128, 192), 8.5, AL.is_ge)
-        ts(C("TI", 128, 256), C("TI", 0, 128), 1023, AL.bitwise_and)
-        ts(C("TI", 256, 384), C("TI", 0, 128), 10, AL.arith_shift_right)
-        tt(C("TI", 128, 384), C("TI", 128, 384), V("HM"), AL.add)
-        w = 192 if rnd else 128
+            for s in (1, 0):
+                ts(one("P1", s, 2), one("P1", 0, 2), 8.5, AL.is_ge)
+            tt(two("TF", DL), two("TF", DL), next_door, AL.subtract)
+            tt(two("P1", 0), two("TF", BASE), done, AL.mult)
+            tt(fy, two("TF", DL), done, AL.mult)
+            tt(two("MS", 0), two("MS", 0), two("P1", 0), AL.add)
+            tt(t, fy, next_door, AL.add)
+        ts(fy, t, 1024 * R1, AL.add, 1024 * R1, AL.subtract)
+        ts(two("P1", 0), fy, 0.125, AL.mult)
+        tt(t, t, fy, AL.subtract)
+        tt(two("MS", 1, 2), two("HM", 0, 2), two("P1", 0, 2), AL.add)
+        clip(two("MS", 2), two("MS", 1), 0)
         for s in (1, 0):
-            ts(C("MS%d" % s, 0, 64), C("TI", 128 + 64 * s, 192 + 64 * s), 0.0, AL.max, 511.0, AL.min)
-            ts(C("MS%d" % s, 64, 128), C("TI", 256 + 64 * s, 320 + 64 * s), 0.0, AL.max, 127.0, AL.min)
-            send(nb[s], st_ap(rnd, s, 0, w), C("MS%d" % s, 0, w), "a_st%d%d" % (rnd, s))
-        for s in (1, 0):
-            arrive("a_st%d%d" % (rnd, s), [st_ap(rnd, s, 0, w)], nin(src_nb[s]))
+            a = 1 - rnd
+            send(nb[s], one("ST%d" % rnd, s, a, 3 - a), one("MS", s, a, 3 - a), "a_st%d%d" % (rnd, s))
+            arrive("a_st%d%d" % (rnd, s), [one("ST%d" % rnd, s, a, 3 - a)], nin(src_nb[s]))
 
-    def st_ap(rnd, s, a, b):
-        o = 128 * s if rnd == 0 else 256 + 192 * s
-        return C("ST", o + a, o + b)
+    def bank(s, i):
+        return one("P1", 0, i) if s else blk("P0", 0, i)
 
-    SO0, INC = (4096, 8192), ((-4096, 8192), (-8192, 4096))
-
-    def tmp(s, i, n=1):
-        o = 384 + 384 * s + 64 * i
-        return C("TI", o, o + 64 * n)
-
-    def cells(s, buf, o, off, so, dn):
-        ts(tmp(s, 0), C(buf, o, o + 64), 2, AL.arith_shift_right)
-        ts(tmp(s, 1), C(buf, o + 64, o + 128), 124, AL.bitwise_and)
-        if so:
-            tt(tmp(s, 0), tmp(s, 0), tmp(s, 4), AL.add)
-        ts(tmp(s, 1), tmp(s, 1), 32.0, AL.mult, float(SO0[s] - off // 4), AL.add)
-        tt(tmp(s, 0), tmp(s, 0), tmp(s, 1), AL.add)
-        if dn:
-            tt(tmp(s, 0), tmp(s, 0), tmp(s, 3), AL.max)
-        cp(C("UL", LS + 64 * s, LS + 64 * s + 64), tmp(s, 0))
+    def cells(part, pb_, buf, off):
+        ts(pb_(1), part(buf, 2), 4 * R1, AL.add, 4 * R1, AL.subtract)
+        ts(part("TF", TMP), part(buf, 1), 512 * R1, AL.add, 512 * R1, AL.subtract)
+        tt(pb_(2), part(buf, 0), pb_(1), AL.add)
+        tt(pb_(2), part("TF", TMP), pb_(2), AL.add)
+        ts(part("LS", 0), pb_(2), 0.25, AL.mult, float(-129 * off // 4), AL.add)
 
     def step(rnd, s, h):
-        Q, em_ = C("P%d" % (1 - s), 0, 64), "EM%d" % s
-        wrap(Q, s, ("O%d" % s, 0))
-        ts(tmp(s, 2), Q, float(2 ** 20), AL.max, CQ, AL.add)
-        ts(tmp(s, 4 + h), Q, float(2 ** 20), AL.is_ge, float(INC[s][h]), AL.mult)
-        ts(tmp(s, 0), tmp(s, 2), 1023, AL.bitwise_and)
-        ts(tmp(s, 1), tmp(s, 2), 10, AL.arith_shift_right, 1023, AL.bitwise_and)
-        if h:
-            ts(tmp(s, 2), tmp(s, 5), -1.0 / INC[s][1], AL.mult, 2.0, AL.add)
-            tt(tmp(s, 4), tmp(s, 4), tmp(s, 5), AL.add)
-        tt(tmp(s, 0, 2), tmp(s, 0, 2), C(em_, 0, 128) if h else st_ap(rnd, s, 0, 128), AL.add)
-        if h:
-            tt(C(em_, 128, 192), C(em_, 128, 192), tmp(s, 2), AL.mult)
-        else:
-            ts(C(em_, 128, 192), tmp(s, 4), -1.0 / INC[s][0], AL.mult, 2.0, AL.add)
+        src, t = "EM" if h else "ST%d" % rnd, one("FI", s, 3)
+        wrap(bank(s, 0), s, "O%d" % s)
+        ts(t, bank(s, 0), BIG / 2, AL.max, CQ, AL.add)
+        ts(one("FI", s, 0), bank(s, 0), BIG / 2, AL.is_ge, (1 - 2 * s) * MOVE, AL.mult)
+        ts(one("FI", s, 2), t, 1023, AL.bitwise_and)
+        ts(one("FI", s, 1), t, 3, AL.arith_shift_right, 1023 * 128, AL.bitwise_and)
+        tt(one("EM", s, 0, 3), one("FI", s, 0, 3), one(src, s, 0, 3), AL.add)
         off = 512 * (h + 1)
-        ts(C(em_, 0, 64), tmp(s, 0), float(off), AL.max, float(off + 511), AL.min)
-        ts(C(em_, 64, 128), tmp(s, 1), float(off), AL.max, float(off + 127), AL.min)
-        cells(s, em_, 0, off, True, rnd and h)
-        if h:
-            send(src_nb[s], C("EN", 192 * s, 192 * s + 192), V(em_), "a_en%d%d" % (rnd, s))
-            sl = C("SL", 64 * s, 64 * s + 64)
-            if rnd:
-                ts(tmp(s, 5), tmp(s, 4), float(SO0[s]), AL.add, 5.0 / 4096, AL.mult)
-                ts(tmp(s, 2), st_ap(1, s, 128, 192), 15.0 + s, AL.mult)
-                tt(sl, tmp(s, 5), tmp(s, 2), AL.max)
-            else:
-                ts(sl, tmp(s, 4), float(SO0[s]), AL.add, 1.0 / 1024, AL.mult)
-            ts(tmp(s, 0, 2), C(em_, 0, 128), 3, AL.bitwise_and)
-            cp(C("UL", UVL + 128 * s, UVL + 128 * s + 128), tmp(s, 0, 2))
+        clip(one("EM", s, 2), one("EM", s, 1), off)
+        cells(lambda b, i: one(b, s, i), lambda i: bank(s, i), "EM", off)
+
+    def ends(rnd, s):
+        send(src_nb[s], one("EN", s, 0, 3), one("EM", s, 0, 3), "a_en%d%d" % (rnd, s))
+        ts(one("SL", s, 0), one("EM", s, 0), (5120.0 if rnd else 4096.0) / MOVE, AL.mult)
+        tt(bank(s, 1), one("EM", s, 2), bank(s, 1), AL.subtract)
+        tt(one("TF", s, TMP), one("EM", s, 1), one("TF", s, TMP), AL.subtract)
+        tt(bank(s, 1), one("TF", s, TMP), bank(s, 1), AL.add)
+        ts(one("UV", s, 0), bank(s, 1), 512 + 1.5 * 129, AL.add)
 
     def look(s, win, on_act=True):
-        i = IND(win, C("UL", LS + 64 * s, LS + 64 * s + 64))
+        i = IND(win, one("LS", s, 0))
         if on_act:
             act(V("O%d" % s), i)
         else:
             cp(V("O%d" % s), i)
 
-    def taps_mm(s, bank, c0, fields):
+    def taps_mm(s, bank, fields):
         for n, i in enumerate(fields):
-            o = C(bank, c0 + 64 * n, c0 + 64 * n + 64)
-            mm(o, mat(I1024), C("SL", 64 * s, 64 * s + 64), True, False)
-            wrap(o, 2 + i, ("O%d" % s, 0), False, True)
+            mm(blk(bank, 0, n), mat(I1), one("SL", s, 0), True, False)
+            wrap(blk(bank, 0, n), 2 + i, "O%d" % s, False, True)
 
     def taps_list(rnd, s, bank, fields):
         a = TL + 256 * s + 64 * fields[0]
         ts(C("UL", a, a + 64 * len(fields)), C(bank, 0, 64 * len(fields)), float((SN2 if rnd else SN1) + s), AL.min)
 
-    def own_lists(rnd):
+    def own_scale(rnd):
         for s in range(2):
-            arrive("a_en%d%d" % (rnd, s), [C("EN", 192 * s, 192 * s + 192)], nin(nb[s]))
-        for i in range(4):
-            o = 192 * (i // 2) + 64 * (i % 2)
-            tt(C("TI", 64 * i, 64 * i + 64), C("EN", o, o + 64), C("HM", 128 * (i % 2), 128 * (i % 2) + 64), AL.subtract)
-        ts(C("TI", 0, 256), C("TI", 0, 256), -1536.0, AL.add)
-        for i in range(4):
-            o = 192 * (i // 2) + 128
-            tt(C("TI", 64 * i, 64 * i + 64), C("TI", 64 * i, 64 * i + 64), C("EN", o, o + 64), AL.mult)
-        new = C("TI", 1152 + 256 * rnd, 1408 + 256 * rnd)
-        ts(new, C("TI", 0, 256), 0.25, AL.mult, 511.625, AL.add)
-        if rnd:
-            tt(C("TI", 0, 256), C("TI", 1152, 1408), new, AL.subtract)
-            for i in range(4):
-                tt(C("TI", 64 * i, 64 * i + 64), C("TI", 64 * i, 64 * i + 64), C("MS0", 128, 192), AL.mult)
-            tt(new, new, C("TI", 0, 256), AL.add)
-        cp(C("UL", OWL, OWL + 256), new)
+            arrive("a_en%d%d" % (rnd, s), [one("EN", s, 0, 3)], nin(nb[s]))
+            act(one("P1", s, 0), one("EN", s, 0), AF.Relu, scale=(s - 0.5) / MOVE, bias=0.75 - s)
+        act(two("P1", 0), two("P1", 0), bias=0.25)
+
+    def own_parts():
+        tt(two("TF", DXY, 2), two("EN", 1, 2), two("HM", 2, 2), AL.subtract)
+        for i in range(2):
+            tt(two("TF", PR + i), two("TF", DXY + i), two("P1", 0), AL.mult)
+            act(two("TF", PR + i), two("TF", PR + i), scale=(1.0 / 128, 1.0)[i], bias=511.625)
+
+    def own_lists():
+        ts(two("OW", 0, 2), two("TF", PR, 2), R1, AL.add, R1, AL.subtract)
 
     def own_look(i):
-        act(C("GB", 1024 * i, 1024 * i + 1024), IND(V("CT"), C("UL", OWL + 64 * i, OWL + 64 * i + 64)), scale=col(17 + i))
+        act(C("GB", 1024 * i, 1024 * i + 1024), IND(V("CT"), one("OW", i // 2, 1 - i % 2)), scale=pair(i))
 
-    def own_mm(rnd, last):
-        for h in range(2):
-            if not last:
-                mm(V("P%d" % (6 + h)), mat(EN_ if rnd else DHN), C("NR", 512 * h, 512 * h + 512), True, False)
-            for i in ((3,) if last else (0, 1, 2)):
-                mm(V("P%d" % (6 + h)), mat(EO if rnd else DH), C("GB", 1024 * i + 512 * h, 1024 * i + 512 * h + 512), False, last)
+    OB = (0, 7)
 
-    def widen(i, on_act=True):
-        a = 1024 * i
-        b = 5120 * (i // 4) + 1024 * (i % 4)
-        (act if on_act else cp)(C("XF", b, b + 1024), C("XB", a, a + 1024))
+    def own_mm(rnd, h):
+        mm(V("P%d" % OB[h]), mat(EN_ if rnd else DHN), C("NR", 512 * h, 512 * h + 512), True, False)
+        for i in range(4):
+            mm(V("P%d" % OB[h]), mat(EO if rnd else DH), C("GB", 1024 * i + 512 * h, 1024 * i + 512 * h + 512), False, i == 3)
+
+    def widen(*js, on_pool=False):
+        for i in js:
+            b = 5120 * (i // 4) + 1024 * (i % 4)
+            o, a = C("XF", b, b + 1024), C("XB", 1024 * i, 1024 * i + 1024)
+            if on_pool:
+                rec("g", lambda o=o, a=a: g.affine_select(ap(o), ap(a), [[0, 1024]], AL.is_ge, 0.0, 0, 0), [o], [a])
+            else:
+                act(o, a)
 
     def hb(n, c, p=ALL):
         return V(n, p, slice(CH[c][1], CH[c][2]))
 
+    def wb(n, c):
+        a = sum(e - b for s, b, e in CH[:c]) % 1024
+        return C(n, a, a + CH[c][2] - CH[c][1])
+
     def pb(bank, c):
         return C("P%d" % bank, 0, CH[c][2] - CH[c][1])
 
-    def pc(bank, c, p=ALL):
-        return V("P%d" % (bank + CH[c][1] // 512), p, slice(CH[c][1] % 512, (CH[c][2] - 1) % 512 + 1))
+    def pc(banks, c, p=ALL):
+        return V("P%d" % banks[CH[c][1] // 512], p, slice(CH[c][1] % 512, (CH[c][2] - 1) % 512 + 1))
 
     def lst(base, c):
         return C("UL", base + CH[c][1] // 16, base + CH[c][2] // 16)
 
+    FC = [c for c in range(NC) if CH[c][0] == 0]
+    ZB = (3, 5)
     for rnd in range(2):
         win = FB if rnd else V("KB")
-        abuf = "KB" if rnd else "W2"
-        mrow = 8 if rnd else 1
-        for half, buf in enumerate((abuf, "GB")):
+        abuf, a0 = ("KB", 0) if rnd else ("W2", 4096)
+        for half, (buf, b0) in enumerate(((abuf, a0), ("GB", 0))):
             cuts = [0, 1024, 2048, 3072, 4096] if half else [0, 256, 768, 1792, 2944, 4096]
             for c in range(len(cuts) - 1):
-                o = C(buf, cuts[c], cuts[c + 1])
+                o = C(buf, b0 + cuts[c], b0 + cuts[c + 1])
                 a, w = 512 * half + 256 + cuts[c] // 16, (cuts[c + 1] - cuts[c]) // 16
-                act(o, IND(win, C("CL", a, a + w)), scale=col(8) if rnd == 0 else 1.0)
+                act(o, IND(win, C("CL", a, a + w)), scale=col(SMK) if rnd == 0 else 1.0)
+                if rnd == 0 and half == 1 and c == 0:
+                    act(V("NR"), IND(FB, C("UL", MSL, MSL + 64)), scale=col(LT8))
+                    for s in range(2):
+                        wrap(one("P1", s, 1), s, "NR")
+                if rnd == 1 and half == 1 and c == 3:
+                    act(V("UU"), IND(win, C("CL", a - 256, a - 256 + w)))
+                else:
+                    tt(o, IND(win, C("CL", a - 256, a - 256 + w)), o, AL.add)
+                if rnd == 0 and half == 0 and c == 0:
+                    homes()
+                if rnd == 0 and half == 0 and c == 2:
+                    act(one("HM", 1, 0, 2), one("HM", 0, 0, 2))
                 if rnd == 0 and half == 1 and c == 1:
-                    act(V("NR"), IND(FB, C("UL", MSL, MSL + 64)), scale=col(21))
-                    wrap(C("P0", 0, 64), 0, ("NR", 0))
-                    wrap(C("P0", 64, 128), 1, ("NR", 0))
-                tt(o, IND(win, C("CL", a - 256, a - 256 + w)), o, AL.add)
-                if rnd == 0 and half == 1 and c == 2:
                     starts(0)
-            if half == 0:
-                rows_to_slots("s", "W1", 9, abuf, mrow, "ma%d" % rnd, mid=False)
-                if rnd == 1:
-                    rows_to_slots("s", "W2", 1, abuf, mrow, "wa2")
+                    dma("g", C("EP", 0, 1), V("eps"), "ep", True)
+                if rnd == 1 and half == 0 and c == 3:
                     starts(1)
+            if half == 0:
+                rows_to_slots("s", "W1", 10, abuf, 8, "ma%d" % rnd, mid=False, c0=a0)
+                if rnd == 1:
+                    rows_to_slots("s", "W2", 8, abuf, 8, "wa2")
+        rows_to_slots("s", "W1", 11, "GB", 8, "mb%d" % rnd, mid=False)
         if rnd:
-            for c in (2, 3, 4):
-                act(pc(4, c), hb("DF", c), scale=0.5)
-            widen(5)
-            widen(6)
-        rows_to_slots("s", "W1", 10, "GB", mrow, "mb%d" % rnd, mid=False)
-        rows_to_slots("a", "W1", 10, "GB", mrow, "mb%d" % rnd, side=False)
-        rows_to_slots("a", "W1", 9, abuf, mrow, "mb%d" % rnd, side=False)
-        if rnd == 0:
-            for gm in range(8):
-                for sl, sh in ((1, -1), (2, 1)):
-                    dma("s", V("W2", grp(gm, 1, 6), slice(4096 * sl, 4096 * sl + 4096)),
-                        V("W2", grp(gm + sh, 1, 6), slice(0, 4096)), "wa")
-                for sl, sh in enumerate((0, -1, 1)):
-                    dma("s", V("W2", grp(gm, 7, 12), slice(4096 * sl, 4096 * sl + 4096)), V("GB", grp(gm + sh, 1, 6)), "wb")
-            act(C("CT", 0, 32), C("IN", 0, 32), scale=col(25), bias=col(10))
-            for i in range(5):
-                act(C("CT", 32 << i, 64 << i), C("CT", 0, 32 << i), bias=col(1 + i))
-            late_constants()
-        else:
-            rows_to_slots("s", "W2", 7, "GB", mrow, "wb2")
-            widen(7)
-            widen(8)
-        for s in (1, 0):
-            o = st_ap(rnd, s, 0, 1)[1][1].start
-            cells(s, "ST", o, 0, False, False)
-            if rnd:
-                tt(tmp(s, 3), st_ap(1, s, 128, 192), V("JT"), AL.mult)
+            rows_to_slots("s", "W1", 12, "UU", 8, "mb1", d0=3072)
+        rows_to_slots("a", "W1", 11, "GB", 8, "mb%d" % rnd, side=False)
+        rows_to_slots("a", "W1", 10, abuf, 8, "mb%d" % rnd, side=False, c0=a0)
         if rnd:
             for h in range(2):
-                tt(C("XF", 4096 + 512 * h, 4608 + 512 * h), hb("ZI1", h), V("P%d" % (4 + h)), AL.add)
-            va = slice(4096, 5120)
-            dma("s", V("XF", slice(16, 128), slice(9216, 10240)), V("XF", slice(0, 112), va), "vs")
+                act(V("P%d" % (4 + h)), hb("DF", 2 * h), scale=0.5)
+            rows_to_slots("s", "W2", 14, "GB", 8, "wb2")
+            rows_to_slots("s", "W2", 15, "UU", 8, "wb2", d0=3072)
+        else:
+            for gm in range(8):
+                for sl in (0, 2):
+                    dma("s", V("W2", grp(gm, 4, 9), slice(4096 * sl, 4096 * sl + 4096)),
+                        V("W2", grp(gm + sl - 1, 4, 9), slice(4096, 8192)), "wa")
+                for sl in range(3):
+                    dma("s", V("W2", grp(gm, 10, 15), slice(4096 * sl, 4096 * sl + 4096)), V("GB", grp(gm + sl - 1, 4, 9)), "wb")
+            late_constants()
+        cells(two, lambda i: two("P1", i), "ST%d" % rnd, 0)
+        if rnd:
+            for h in range(2):
+                tt(C("XF", 9216 + 512 * h, 9728 + 512 * h), hb("ZI1", 2 * h), V("P%d" % (4 + h)), AL.add)
+            va = slice(9216, 10240)
+            dma("s", V("XF", slice(16, 128), slice(4096, 5120)), V("XF", slice(0, 112), va), "vs")
             dma("s", V("XF", slice(0, 112), slice(14336, 15360)), V("XF", slice(16, 128), va), "vs")
-            dma("s", V("XF", slice(0, 16), slice(9216, 10240)), V("XF", slice(112, 128), va), "vs")
+            dma("s", V("XF", slice(0, 16), slice(4096, 5120)), V("XF", slice(112, 128), va), "vs")
             dma("s", V("XF", slice(112, 128), slice(14336, 15360)), V("XF", slice(0, 16), va), "vs")
-            widen(9, False)
         look(1, V("W1"))
         look(0, V("W1"), False)
         a = NB2 if rnd else NB1
-        act(V("NR"), IND(FB, C("UL", a, a + 64)), scale=col(21), bias=col(22))
+        act(V("NR"), IND(FB, C("UL", a, a + 64)), scale=col(LT8), bias=col(F21))
+        if rnd:
+            fill(V("ZI0", slice(32, 64)), 0.5)
         step(rnd, 1, 0)
         look(1, V("W1"))
         step(rnd, 0, 0)
         look(0, V("W1"))
         if rnd:
-            widen(4)
+            fill(V("ZI1", slice(32, 64)), 1.0)
         step(rnd, 1, 1)
         look(1, V("W2"))
-        if rnd:
-            widen(10)
-            widen(11)
+        ends(rnd, 1)
         step(rnd, 0, 1)
-        taps_mm(1, "P0", 0, [0])
-        taps_list(rnd, 1, "P0", [0])
+        taps_mm(1, "P6", [0, 1])
         look(0, V("W2"), False)
-        taps_mm(1, "P6", 0, [1])
-        taps_list(rnd, 1, "P6", [1])
-        taps_mm(1, "P7", 0, [2, 3])
+        taps_list(rnd, 1, "P6", [0, 1])
+        ends(rnd, 0)
+        if rnd == 0:
+            ts(V("EW"), C("IN", 0, 16), 0.0, AL.mult, C("EP", 0, 1), AL.add)
+            deal("a_eps", "SE", "LE", in_plan, stage=V("EW"), own_src=lambda i: V("EW", grp(i, 0, 16)))
         xw = C("XF", 0, SN2 + 2) if rnd else C("XB", 0, SN1 + 2)
 
+        def take(c, i):
+            act(wb(("A0", "A2")[i], c), IND(xw, lst(TL + 256 * CH[c][0] + 128 * i, c)))
+
+        def parts(c):
+            act(wb("UU", c), IND(V("CT"), V("UV", ALL, CH[c][0], slice(CH[c][1] // 16, CH[c][2] // 16))))
+            mm(pb(2 + c % 2, c), mat(SELU), wb("UU", c), True, True)
+            mm(pb(4 + c % 2, c), mat(SELV), wb("UU", c), True, True)
+
         def fetch(c):
-            s = CH[c][0]
-            act(hb("A0", c), IND(xw, lst(TL + 256 * s, c)))
-            if c == 0:
-                diff(0, 0)
-                taps_list(rnd, 1, "P7", [2, 3])
-            act(hb("UU", c), IND(V("UC"), lst(UVL + 128 * s, c)))
-            mm(pb(2 + c % 2, c), mat(I1), hb("UU", c), True, True)
-            act(hb("A2", c), IND(xw, lst(TL + 256 * s + 128, c)))
-            act(hb("VV", c), IND(V("UC"), lst(UVL + 128 * s + 64, c)))
+            take(c, 0)
+            parts(c)
+            take(c, 1)
 
         def diff(c, i):
             s = CH[c][0]
-            tt(hb(("D0", "D2")[i], c), IND(xw, lst(TL + 256 * s + 64 + 128 * i, c)), hb(("A0", "A2")[i], c), AL.subtract)
+            tt(wb(("D0", "D2")[i], c), IND(xw, lst(TL + 256 * s + 64 + 128 * i, c)), wb(("A0", "A2")[i], c), AL.subtract)
 
-        def zout(c):
-            s, a, b = CH[c]
-            return hb("ZI%d" % s, c) if rnd else C("XF", ZF0 + 1024 * s + a, ZF0 + 1024 * s + b)
-
-        fetch(0)
-        taps_mm(0, "P1", 0, [0, 1, 2, 3])
-        fetch(1)
+        taps_mm(1, "P7", [2, 3])
+        if rnd == 0:
+            widen(0, 1, 2, on_pool=True)
+        take(0, 0)
+        parts(0)
+        diff(0, 0)
+        taps_list(rnd, 1, "P7", [2, 3])
+        take(0, 1)
+        own_scale(rnd)
+        taps_mm(0, "P0", [0, 1])
+        taps_mm(0, "P7", [2, 3])
+        tt(pb(6, 0), wb("D0", 0), pb(2, 0), AL.mult)
         diff(0, 1)
-        for c in range(5):
+        for c in range(NC):
             s = CH[c][0]
-            U, M1, M2 = pb(2 + c % 2, c), pb(4, c), pb(5, c)
-            tt(M1, hb("D0", c), U, AL.mult)
-            tt(M2, hb("D2", c), U, AL.mult)
-            tt(hb("SS", c), hb("A0", c), M1, AL.add)
-            tt(M2, hb("A2", c), M2, AL.add)
+            late = c >= EARLY if rnd == 0 else not carry[c]
+            U, W, M, Z = pb(2 + c % 2, c), pb(4 + c % 2, c), pb(6, c), hb("ZO%d" % s, c)
+            tt(U, wb("D2", c), U, AL.mult)
+            sb = ("SS", "GP")[s]
+            tt(hb(sb, c), wb("A0", c), M, AL.add)
             if c == 0:
-                taps_list(rnd, 0, "P1", [0, 1, 2, 3])
-                own_lists(rnd)
-                own_look(0)
-            tt(M2, M2, hb("SS", c), AL.subtract)
-            if c < 4:
+                taps_list(rnd, 0, "P0", [0, 1])
+                take(1, 0)
+                parts(1)
+            tt(U, wb("A2", c), U, AL.add)
+            if c == 0:
+                own_parts()
+            if c < NC - 1:
                 diff(c + 1, 0)
-            tt(M2, M2, hb("VV", c), AL.mult)
-            if c < 4:
-                diff(c + 1, 1)
-            tt(zout(c), hb("SS", c), M2, AL.add)
-            if rnd == 0:
-                send(src_nb[s], hb("ZI%d" % s, c), zout(c), "a_z%d" % c)
-                arrive("a_z%d" % c, [hb("ZI%d" % s, c)], nin(nb[s]))
-                for gm in range(4 * c, 4 * c + 4) if c < 2 else ():
-                    r = (gm - 2 * k + 2) % 8
-                    s_ = V("eps", grp(r + k, 0, 16)) if r == rank else V("LE", r, grp(r + k, 0, 16))
-                    dma("g", V("ED", grp(gm, 0, 16), slice(0, 1)), s_, "ed", True)
-            elif carry[c] != core:
-                send(carry[c], zout(c), zout(c), "h_f%d" % c)
-                arrive("a_f%d" % c, [V("LZ%d" % c)], 8)
-            else:
-                deal("a_f%d" % c, "SZ%d" % c, "LZ%d" % c, final_plan(T, k, s), stage=zout(c),
-                     own_src=lambda i: hb("ZI%d" % s, c, grp(i, 0, 16)))
-            if c < 3:
-                fetch(c + 2)
+            tt(wb("D2", c), U, hb(sb, c), AL.subtract)
             if c == 0:
-                own_look(1)
-                own_look(2)
-                own_mm(rnd, False)
+                taps_list(rnd, 0, "P7", [2, 3])
+                take(1, 1)
+                own_lists()
+                tt(Z, wb("D2", c), W, AL.mult)
+            if c < NC - 1:
+                diff(c + 1, 1)
+            if late:
+                tt(W, wb("D2", c), W, AL.mult)
+            if c < NC - 1:
+                tt(pb(6, c + 1), wb("D0", c + 1), pb(3 - c % 2, c + 1), AL.mult)
+            if late:
+                tt(Z, hb(sb, c), W, AL.add)
+            elif c:
+                tt(Z, wb("D2", c), W, AL.mult)
+            if rnd == 0 and c < EARLY:
+                m = (CH[c][1] + CH[c][2]) // 2
+                for i, o in enumerate(relays(T, topo, core, src_nb[s], c)):
+                    a, b = ((CH[c][1], m), (m, CH[c][2]))[i]
+                    folds.append(([o], topo.engines(core, o)[i::2], [C(sb, a, b), C("ZO%d" % s, a, b)], C("ZO%d" % s, a, b)))
+                fold("h_r%d" % c)
+                arrive("a_z%d" % c, [hb("ZI%d" % s, c)], 2 * nin(nb[s]))
+            elif rnd == 0:
+                send(src_nb[s], hb("ZI%d" % s, c), Z, "a_z%d" % c)
+                arrive("a_z%d" % c, [hb("ZI%d" % s, c)], nin(nb[s]))
+            elif not late:
+                folds.append((carry[c], topo.engines(core, carry[c][0]), [hb(sb, c), Z], Z))
+                fold("h_f%d" % c)
+                arrive("a_f%d" % c, [V("LZ%d" % c)], 16)
+            else:
+                deal("a_f%d" % c, "SZ%d" % c, "LZ%d" % c, final_plan(T, k, s), stage=Z,
+                     own_src=lambda i: hb("ZO%d" % s, c, grp(i, 0, 16)))
+            if c < NC - 2:
+                fetch(c + 2)
+            for i in (((0,), (1,), (2, 3), (), ()), ((0, 1), (2, 3), (), (), ()))[rnd][c]:
+                own_look(i)
+            if c == 2 - rnd:
+                own_mm(rnd, 0)
+                own_mm(rnd, 1)
             if c == 1:
-                own_look(3)
-            if c == 2:
-                own_mm(rnd, True)
                 if rnd == 0:
-                    act(V("P0"), hb("ZI1", 0))
-                    act(V("P1"), hb("ZI1", 1))
-                else:
-                    dma("s", hb("GP", 0), V("LZ0"), "gb0")
-                    act(C("DF", 0, 512), V("P6"))
-                    act(C("DF", 512, 1024), V("P7"))
-                    for i in range(8):
-                        dma("a", V("SH", ALL, slice(16 * i, 16 * i + 16)), V("DF", slice(i, 128, 16)), "sh")
+                    dma("s", V("ED"), V("LE"), "ed")
+                    act(two("TF", TMP), two("TF", DXY), scale=8.0)
+            if c == 2 and rnd:
+                dma("a", hb("GP", 0), V("LZ0"), "gb0")
+                for h in range(2):
+                    act(C("DF", 512 * h, 512 * h + 512), V("P%d" % OB[h]))
+                for i in range(8):
+                    dma("a", V("SH", ALL, slice(16 * i, 16 * i + 16)), V("DF", slice(i, 128, 16)), "sh")
             if c == 3 and rnd:
-                hand("SH", range(8), range(8), carry[5], "h_f5")
-                arrive("a_mh", [V("LH")], 8)
-        if rnd == 1:
-            dma("s", hb("GP", 1), V("LZ1"), "gb1")
+                es = topo.engines(core, carry[NC][0])
+                fused("sh", [(carry[NC][0 if topo.may_write(carry[NC][0], o) else 1], es[i::8], "h_f%d" % NC, V("SH", i), V("SH", i))
+                             for o, i, j in final_plan(T, k, 2)])
+                arrive("a_mh", [V("LH")], 16)
+            if rnd == 0 and c == 0:
+                widen(3, 11, on_pool=True)
+            if c == NC - 2:
+                if rnd == 0:
+                    act(V("P%d" % ZB[0]), hb("ZI1", 0))
+                else:
+                    dma("a", hb("A0", FC[0]), V("LZ%d" % FC[0]), "zf0")
+                    act(V("P%d" % OB[0]), hb("GP", 0))
         if rnd == 0:
             def gap(c):
-                tt(hb("DF", c), hb("ZI0", c), pc(0, c), AL.subtract)
+                tt(hb("DF", c), hb("ZI0", c), pc(ZB, c), AL.subtract)
                 act(hb("GP", c), hb("DF", c), AF.Abs)
 
             def vote(c):
                 ts(hb("O0", c), hb("GP", c), C("ED", 0, 1), AL.is_le)
-                mm(pb(2 + c % 2, c), mat(ONES), hb("O0", c), True, True)
+                mm(pb(4 if c == 3 else 2, c), mat(ONES), hb("O0", c), True, True)
 
-            def pick(c):
-                ts(hb("VV", c), pb(2 + c % 2, c), 8.5, AL.is_ge)
-                tt(hb("O1", c), hb("VV", c), pc(6, c), AL.mult)
+            def flag(c):
+                act(hb("VV", c), pb(4 if c == 3 else 2, c), AF.Relu, bias=-8.0)
+                act(hb("VV", c), hb("VV", c), AF.Sign)
 
             def put(c):
+                tt(hb("O1", c), hb("VV", c), pc(OB, c), AL.mult)
                 tt(IND(FB, lst(MSL, c)), hb("NR", c), hb("O1", c), AL.add)
-            widen(0)
-            widen(1)
-            gap(2)
-            vote(2)
+            widen(7, 8, 9, 10, on_pool=True)
+            gap(1)
+            act(V("P%d" % ZB[1]), hb("ZI1", 2))
+            tt(two("TF", DL), two("TF", DXY + 1), two("TF", TMP), AL.add)
+            tt(two("TF", BASE), two("EN", 0), two("MS", 0), AL.subtract)
+            vote(1)
             gap(3)
-            pick(2)
-            widen(2)
+            ts(hb("VV", 1), pb(2, 1), 8.5, AL.is_ge)
             vote(3)
-            put(2)
+            flag(3)
+            widen(4)
+            put(1)
             gap(4)
-            pick(3)
+            widen(5, 6)
             vote(4)
             put(3)
-            pick(4)
+            ts(hb("VV", 4), pb(2, 4), 8.5, AL.is_ge)
             put(4)
-            widen(3)
-            for gm in range(8):
-                dma("s", V("W1", grp(gm, 0, 8), slice(4096, 8192)), V("W1", grp(gm - 1, 0, 8), slice(0, 4096)), "f3")
-                dma("s", V("W1", grp(gm, 0, 8), slice(8192, 12288)), V("W1", grp(gm + 1, 0, 8), slice(0, 4096)), "f3")
-            wrap(C("P0", 128, 192), 6, ("O0", 0))
+            wrap(one("P1", 0, 2), 6, "O0")
             for s in range(2):
-                wrap(C("P0", 64 * s, 64 * s + 64), s, ("NR", 0), True, False)
-                wrap(C("P0", 64 * s, 64 * s + 64), s, ("O1", 0), False, True)
+                wrap(one("P1", s, 3), s, "NR")
+            for gm in range(8):
+                for sl in (0, 2):
+                    dma("s", V("W1", grp(gm, 2 * sl, 2 * sl + 4), slice(4096 * sl, 4096 * sl + 4096)),
+                        V("W1", grp(gm + sl - 1, 2 * sl, 2 * sl + 4), slice(4096, 8192)), "f3")
 
     p40 = slice(0, 40)
-    fill(V("D0", slice(32, 64)), 0.5)
-    fill(V("D2", slice(32, 64)), 0.5)
-    for c in (2, 3, 4):
+    dma("s", hb("GP", 2), V("LZ2"), "gb1")
+    for c in FC[1:]:
         dma("s", hb("A0", c), V("LZ%d" % c), "zf%d" % c)
-    for h in range(2):
-        act(V("P%d" % (6 + h)), hb("GP", h))
-    for c in (2, 3, 4):
-        cnt, hh = pb(2 + c % 2, c), pb(4 + c % 2, c)
-        tt(hb("A2", c), hb("A0", c), pc(6, c), AL.subtract)
+    for i in range(8):
+        dma("s", V(("ZI0", "ZI1")[i // 4], slice(8 * (i % 4), 8 * (i % 4) + 8)), V("LH", ALL, slice(16 * i, 16 * i + 16)), "mh")
+
+    def gaps(c):
+        tt(hb("A2", c), hb("A0", c), pc(OB, c), AL.subtract)
         act(hb("SS", c), hb("A2", c), AF.Abs)
-        act(hh, hb("A2", c), scale=0.5)
-        ts(hb("O0", c), hb("SS", c), C("EP", 0, 1), AL.is_le)
-        mm(cnt, mat(ONES), hb("O0", c), True, True)
-        mm(pc(0, c, p40), mat(C40, 40), hb("O0", c), True, True)
-        tt(hh, hb("GP", c), hh, AL.add)
+        act(pb(4 + c % 2, c), hb("A2", c), scale=0.5)
         act(hb("DF", c), hb("SS", c), AF.Exp, scale=-1.0)
         dma("a", hb("ye", c), hb("DF", c), "oe%d" % c)
-        ts(hb("O1", c), cnt, 8.5, AL.is_ge)
-        act(pc(0, c, p40), pc(0, c, p40), AF.Sign, bias=-8.5)
-        tt(hb("ZI1", c), hh, hb("O1", c), AL.mult)
-        dma("s", hb("y", c), hb("ZI1", c), "oy%d" % c)
-        if c == 2:
-            for i in range(8):
-                dma("s", V(("D0", "D2")[i // 4], slice(8 * (i % 4), 8 * (i % 4) + 8)),
-                    V("LH", ALL, slice(16 * i, 16 * i + 16)), "mh")
-        for b in ((), (2, 3), (4,))[c - 2]:
-            tt(pc(0, b, p40), pc(0, b, p40), hb("D2", b, p40), AL.mult)
-            tt(hb("D0", b, p40), hb("D0", b, p40), pc(0, b, p40), AL.add)
-            dma("s", hb("yf", b), hb("D0", b, p40), "of%d" % b)
+        if c == FC[0]:
+            act(V("P%d" % OB[1]), hb("GP", 2))
+
+    def sign(c):
+        return one("P1", c - FC[1], 0, 4, p40) if c > FC[0] else V("P6", p40)
+
+    def votes(c):
+        ts(hb("O0", c), hb("SS", c), C("EP", 0, 1), AL.is_le)
+        mm(pb(2 + c % 2, c), mat(ONES), hb("O0", c), True, True)
+        mm(sign(c), mat(C40, 40), hb("O0", c), True, True)
+        tt(pb(4 + c % 2, c), hb("GP", c), pb(4 + c % 2, c), AL.add)
+        ts(hb("D2", c), pb(2 + c % 2, c), 8.5, AL.is_ge, 8.0, AL.mult)
+
+    def stores(c):
+        tt(hb("D0", c), pb(4 + c % 2, c), hb("D2", c), AL.min)
+        dma("a", hb("y", c), hb("D0", c), "oy%d" % c)
+        ts(sign(c), sign(c), 8.5, AL.is_ge, 0.5, AL.subtract)
+
+    def flows(c):
+        tt(sign(c), hb("ZI1", c, p40), sign(c), AL.mult)
+        tt(hb("ZI0", c, p40), hb("ZI0", c, p40), sign(c), AL.add)
+        dma("s", hb("yf", c), hb("ZI0", c, p40), "of%d" % c)
+
+    gaps(FC[0])
+    votes(FC[0])
+    stores(FC[0])
+    gaps(FC[1])
+    votes(FC[1])
+    gaps(FC[2])
+    stores(FC[1])
+    flows(FC[0])
+    votes(FC[2])
+    flows(FC[1])
+    stores(FC[2])
+    flows(FC[2])
 
     def meets(a, b):
         return a[0] == b[0] and a[2] < b[3] and b[2] < a[3] and not a[1].isdisjoint(b[1])
 
-    total, semof, free = {}, {}, ["d%d" % i for i in range(100)]
+    def earlier(calls):
+        seen, out = {}, []
+        for i, o in enumerate(calls):
+            dep = set()
+            for kind in ("rd", "wr"):
+                for r in o[kind]:
+                    for j, wj, rj in seen.get(r[0], []):
+                        pj = calls[j]
+                        clash = (r[4] and pj["q"] != o["q"]) or ((wj or kind == "wr") and meets(r, rj))
+                        if clash and not (o["q"] == "p" and pj["q"] == "p") and not (pj["grp"] and pj["grp"] == o["grp"]):
+                            dep.add(j)
+            out.append(dep)
+            for kind in ("rd", "wr"):
+                for r in o[kind]:
+                    seen.setdefault(r[0], []).append((i, kind == "wr", r))
+        return out
+
+    deps, order, done, had, prev = earlier(ops), [], set(), {}, None
+
+    def free_now(j):
+        return all(d in done and d != prev and (ops[d]["q"] == "v" or d <= had.get(ops[d]["grp"] or ops[d]["q"], -1)) for d in deps[j])
+
+    for i, o in enumerate(ops):
+        if i in done:
+            continue
+        if o["q"] == "v" and prev in deps[i]:
+            for j in [j for j in range(i + 1, min(i + AHEAD, len(ops))) if ops[j]["q"] == "v" and j not in done
+                      and ops[j]["wr"][0][3] - ops[j]["wr"][0][2] <= 512 and free_now(j)][:1]:
+                order.append(j)
+                done.add(j)
+        order.append(i)
+        done.add(i)
+        if o["q"] == "v":
+            prev = i
+            for d in deps[i]:
+                key = ops[d]["grp"] or ops[d]["q"]
+                had[key] = max(had.get(key, -1), d)
+    ops = [ops[i] for i in order]
+
+    total, semof, free = {}, {}, ["d%d" % i for i in range(95)]
     for o in ops:
         if o["grp"]:
             total[o["grp"]] = total.get(o["grp"], 0) + o["n"]
             if o["grp"] not in semof:
                 semof[o["grp"]] = o["grp"] if o["q"] is None else free.pop(0)
-    seen, need = {}, set()
-    for i, o in enumerate(ops):
-        dep = set()
-        for kind in ("rd", "wr"):
-            for r in o[kind]:
-                for j, wj, rj in seen.get(r[0], []):
-                    pj = ops[j]
-                    clash = wj or kind == "wr" or (r[4] and pj["q"] != o["q"])
-                    if clash and meets(r, rj) and not (o["q"] == "p" and pj["q"] == "p"):
-                        if not (pj["grp"] and pj["grp"] == o["grp"]):
-                            dep.add(j)
+    need = set()
+    for o, dep in zip(ops, earlier(ops)):
         last = {}
         for j in dep:
             if not ops[j]["grp"]:
@@ -859,9 +1021,6 @@ def rank_program(g, core, T, topo):
         o["dep"] = (sorted(set(ops[j]["grp"] for j in dep if ops[j]["grp"])), last)
         if o["q"] is not None:
             need.update(last.values())
-        for kind in ("rd", "wr"):
-            for r in o[kind]:
-                seen.setdefault(r[0], []).append((i, kind == "wr", r))
     eng = {"v": g.vector, "a": g.scalar, "p": g.tensor, "s": g.sync, "g": g, "r": g}
     cnt, idx, waited = {"v": 0, "a": 0, "p": 0, "g": 0}, {}, {}
     for i, o in enumerate(ops):

from concourse.bass import DstId, RemoteDMATransfer
from concourse.mybir import AluOpType as AL, ActivationFunctionType as AF

F32, BF, I32, U16 = "float32", "bfloat16", "int32", "uint16"
SN2, SN1 = 15360, 12288
EARLY = 2
CH = [(1, 0, 512), (0, 0, 512), (1, 512, 1024), (0, 512, 768), (0, 768, 1024)]
NC = len(CH)
AHEAD = 40
SCRATCH = {
    "W1": ("sbuf", [128, 12288], BF), "W2": ("sbuf", [128, 12288], BF), "KB": ("sbuf", [128, 4096], BF),
    "GB": ("sbuf", [128, 4096], BF), "XB": ("sbuf", [128, 12304], BF), "XF": ("sbuf", [128, 15368], F32),
    "CL": ("sbuf", [128, 1024], U16),
    "A0": ("sbuf", [128, 1024], F32), "A2": ("sbuf", [128, 1024], F32), "D0": ("sbuf", [128, 1024], F32),
    "D2": ("sbuf", [128, 1024], F32), "SS": ("sbuf", [128, 1024], F32), "ZI0": ("sbuf", [128, 1024], F32),
    "ZI1": ("sbuf", [128, 1024], F32), "DF": ("sbuf", [128, 1024], F32), "GP": ("sbuf", [128, 1024], F32),
    "ZO0": ("sbuf", [128, 1024], F32), "ZO1": ("sbuf", [128, 1024], F32),
    "UU": ("sbuf", [128, 1024], BF), "VV": ("sbuf", [128, 1024], BF), "O0": ("sbuf", [128, 1024], BF),
    "O1": ("sbuf", [128, 1024], BF), "NR": ("sbuf", [128, 1024], BF),
    "CT": ("sbuf", [128, 1024], BF), "ZM": ("sbuf", [128, 7 * 144], BF), "MM": ("sbuf", [128, 9 * 128], BF),
    "SL": ("sbuf", [128, 2, 64], BF),
    "IN": ("sbuf", [128, 144], F32), "JB": ("sbuf", [128, 168], F32), "PC": ("sbuf", [128, 24], F32),
    "EE": ("sbuf", [128, 24], F32), "BC": ("sbuf", [128, 68], F32),
    "PJ": ("sbuf", [128, 40], I32), "EP": ("sbuf", [128, 4], F32), "EW": ("sbuf", [128, 16], F32), "ED": ("sbuf", [128, 16], F32),
    "MI": ("sbuf", [128, 64], I32), "HM": ("sbuf", [128, 2, 256], F32),
    "TI": ("sbuf", [128, 2048], I32), "TF": ("sbuf", [128, 2, 448], F32), "FI": ("sbuf", [128, 2, 256], I32),
    "UL": ("sbuf", [128, 704], U16), "LS": ("sbuf", [128, 2, 64], U16), "UV": ("sbuf", [128, 2, 64], U16),
    "OW": ("sbuf", [128, 2, 128], U16),
    "MS": ("sbuf", [128, 2, 192], F32), "EM": ("sbuf", [128, 2, 192], F32), "EN": ("sbuf", [128, 2, 192], F32),
    "ST0": ("sbuf", [128, 2, 192], F32), "ST1": ("sbuf", [128, 2, 192], F32),
    "SE": ("dram", [8, 128, 2], F32), "LE": ("dram", [8, 128, 2], F32),
    "SM": ("dram", [8, 128, 8], I32), "LM": ("dram", [8, 128, 8], I32),
    "SC0": ("dram", [8, 128, 64], U16), "LC0": ("dram", [8, 128, 64], U16),
    "SC1": ("dram", [8, 128, 64], U16), "LC1": ("dram", [8, 128, 64], U16),
    "SF": ("dram", [16, 128, 128], BF), "LF": ("dram", [16, 128, 128], BF),
    "SX": ("dram", [32, 128, 128], BF), "LX": ("dram", [8, 128, 128], BF),
    "SH": ("dram", [8, 128, 64], F32), "LH": ("dram", [8, 128, 64], F32),
}
for _c, (_s, _a, _b) in enumerate(CH):
    SCRATCH["SZ%d" % _c] = ("dram", [8, 128, (_b - _a) // 8], F32)
    SCRATCH["LZ%d" % _c] = ("dram", [8, 128, (_b - _a) // 8], F32)
for _c in range(8):
    SCRATCH["P%d" % _c] = ("psum", [128, 2, 256] if _c == 1 else [128, 512], F32)
ARR = (["a_ms", "a_c0", "a_c1", "a_w1", "a_w2", "a_xb", "h_in", "h_z", "h_x", "h_c1", "h_fl", "a_fl", "a_eps", "a_mh"]
       + ["h_r%d" % i for i in range(NC - 1)]
       + ["a_%s%d%d" % (n, r, s) for n in ("st", "en") for r in range(2) for s in range(2)]
       + ["a_z%d" % i for i in range(NC)] + ["a_f%d" % i for i in range(NC)] + ["h_f%d" % i for i in range(NC + 1)])
SEMAPHORES = ARR + ["e_v", "e_a", "e_p", "e_g"] + ["d%d" % i for i in range(95)]
IO = {"x": [128, 4096], "eps": [128, 1], "fl": [32, 4096], "cor": [128, 1024], "ms": [128, 64],
      "y": [128, 1024], "ye": [128, 1024], "yf": [40, 1024]}
ALL = slice(None)


def diag_ring(T, topo):
    n = len(T.cores)
    ch = [topo.chip(c) for c in T.cores]
    best = [-1, list(range(n))]

    def go(path, score):
        if len(path) == n:
            a, b = ch[path[-1]], ch[path[0]]
            if topo.mates(a, b) or topo.same_plane(a, b):
                s = score + (1 if topo.mates(a, b) else 0)
                if s > best[0]:
                    best[0], best[1] = s, list(path)
            return
        for r in range(n):
            if r not in path:
                a, b = ch[path[-1]], ch[r]
                if topo.mates(a, b) or topo.same_plane(a, b):
                    go(path + [r], score + (1 if topo.mates(a, b) else 0))
    go([0], 0)
    return best[1]


def V(name, p=ALL, c=None, e=None):
    return (name, (p,) if c is None else ((p, c) if e is None else (p, c, e)))


def C(name, a, b, step=1):
    return (name, (ALL, slice(a, b, step) if step != 1 else slice(a, b)))


def one(name, s, i, n=1, p=ALL):
    return (name, (p, s, slice(64 * i, 64 * (i + n))))


def two(name, i, n=1):
    return (name, (ALL, ALL, slice(64 * i, 64 * (i + n))))


def IND(win, off):
    return ("*", win, off)


def region(v):
    name, idx = v
    shp = IO[name] if name in IO else SCRATCH[name][1]
    p = idx[0]
    ps = frozenset(range(*p.indices(shp[0]))) if isinstance(p, slice) else frozenset([p])
    bank = name not in IO and SCRATCH[name][0] == "psum"
    if len(idx) == 3 and SCRATCH[name][0] != "dram":
        a, b, _ = idx[2].indices(shp[2])
        if idx[1] != ALL:
            ps = frozenset((q, idx[1]) for q in ps)
        else:
            ps = frozenset((q, s) for q in ps for s in range(2))
        return (name, ps, a, b, bank)
    if len(idx) > 1:
        r = range(*idx[1].indices(shp[1]))
        return (name, ps, r[0], r[-1] + 1, bank)
    return (name, ps, 0, shp[1], bank)


def dst_id(topo, c):
    return DstId(rid=topo.addr(c)[0], pnc=topo.addr(c)[1])


def helpers(T, topo, c):
    mine = [o for o in topo.cores_of(c) if o != c]
    out = []
    for same in (False, True):
        die = [o for o in mine if (topo.die(o) == topo.die(c)) == same]
        wide = [o for o in die if all(topo.may_write(o, t) for t in T.cores)]
        out.append((wide, [o for o in die if o not in wide]))
    return out


def carriers(T, topo, c):
    far, near = helpers(T, topo, c)
    two = [(far[1][0], far[0][0]), (far[1][1], far[0][1]), (near[1][0], near[0][0])]
    return [two[0], (), (), (), (), two[1]]


def relays(T, topo, c, dst, i):
    out = []
    for wide, narrow in helpers(T, topo, c):
        can = narrow if topo.may_write(narrow[0], dst) else wide
        out.append(can[i % len(can)])
    return out


def routes(T, topo, boss, dies):
    out = []
    for h, d in enumerate(dies):
        wide, narrow = helpers(T, topo, boss)[d]
        for c, v, gm in input_plan(T, diag_ring(T, topo), T.rank_of(boss)):
            can = narrow if topo.may_write(narrow[0], c) else wide
            load = [len([r for r in out if r[0] == o]) for o in can]
            out.append((boss if c == boss else can[load.index(min(load))], c, len(dies) * v + h, len(dies) * gm + h))
    return out


RELAYED = (("c1", "SC1", "LC1", (0,)), ("fl", "SF", "LF", (0, 1)))


def input_plan(T, ring, rank):
    return [(T.cores[ring[(v - rank) % 8]], v, (rank + 2 * ((v - rank) % 8) - 2) % 8) for v in range(8)]


def final_plan(T, k, s):
    rs = [(gm - 2 * k + (0, 4, 2)[s]) % 8 for gm in range(8)]
    return [(T.cores[r], gm, (r + k + (1, -1, 0)[s]) % 8) for gm, r in enumerate(rs)]


def x_routes(T, topo, boss):
    out = []
    for q in range(4):
        wide, narrow = helpers(T, topo, boss)[q // 2]
        for c, v, gm in input_plan(T, diag_ring(T, topo), T.rank_of(boss)):
            lay = helpers(T, topo, c)[q // 2][1][q % 2]
            who = boss if c == boss else (narrow[q % 2] if topo.may_write(narrow[q % 2], lay) else wide[q % len(wide)])
            out.append((who, lay, 8 * q + v, gm))
    return out


def x_width(routes, who, boss):
    n = len([r for r in routes if r[0] == who])
    return 1 if who == boss or n > 4 else (2 if n > 2 else 4)


def helper_program(g, core, T, topo):
    boss = [c for c in T.cores if topo.chip(c) == topo.chip(core)]
    if not boss:
        return
    boss = boss[0]
    far, near = helpers(T, topo, boss)
    near = near[1] + near[0]
    S = T.sem
    rank, ring = T.rank_of(boss), diag_ring(T, topo)
    m, n = topo.mask(core, boss), len(topo.engines(core, boss))
    rid, pid, _ = topo.addr(boss)
    sent = [0]

    def deal(plan, src, dst, sem, w=1):
        g.remote_dma_fused([RemoteDMATransfer(dst_ids=[dst_id(topo, c)], remote_sem=S[sem], src=T[src][i], dst=T[dst][j],
                                              dma_engine_mask=sum(1 << x for x in topo.engines(core, c)[w * e:w * e + w]))
                            for e, (c, i, j) in enumerate(plan)], local_sem=S["d0"])
        sent[0] += w * len(plan)

    def zeros(buf, js, sem):
        g.remote_dma_fused([RemoteDMATransfer(dst_ids=[dst_id(topo, boss)] * len(js), dma_engine_mask=m, remote_sem=S[sem],
                                              src=T["O0"][:, 0:512], dsts=[T[buf][:, 512 * j:512 * j + 512] for j in js])],
                           local_sem=S["d0"])
        sent[0] += n

    if core in near:
        i = near.index(core)
        g.wait_ge(S["h_z"], n)
        zeros("W1", range(8 * i, 8 * i + 8), "a_w1")
    for name, src, dst, dies in RELAYED:
        way = routes(T, topo, boss, dies)
        mine = [(c, i, j) for who, c, i, j in way if who == core]
        if mine:
            g.wait_ge(S["h_" + name], len(mine))
            deal(mine, src, dst, "a_" + name, x_width(way, core, boss))
    if core in near:
        zeros("W2", (list(range(8)) + list(range(16, 24)))[near.index(core)::3], "a_w2")
    way = x_routes(T, topo, boss)
    mine = [(lay, i, j) for who, lay, i, j in way if who == core]
    if mine:
        g.wait_ge(S["h_in"], len(mine))
        deal(mine, "SX", "LX", "h_x", x_width(way, core, boss))
    comes = [(i // 8, x_width(x_routes(T, topo, c), who, c)) for c in T.cores
             for who, lay, i, j in x_routes(T, topo, c) if lay == core]
    if comes:
        a = 1024 * comes[0][0]
        XB, LX = T["XB"], T["LX"]
        g.sync.wait_ge(S["h_x"], sum(w for q, w in comes))
        g.scalar.wait_ge(S["h_x"], sum(w for q, w in comes))
        g.sync.dma_start(XB[16:128, a:a + 1024], LX[0:7]).then_inc(S["d1"], 16)
        g.scalar.dma_start(XB[0:16, a:a + 1024], LX[7]).then_inc(S["d1"], 16)
        g.sync.dma_start(XB[0:112, 8192 + a:9216 + a], LX[1:8]).then_inc(S["d3"], 16)
        g.scalar.dma_start(XB[112:128, 8192 + a:9216 + a], LX[0]).then_inc(S["d3"], 16)
        g.sync.dma_start(XB[:, 4096 + a:5120 + a], LX[:]).then_inc(S["d2"], 16)
        for sl, cnt in ((0, 32), (2, 32), (1, 16)):
            g.wait_ge(S["d%d" % (sl + 1)], cnt)
            blk = XB[:, 4096 * sl + a:4096 * sl + a + 1024]
            g.remote_dma(blk, blk, S["a_xb"], S["d0"], pid, rid, m)
            sent[0] += n
    k = ring.index(rank)
    for c in range(EARLY):
        s, a, b = CH[c]
        dst = T.cores[ring[(k + 1 - 2 * s) % 8]]
        who = relays(T, topo, boss, dst, c)
        if core in who:
            a, b = ((a, (a + b) // 2), ((a + b) // 2, b))[who.index(core)]
            g.wait_ge(S["h_r%d" % c], n // 2)
            g.remote_dma(T["ZI%d" % s][:, a:b], T["ZO%d" % s][:, a:b], S["a_z%d" % c], S["d0"], topo.addr(dst)[1], topo.addr(dst)[0],
                         topo.mask(core, dst))
            sent[0] += len(topo.engines(core, dst))
    carry = carriers(T, topo, boss)
    for c in [0, 1, 2, NC] + list(range(3, NC)):
        if core not in carry[c]:
            continue
        s = CH[c][0] if c < NC else 2
        plan = [p for p in final_plan(T, k, s) if topo.may_write(carry[c][0], p[0]) == (core == carry[c][0])]
        if c == NC:
            g.wait_ge(S["h_f%d" % c], 2 * len(plan))
            deal(plan, "SH", "LH", "a_mh", 2)
            continue
        s, a, b = CH[c]
        g.sync.wait_ge(S["h_f%d" % c], n)
        g.sync.dma_start(T["SZ%d" % c][:], T["ZO%d" % s][:, a:b]).then_inc(S["d%d" % (10 + c)], 16)
        g.wait_ge(S["d%d" % (10 + c)], 16)
        deal(plan, "SZ%d" % c, "LZ%d" % c, "a_f%d" % c, 2)
    g.wait_ge(S["d0"], sent[0])


def rank_program(g, core, T, topo):
    rank = T.rank_of(core)
    if rank is None:
        helper_program(g, core, T, topo)
        return
    ring = diag_ring(T, topo)
    k = ring.index(rank)
    dcore = [T.cores[ring[d]] for d in range(8)]
    ops = []

    def ap(v):
        if v[0] == "*":
            return ap(v[1]).indirect(ap(v[2]))
        return T[v[0]][v[1]]

    def sc(s):
        return ap(s) if isinstance(s, tuple) else s

    def rec(q, fn, outs, ins, grp=None, n=1):
        rd, wr = [], []
        for v in ins:
            if isinstance(v, tuple):
                rd += [region(v[1]), region(v[2])] if v[0] == "*" else [region(v)]
        for v in outs:
            if v[0] == "*":
                wr.append(region(v[1]))
                rd.append(region(v[2]))
            else:
                wr.append(region(v))
        ops.append({"q": q, "fn": fn, "rd": rd, "wr": wr, "grp": grp, "n": n})

    def tt(o, a, b, op):
        rec("v", lambda: g.vector.tensor_tensor(ap(o), ap(a), ap(b), op), [o], [a, b])

    def ts(o, a, s1, op0, s2=None, op1=None):
        if op1 is None:
            rec("v", lambda: g.vector.tensor_scalar(ap(o), ap(a), sc(s1), None, op0), [o], [a, s1])
        else:
            rec("v", lambda: g.vector.tensor_scalar(ap(o), ap(a), sc(s1), sc(s2), op0, op1), [o], [a, s1, s2])

    def cp(o, a):
        rec("v", lambda: g.vector.tensor_copy(ap(o), ap(a)), [o], [a])

    def fill(o, val):
        rec("v", lambda: g.vector.memset(ap(o), val), [o], [])

    def act(o, a, f=AF.Identity, bias=0.0, scale=1.0):
        rec("a", lambda: g.scalar.activation(ap(o), ap(a), f, bias=sc(bias), scale=sc(scale)), [o], [a, bias, scale])

    def mm(o, l, r, st, sp):
        rec("p", lambda: g.tensor.matmul(ap(o), ap(l), ap(r), st, sp), [o], [l, r])

    def dma(q, o, a, grp, slow=False):
        eng = {"s": g.sync, "a": g.scalar, "g": g}[q]
        if slow:
            rec(q, lambda: eng.dma_start(ap(o), ap(a), allow_slow_non_contiguous=True), [o], [a], grp, 16)
        else:
            rec(q, lambda: eng.dma_start(ap(o), ap(a)), [o], [a], grp, 16)

    def iota(o, pat, base, cm, small=False):
        if small:
            rec("g", lambda: g.iota(ap(o), pat, base, cm, allow_small_or_imprecise_dtypes=True), [o], [])
        else:
            rec("g", lambda: g.iota(ap(o), pat, base, cm), [o], [])

    def arrive(name, outs, n):
        rec(None, None, outs, [], name, n)

    def send(dst, o, a, name):
        rid, pid, _ = topo.addr(dst)
        m = topo.mask(core, dst)
        n = len(topo.engines(core, dst))
        rec("r", lambda ls: g.remote_dma(ap(o), ap(a), T.sem[name], ls, pid, rid, m), [], [a], "t" + name, n)
        return n

    def fused(name, tr):
        rec("r", lambda ls: g.remote_dma_fused(
            [RemoteDMATransfer(dst_ids=[dst_id(topo, c)], dma_engine_mask=sum(1 << e for e in es), remote_sem=T.sem[sem],
                               src=ap(a), dst=ap(o)) for c, es, sem, a, o in tr], local_sem=ls),
            [], [t[3] for t in tr], "t" + name, sum(len(t[1]) for t in tr))

    def deal(name, src, dst, plan, q="s", stage=None, own_src=None):
        tr = []
        if stage:
            dma(q, V(src), stage, "s" + name)
        for c, i, j in plan:
            if c == core:
                dma(q, V(dst, j), own_src(i) if own_src else V(src, i), "l" + name)
                own = j
            else:
                tr.append((c, [topo.engines(core, c)[len(tr)]], name, V(src, i), V(dst, j)))
        fused(name, tr)
        arrive(name, [V(dst, j) for j in range(8) if j != own], len(tr))

    def relay(name, src, dst, dies):
        way = routes(T, topo, core, dies)
        fused(name, [(who, [topo.engines(core, who)[e]], "h_" + name, V(src, i), V(src, i))
                     for e, (who, c, i, j) in enumerate(way) if who != core])
        own = [(i, j) for who, c, i, j in way if who == core]
        for i, j in own:
            dma("s", V(dst, j), V(src, i), "l" + name)
        arrive("a_" + name, [V(dst, j) for j in range(len(way)) if j not in [o[1] for o in own]],
               sum(x_width(routes(T, topo, o, dies), who, o) for o in T.cores if o != core
                   for who, c, i, j in routes(T, topo, o, dies) if c == core))

    def spread(name, cores, a):
        rec("r", lambda ls: g.remote_dma_fused(
            [RemoteDMATransfer(dst_ids=[dst_id(topo, c) for c in cores], dma_engine_mask=topo.mask(core, cores[0]),
                               remote_sem=T.sem[name], src=ap(a), dsts=[ap(a)] * len(cores))], local_sem=ls),
            [], [a], "t" + name, len(topo.engines(core, cores[0])))

    folds = []

    def fold(name):
        tr = list(folds)
        del folds[:]
        rec("r", lambda ls: g.remote_dma_fused(
            [RemoteDMATransfer(dst_ids=[dst_id(topo, c) for c in cs], dma_engine_mask=sum(1 << e for e in es), remote_sem=T.sem[name],
                               srcs=[ap(a) for a in srcs], dsts=[ap(o)] * len(cs), alu_op=1) for cs, es, srcs, o in tr], local_sem=ls),
            [], [a for t in tr for a in t[2]], "t" + name, sum(len(t[1]) for t in tr))

    (PP, G16, GG, LT8, ODD, EVN, CTB, SRB, F21, WF, WB, T0, T1, T3, SMK, LE8, NLE8, HF8, SU, SV, C4, C5) = range(22)

    def col(f, n=1):
        return C("PC", f, f + n)

    def row(i):
        return C("EE", i, i + 1)

    def pair(i):
        return C("EE", 16 + i, 17 + i)

    def wrap(out, f, src, first=True, last=True):
        for q in range(16):
            mm(out, C("ZM", 144 * f + 15 - q, 144 * f + 143 - q), C(src, q, 1024, 16), first and q == 0, last and q == 15)

    def mat(i, m=128):
        return C("MM", 128 * i, 128 * i + m)
    I1, ONES, SELU, SELV, DH, DHN, EO, EN_, C40 = range(9)

    def grp(gm, a, b):
        return slice(16 * (gm % 8) + a, 16 * (gm % 8) + b)

    def rows_to_slots(q, dst, r1, src, r0, name, mid=True, side=True, c0=0, d0=0):
        cs = slice(c0, c0 + 4096 - d0)
        if side:
            dma(q, V(dst, slice(16 + r1, 128, 16), slice(d0, 4096)), V(src, slice(r0, 112, 16), cs), name)
            dma(q, V(dst, slice(r1, 112, 16), slice(8192 + d0, 12288)), V(src, slice(16 + r0, 128, 16), cs), name)
            dma(q, V(dst, slice(r1, r1 + 1), slice(d0, 4096)), V(src, slice(112 + r0, 113 + r0), cs), name)
            dma(q, V(dst, slice(112 + r1, 113 + r1), slice(8192 + d0, 12288)), V(src, slice(r0, r0 + 1), cs), name)
        if mid:
            dma(q, V(dst, slice(r1, 128, 16), slice(4096 + d0, 8192)), V(src, slice(r0, 128, 16), cs), name)

    in_plan = input_plan(T, ring, rank)
    nb = [dcore[(k - 1) % 8], dcore[(k + 1) % 8]]
    src_nb = [nb[1], nb[0]]
    near = helpers(T, topo, core)[1]
    near = near[1] + near[0]
    carry = carriers(T, topo, core)
    wide = len(topo.engines(core, near[0]))

    def nin(c):
        return len(topo.engines(c, core))

    MSL, NB1, NB2, TL = 0, 64, 128, 192
    CQ = float(512 + 512 * 1024)
    FB = C("W1", 4096, 8192)
    BIG = float(2 ** 21)
    MOVE = 16384.0
    R1 = 1.5 * 2 ** 23
    pm = C("PJ", 16, 17)
    n128 = C("IN", 0, 128)

    dma("a", V("SM"), V("ms"), "sm")
    dma("s", C("TI", 0, 512), C("cor", 0, 512), "ci0")
    dma("a", C("TI", 1024, 2048), V("fl"), "fi")
    dma("s", C("TI", 512, 1024), C("cor", 512, 1024), "ci1")
    fill(C("O0", 0, 512), 0.0)
    iota(C("PJ", 0, 16), [[-1, 16]], 16, 1)
    iota(V("IN"), [[1, 144]], 0, 0, True)
    spread("h_z", near, C("O0", 0, 512))
    deal("a_ms", "SM", "LM", in_plan, "a", own_src=lambda i: V("ms", grp(i, 0, 16)))
    ts(C("PJ", 16, 32), C("PJ", 0, 16), 15, AL.bitwise_and)
    ts(C("PJ", 32, 33), C("PJ", 0, 1), 1, AL.bitwise_and)
    ts(col(LT8), pm, 8.0, AL.is_lt)
    ts(C("EE", 0, 16), C("PJ", 16, 32), 0.0, AL.is_equal)
    ts(col(ODD), C("PJ", 32, 33), col(LT8), AL.mult)
    tt(col(EVN), col(LT8), col(ODD), AL.subtract)
    ts(C("KB", 0, 64), C("IN", 0, 64), col(ODD), AL.mult)
    ts(C("BC", 0, 65), C("IN", 0, 65), col(EVN), AL.mult, 64.0, AL.mult)
    for i in range(4):
        ts(C("KB", 64 << i, 128 << i), C("KB", 0, 64 << i), C("BC", 1 << i, (1 << i) + 1), AL.add)
    ts(col(F21), row(8), BIG, AL.mult)
    ts(col(SRB), row(8), BIG, AL.mult, C("BC", 64, 65), AL.add)
    ts(col(CTB), col(EVN), -512.0, AL.mult)
    ts(C("KB", 1024, 2048), C("KB", 0, 1024), C("BC", 16, 17), AL.add)
    act(C("KB", 2048, 4096), C("KB", 0, 2048), bias=C("BC", 32, 33))
    cp(C("CL", 0, 512), C("TI", 0, 512))
    deal("a_c0", "SC0", "LC0", in_plan, stage=C("CL", 0, 512), own_src=lambda i: V("CL", grp(i, 0, 16), slice(0, 512)))
    cp(C("CL", 512, 1024), C("TI", 512, 1024))
    dma("s", V("SC1"), C("CL", 512, 1024), "sc1")
    relay(*RELAYED[0])
    iota(C("JB", 0, 128), [[1, 8], [0, 16]], 0, 0, True)
    iota(C("JB", 128, 168), [[0, 5], [1, 8]], 0, 0, True)
    for h in range(2):
        fi = C("TI", 1024 + 512 * h, 1536 + 512 * h)
        ts(V("P%d" % (2 + h)), fi, 32 * R1, AL.add, 32 * R1, AL.subtract)
        tt(C("GB", 1024 + 512 * h, 1536 + 512 * h), fi, V("P%d" % (2 + h)), AL.subtract)
        act(C("GB", 512 * h, 512 * h + 512), V("P%d" % (2 + h)))
    for i in range(8):
        dma("sa"[i % 2], V("SF", slice(i // 4, 16, 2), slice(32 * (i % 4), 32 * (i % 4) + 32)),
            V("GB", slice(32 * (i // 2), 32 * (i // 2) + 32), slice(1024 * (i % 2), 1024 * (i % 2) + 1024)), "sf")
    dma("s", V("MI"), V("LM"), "mi")
    dma("s", C("CL", 0, 512), V("LC0"), "cl0")
    act(C("GB", 2048, 3072), C("KB", 0, 1024), bias=col(SRB))
    act(V("CT"), C("KB", 0, 1024), bias=col(CTB))
    relay(*RELAYED[1])
    tt(C("EE", 16, 24), C("EE", 0, 16, 2), C("EE", 1, 16, 2), AL.add)
    ts(C("PJ", 33, 34), C("PJ", 0, 1), 4, AL.arith_shift_right)
    ts(col(PP), C("PJ", 0, 1), -16.0, AL.add)
    ts(col(G16), C("PJ", 33, 34), 16.0, AL.mult, -1.0, AL.add)
    ts(col(GG), C("PJ", 33, 34), -1.0, AL.add)
    ts(col(SMK), pair(3), pair(4), AL.add)
    ts(col(C4), pair(5), pair(6), AL.add)
    ts(col(WF, 2), C("EE", 17, 20, 2), 1024.0, AL.mult, col(C4), AL.add)
    tt(col(WF, 2), col(WF, 2), C("EE", 16, 19, 2), AL.add)
    ts(C("ZM", 144 * 6, 144 * 7), V("IN"), col(G16), AL.is_equal)
    for buf in ("MS", "ST0"):
        fill(one(buf, 0, 0), 0.0)
        fill(one(buf, 1, 0), 2 * MOVE)
    ts(col(T0), pair(2), pair(4), AL.add, pair(7), AL.add)
    tt(col(T1, 2), C("EE", 19, 23, 3), C("EE", 18, 22, 3), AL.subtract)
    for f, w in enumerate((col(WF), col(WB), col(T0), col(T1), pair(5), col(T3))):
        act(C("ZM", 144 * f, 144 * f + 144), C("ZM", 144 * 6, 144 * 7), scale=w)
    ts(col(LE8), pm, 8.0, AL.is_le)
    ts(col(SU), row(1), 0.25, AL.mult)
    ts(col(SV), row(0), 1.0 / 512, AL.mult)
    ts(mat(I1), n128, col(PP), AL.is_equal)
    ts(mat(DH), mat(I1), col(LE8), AL.mult)
    ts(mat(DHN), mat(I1), col(LE8), AL.mult, -1.0, AL.mult)
    for buf, a, lo, hi in (("XB", SN1, 2.0 ** 12, 2.0 ** 17), ("XF", SN2, 2.0 ** 20, 2.0 ** 26)):
        fill(C(buf, a, a + 1), lo)
        fill(C(buf, a + 1, a + 2), hi)
    ts(C("PJ", 34, 35), pm, 1, AL.arith_shift_right)
    ts(col(HF8), col(LT8), 0.5, AL.mult)
    ts(col(C4), C("PJ", 34, 35), col(G16), AL.add, -15.0, AL.add)
    ts(col(C5), C("PJ", 34, 35), col(G16), AL.add, -11.0, AL.add)
    ts(C("P7", 0, 128), n128, col(C4), AL.is_equal, col(HF8), AL.mult)
    ts(C("GP", 0, 128), n128, col(C5), AL.is_equal, col(LT8), AL.mult)
    ts(mat(ONES), C("JB", 0, 128), col(GG), AL.is_equal)
    ts(mat(C40, 40), C("JB", 128, 168), col(GG), AL.is_equal)
    tt(mat(EO), C("P7", 0, 128), C("GP", 0, 128), AL.add)
    tt(mat(EN_), C("P7", 0, 128), C("GP", 0, 128), AL.subtract)
    act(mat(SELU), mat(ONES), scale=col(SU))
    act(mat(SELV), mat(ONES), scale=col(SV))
    cp(C("UL", MSL, MSL + 64), V("MI"))
    cp(IND(V("KB"), C("UL", MSL, MSL + 64)), C("GB", 2048, 3072))
    for q in range(4):
        dma("s", V("SX", slice(8 * q, 8 * q + 8)), C("x", 1024 * q, 1024 * q + 1024), "sx%d" % (q // 2))
    dma("s", C("CL", 512, 1024), V("LC1"), "cl1")
    way = x_routes(T, topo, core)
    for h in range(2):
        fused("x%d" % h, [(lay, [topo.engines(core, lay)[e]], "h_x", V("SX", i), V("LX", j)) if who == core else
                          (who, [topo.engines(core, who)[e]], "h_in", V("SX", i), V("SX", i))
                          for e, (who, lay, i, j) in enumerate(way[16 * h:16 * h + 16])])
    arrive("a_w1", [V("W1")], 24 * wide)
    arrive("a_w2", [C("W2", 0, 4096), C("W2", 8192, 12288)], 16 * wide)
    arrive("a_xb", [C("XB", 0, 12288)], 12 * wide)
    for gm in range(8):
        dma("s", V("W1", grp(gm, 0, 8), slice(4096, 8192)), V("LF", slice(2 * gm, 2 * gm + 2)), "f1")
    for gm in range(8):
        for sl in (0, 2):
            dma("s", V("W1", grp(gm, 2 * sl, 2 * sl + 4), slice(4096 * sl, 4096 * sl + 4096)),
                V("LF", 2 * ((gm + sl - 1) % 8) + sl // 2), "f2")

    def homes():
        ts(C("TI", 0, 64), V("MI"), 7, AL.arith_shift_right)
        ts(C("TI", 64, 128), V("MI"), 127, AL.bitwise_and)
        ts(one("HM", 0, 0), C("TI", 0, 64), 512.0, AL.mult, -192.0, AL.add)
        ts(one("HM", 0, 1), C("TI", 64, 128), 4.0, AL.mult, -1.5, AL.add)

    def late_constants():
        act(two("HM", 2), two("HM", 0), bias=131072.0)
        act(two("HM", 3), two("HM", 1), bias=1024.0)
        for i, (edge, back, on) in enumerate(((506.5, -128.0, 1.0), (128 * 122.5, -4096.0, 128.0))):
            ts(C("TI", 64 * i, 64 * i + 64), one("HM", 0, 1 - i), edge, AL.is_equal, back, AL.mult)
            tt(C("TI", 64 * i, 64 * i + 64), C("TI", 64 * i, 64 * i + 64), V("MI"), AL.add)
            ts(C("UL", NB1 + 64 * i, NB1 + 64 * i + 64), C("TI", 64 * i, 64 * i + 64), on, AL.add)

    def blk(buf, o, i, n=1):
        return C(buf, o + 64 * i, o + 64 * (i + n))
    TMP, DL, DXY, PR, BASE = 0, 1, 2, 4, 6

    def clip(x, y, off):
        ts(x, x, off - 1.5, AL.max, off + 509.5, AL.min)
        ts(y, y, 128 * (off - 1.5), AL.max, 128 * (off + 125.5), AL.min)

    def starts(rnd):
        t, fy, done, next_door = two("P1", 1), two("TF", TMP), two("P1", 2), two("P1", 3)
        if rnd:
            for s in (1, 0):
                ts(one("P1", s, 2), one("P1", 0, 2), 8.5, AL.is_ge)
            tt(two("TF", DL), two("TF", DL), next_door, AL.subtract)
            tt(two("P1", 0), two("TF", BASE), done, AL.mult)
            tt(fy, two("TF", DL), done, AL.mult)
            tt(two("MS", 0), two("MS", 0), two("P1", 0), AL.add)
            tt(t, fy, next_door, AL.add)
        ts(fy, t, 1024 * R1, AL.add, 1024 * R1, AL.subtract)
        ts(two("P1", 0), fy, 0.125, AL.mult)
        tt(t, t, fy, AL.subtract)
        tt(two("MS", 1, 2), two("HM", 0, 2), two("P1", 0, 2), AL.add)
        clip(two("MS", 2), two("MS", 1), 0)
        for s in (1, 0):
            a = 1 - rnd
            send(nb[s], one("ST%d" % rnd, s, a, 3 - a), one("MS", s, a, 3 - a), "a_st%d%d" % (rnd, s))
            arrive("a_st%d%d" % (rnd, s), [one("ST%d" % rnd, s, a, 3 - a)], nin(src_nb[s]))

    def bank(s, i):
        return one("P1", 0, i) if s else blk("P0", 0, i)

    def cells(part, pb_, buf, off):
        ts(pb_(1), part(buf, 2), 4 * R1, AL.add, 4 * R1, AL.subtract)
        ts(part("TF", TMP), part(buf, 1), 512 * R1, AL.add, 512 * R1, AL.subtract)
        tt(pb_(2), part(buf, 0), pb_(1), AL.add)
        tt(pb_(2), part("TF", TMP), pb_(2), AL.add)
        ts(part("LS", 0), pb_(2), 0.25, AL.mult, float(-129 * off // 4), AL.add)

    def step(rnd, s, h):
        src, t = "EM" if h else "ST%d" % rnd, one("FI", s, 3)
        wrap(bank(s, 0), s, "O%d" % s)
        ts(t, bank(s, 0), BIG / 2, AL.max, CQ, AL.add)
        ts(one("FI", s, 0), bank(s, 0), BIG / 2, AL.is_ge, (1 - 2 * s) * MOVE, AL.mult)
        ts(one("FI", s, 2), t, 1023, AL.bitwise_and)
        ts(one("FI", s, 1), t, 3, AL.arith_shift_right, 1023 * 128, AL.bitwise_and)
        tt(one("EM", s, 0, 3), one("FI", s, 0, 3), one(src, s, 0, 3), AL.add)
        off = 512 * (h + 1)
        clip(one("EM", s, 2), one("EM", s, 1), off)
        cells(lambda b, i: one(b, s, i), lambda i: bank(s, i), "EM", off)

    def ends(rnd, s):
        send(src_nb[s], one("EN", s, 0, 3), one("EM", s, 0, 3), "a_en%d%d" % (rnd, s))
        ts(one("SL", s, 0), one("EM", s, 0), (5120.0 if rnd else 4096.0) / MOVE, AL.mult)
        tt(bank(s, 1), one("EM", s, 2), bank(s, 1), AL.subtract)
        tt(one("TF", s, TMP), one("EM", s, 1), one("TF", s, TMP), AL.subtract)
        tt(bank(s, 1), one("TF", s, TMP), bank(s, 1), AL.add)
        ts(one("UV", s, 0), bank(s, 1), 512 + 1.5 * 129, AL.add)

    def look(s, win, on_act=True):
        i = IND(win, one("LS", s, 0))
        if on_act:
            act(V("O%d" % s), i)
        else:
            cp(V("O%d" % s), i)

    def taps_mm(s, bank, fields):
        for n, i in enumerate(fields):
            mm(blk(bank, 0, n), mat(I1), one("SL", s, 0), True, False)
            wrap(blk(bank, 0, n), 2 + i, "O%d" % s, False, True)

    def taps_list(rnd, s, bank, fields):
        a = TL + 256 * s + 64 * fields[0]
        ts(C("UL", a, a + 64 * len(fields)), C(bank, 0, 64 * len(fields)), float((SN2 if rnd else SN1) + s), AL.min)

    def own_scale(rnd):
        for s in range(2):
            arrive("a_en%d%d" % (rnd, s), [one("EN", s, 0, 3)], nin(nb[s]))
            act(one("P1", s, 0), one("EN", s, 0), AF.Relu, scale=(s - 0.5) / MOVE, bias=0.75 - s)
        act(two("P1", 0), two("P1", 0), bias=0.25)

    def own_parts():
        tt(two("TF", DXY, 2), two("EN", 1, 2), two("HM", 2, 2), AL.subtract)
        for i in range(2):
            tt(two("TF", PR + i), two("TF", DXY + i), two("P1", 0), AL.mult)
            act(two("TF", PR + i), two("TF", PR + i), scale=(1.0 / 128, 1.0)[i], bias=511.625)

    def own_lists():
        ts(two("OW", 0, 2), two("TF", PR, 2), R1, AL.add, R1, AL.subtract)

    def own_look(i):
        act(C("GB", 1024 * i, 1024 * i + 1024), IND(V("CT"), one("OW", i // 2, 1 - i % 2)), scale=pair(i))

    OB = (0, 7)

    def own_mm(rnd, h):
        mm(V("P%d" % OB[h]), mat(EN_ if rnd else DHN), C("NR", 512 * h, 512 * h + 512), True, False)
        for i in range(4):
            mm(V("P%d" % OB[h]), mat(EO if rnd else DH), C("GB", 1024 * i + 512 * h, 1024 * i + 512 * h + 512), False, i == 3)

    def widen(*js, on_pool=False):
        for i in js:
            b = 5120 * (i // 4) + 1024 * (i % 4)
            o, a = C("XF", b, b + 1024), C("XB", 1024 * i, 1024 * i + 1024)
            if on_pool:
                rec("g", lambda o=o, a=a: g.affine_select(ap(o), ap(a), [[0, 1024]], AL.is_ge, 0.0, 0, 0), [o], [a])
            else:
                act(o, a)

    def hb(n, c, p=ALL):
        return V(n, p, slice(CH[c][1], CH[c][2]))

    def wb(n, c):
        a = sum(e - b for s, b, e in CH[:c]) % 1024
        return C(n, a, a + CH[c][2] - CH[c][1])

    def pb(bank, c):
        return C("P%d" % bank, 0, CH[c][2] - CH[c][1])

    def pc(banks, c, p=ALL):
        return V("P%d" % banks[CH[c][1] // 512], p, slice(CH[c][1] % 512, (CH[c][2] - 1) % 512 + 1))

    def lst(base, c):
        return C("UL", base + CH[c][1] // 16, base + CH[c][2] // 16)

    FC = [c for c in range(NC) if CH[c][0] == 0]
    ZB = (3, 5)
    for rnd in range(2):
        win = FB if rnd else V("KB")
        abuf, a0 = ("KB", 0) if rnd else ("W2", 4096)
        for half, (buf, b0) in enumerate(((abuf, a0), ("GB", 0))):
            cuts = [0, 1024, 2048, 3072, 4096] if half else [0, 256, 768, 1792, 2944, 4096]
            for c in range(len(cuts) - 1):
                o = C(buf, b0 + cuts[c], b0 + cuts[c + 1])
                a, w = 512 * half + 256 + cuts[c] // 16, (cuts[c + 1] - cuts[c]) // 16
                act(o, IND(win, C("CL", a, a + w)), scale=col(SMK) if rnd == 0 else 1.0)
                if rnd == 0 and half == 1 and c == 0:
                    act(V("NR"), IND(FB, C("UL", MSL, MSL + 64)), scale=col(LT8))
                    for s in range(2):
                        wrap(one("P1", s, 1), s, "NR")
                if rnd == 1 and half == 1 and c == 3:
                    act(V("UU"), IND(win, C("CL", a - 256, a - 256 + w)))
                else:
                    tt(o, IND(win, C("CL", a - 256, a - 256 + w)), o, AL.add)
                if rnd == 0 and half == 0 and c == 0:
                    homes()
                if rnd == 0 and half == 0 and c == 2:
                    act(one("HM", 1, 0, 2), one("HM", 0, 0, 2))
                if rnd == 0 and half == 1 and c == 1:
                    starts(0)
                    dma("g", C("EP", 0, 1), V("eps"), "ep", True)
                if rnd == 1 and half == 0 and c == 3:
                    starts(1)
            if half == 0:
                rows_to_slots("s", "W1", 10, abuf, 8, "ma%d" % rnd, mid=False, c0=a0)
                if rnd == 1:
                    rows_to_slots("s", "W2", 8, abuf, 8, "wa2")
        rows_to_slots("s", "W1", 11, "GB", 8, "mb%d" % rnd, mid=False)
        if rnd:
            rows_to_slots("s", "W1", 12, "UU", 8, "mb1", d0=3072)
        rows_to_slots("a", "W1", 11, "GB", 8, "mb%d" % rnd, side=False)
        rows_to_slots("a", "W1", 10, abuf, 8, "mb%d" % rnd, side=False, c0=a0)
        if rnd:
            for h in range(2):
                act(V("P%d" % (4 + h)), hb("DF", 2 * h), scale=0.5)
            rows_to_slots("s", "W2", 14, "GB", 8, "wb2")
            rows_to_slots("s", "W2", 15, "UU", 8, "wb2", d0=3072)
        else:
            for gm in range(8):
                for sl in (0, 2):
                    dma("s", V("W2", grp(gm, 4, 9), slice(4096 * sl, 4096 * sl + 4096)),
                        V("W2", grp(gm + sl - 1, 4, 9), slice(4096, 8192)), "wa")
                for sl in range(3):
                    dma("s", V("W2", grp(gm, 10, 15), slice(4096 * sl, 4096 * sl + 4096)), V("GB", grp(gm + sl - 1, 4, 9)), "wb")
            late_constants()
        cells(two, lambda i: two("P1", i), "ST%d" % rnd, 0)
        if rnd:
            for h in range(2):
                tt(C("XF", 9216 + 512 * h, 9728 + 512 * h), hb("ZI1", 2 * h), V("P%d" % (4 + h)), AL.add)
            va = slice(9216, 10240)
            dma("s", V("XF", slice(16, 128), slice(4096, 5120)), V("XF", slice(0, 112), va), "vs")
            dma("s", V("XF", slice(0, 112), slice(14336, 15360)), V("XF", slice(16, 128), va), "vs")
            dma("s", V("XF", slice(0, 16), slice(4096, 5120)), V("XF", slice(112, 128), va), "vs")
            dma("s", V("XF", slice(112, 128), slice(14336, 15360)), V("XF", slice(0, 16), va), "vs")
        look(1, V("W1"))
        look(0, V("W1"), False)
        a = NB2 if rnd else NB1
        act(V("NR"), IND(FB, C("UL", a, a + 64)), scale=col(LT8), bias=col(F21))
        if rnd:
            fill(V("ZI0", slice(32, 64)), 0.5)
        step(rnd, 1, 0)
        look(1, V("W1"))
        step(rnd, 0, 0)
        look(0, V("W1"))
        if rnd:
            fill(V("ZI1", slice(32, 64)), 1.0)
        step(rnd, 1, 1)
        look(1, V("W2"))
        ends(rnd, 1)
        step(rnd, 0, 1)
        taps_mm(1, "P6", [0, 1])
        look(0, V("W2"), False)
        taps_list(rnd, 1, "P6", [0, 1])
        ends(rnd, 0)
        if rnd == 0:
            ts(V("EW"), C("IN", 0, 16), 0.0, AL.mult, C("EP", 0, 1), AL.add)
            deal("a_eps", "SE", "LE", in_plan, stage=V("EW"), own_src=lambda i: V("EW", grp(i, 0, 16)))
        xw = C("XF", 0, SN2 + 2) if rnd else C("XB", 0, SN1 + 2)

        def take(c, i):
            act(wb(("A0", "A2")[i], c), IND(xw, lst(TL + 256 * CH[c][0] + 128 * i, c)))

        def parts(c):
            act(wb("UU", c), IND(V("CT"), V("UV", ALL, CH[c][0], slice(CH[c][1] // 16, CH[c][2] // 16))))
            mm(pb(2 + c % 2, c), mat(SELU), wb("UU", c), True, True)
            mm(pb(4 + c % 2, c), mat(SELV), wb("UU", c), True, True)

        def fetch(c):
            take(c, 0)
            parts(c)
            take(c, 1)

        def diff(c, i):
            s = CH[c][0]
            tt(wb(("D0", "D2")[i], c), IND(xw, lst(TL + 256 * s + 64 + 128 * i, c)), wb(("A0", "A2")[i], c), AL.subtract)

        taps_mm(1, "P7", [2, 3])
        if rnd == 0:
            widen(0, 1, 2, on_pool=True)
        take(0, 0)
        parts(0)
        diff(0, 0)
        taps_list(rnd, 1, "P7", [2, 3])
        take(0, 1)
        own_scale(rnd)
        taps_mm(0, "P0", [0, 1])
        taps_mm(0, "P7", [2, 3])
        tt(pb(6, 0), wb("D0", 0), pb(2, 0), AL.mult)
        diff(0, 1)
        for c in range(NC):
            s = CH[c][0]
            late = c >= EARLY if rnd == 0 else not carry[c]
            U, W, M, Z = pb(2 + c % 2, c), pb(4 + c % 2, c), pb(6, c), hb("ZO%d" % s, c)
            tt(U, wb("D2", c), U, AL.mult)
            sb = ("SS", "GP")[s]
            tt(hb(sb, c), wb("A0", c), M, AL.add)
            if c == 0:
                taps_list(rnd, 0, "P0", [0, 1])
                take(1, 0)
                parts(1)
            tt(U, wb("A2", c), U, AL.add)
            if c == 0:
                own_parts()
            if c < NC - 1:
                diff(c + 1, 0)
            tt(wb("D2", c), U, hb(sb, c), AL.subtract)
            if c == 0:
                taps_list(rnd, 0, "P7", [2, 3])
                take(1, 1)
                own_lists()
                tt(Z, wb("D2", c), W, AL.mult)
            if c < NC - 1:
                diff(c + 1, 1)
            if late:
                tt(W, wb("D2", c), W, AL.mult)
            if c < NC - 1:
                tt(pb(6, c + 1), wb("D0", c + 1), pb(3 - c % 2, c + 1), AL.mult)
            if late:
                tt(Z, hb(sb, c), W, AL.add)
            elif c:
                tt(Z, wb("D2", c), W, AL.mult)
            if rnd == 0 and c < EARLY:
                m = (CH[c][1] + CH[c][2]) // 2
                for i, o in enumerate(relays(T, topo, core, src_nb[s], c)):
                    a, b = ((CH[c][1], m), (m, CH[c][2]))[i]
                    folds.append(([o], topo.engines(core, o)[i::2], [C(sb, a, b), C("ZO%d" % s, a, b)], C("ZO%d" % s, a, b)))
                fold("h_r%d" % c)
                arrive("a_z%d" % c, [hb("ZI%d" % s, c)], 2 * nin(nb[s]))
            elif rnd == 0:
                send(src_nb[s], hb("ZI%d" % s, c), Z, "a_z%d" % c)
                arrive("a_z%d" % c, [hb("ZI%d" % s, c)], nin(nb[s]))
            elif not late:
                folds.append((carry[c], topo.engines(core, carry[c][0]), [hb(sb, c), Z], Z))
                fold("h_f%d" % c)
                arrive("a_f%d" % c, [V("LZ%d" % c)], 16)
            else:
                deal("a_f%d" % c, "SZ%d" % c, "LZ%d" % c, final_plan(T, k, s), stage=Z,
                     own_src=lambda i: hb("ZO%d" % s, c, grp(i, 0, 16)))
            if c < NC - 2:
                fetch(c + 2)
            for i in (((0,), (1,), (2, 3), (), ()), ((0, 1), (2, 3), (), (), ()))[rnd][c]:
                own_look(i)
            if c == 2 - rnd:
                own_mm(rnd, 0)
                own_mm(rnd, 1)
            if c == 1:
                if rnd == 0:
                    dma("s", V("ED"), V("LE"), "ed")
                    act(two("TF", TMP), two("TF", DXY), scale=8.0)
            if c == 2 and rnd:
                dma("a", hb("GP", 0), V("LZ0"), "gb0")
                for h in range(2):
                    act(C("DF", 512 * h, 512 * h + 512), V("P%d" % OB[h]))
                for i in range(8):
                    dma("a", V("SH", ALL, slice(16 * i, 16 * i + 16)), V("DF", slice(i, 128, 16)), "sh")
            if c == 3 and rnd:
                es = topo.engines(core, carry[NC][0])
                fused("sh", [(carry[NC][0 if topo.may_write(carry[NC][0], o) else 1], es[i::8], "h_f%d" % NC, V("SH", i), V("SH", i))
                             for o, i, j in final_plan(T, k, 2)])
                arrive("a_mh", [V("LH")], 16)
            if rnd == 0 and c == 0:
                widen(3, 11, on_pool=True)
            if c == NC - 2:
                if rnd == 0:
                    act(V("P%d" % ZB[0]), hb("ZI1", 0))
                else:
                    dma("a", hb("A0", FC[0]), V("LZ%d" % FC[0]), "zf0")
                    act(V("P%d" % OB[0]), hb("GP", 0))
        if rnd == 0:
            def gap(c):
                tt(hb("DF", c), hb("ZI0", c), pc(ZB, c), AL.subtract)
                act(hb("GP", c), hb("DF", c), AF.Abs)

            def vote(c):
                ts(hb("O0", c), hb("GP", c), C("ED", 0, 1), AL.is_le)
                mm(pb(4 if c == 3 else 2, c), mat(ONES), hb("O0", c), True, True)

            def flag(c):
                act(hb("VV", c), pb(4 if c == 3 else 2, c), AF.Relu, bias=-8.0)
                act(hb("VV", c), hb("VV", c), AF.Sign)

            def put(c):
                tt(hb("O1", c), hb("VV", c), pc(OB, c), AL.mult)
                tt(IND(FB, lst(MSL, c)), hb("NR", c), hb("O1", c), AL.add)
            widen(7, 8, 9, 10, on_pool=True)
            gap(1)
            act(V("P%d" % ZB[1]), hb("ZI1", 2))
            tt(two("TF", DL), two("TF", DXY + 1), two("TF", TMP), AL.add)
            tt(two("TF", BASE), two("EN", 0), two("MS", 0), AL.subtract)
            vote(1)
            gap(3)
            ts(hb("VV", 1), pb(2, 1), 8.5, AL.is_ge)
            vote(3)
            flag(3)
            widen(4)
            put(1)
            gap(4)
            widen(5, 6)
            vote(4)
            put(3)
            ts(hb("VV", 4), pb(2, 4), 8.5, AL.is_ge)
            put(4)
            wrap(one("P1", 0, 2), 6, "O0")
            for s in range(2):
                wrap(one("P1", s, 3), s, "NR")
            for gm in range(8):
                for sl in (0, 2):
                    dma("s", V("W1", grp(gm, 2 * sl, 2 * sl + 4), slice(4096 * sl, 4096 * sl + 4096)),
                        V("W1", grp(gm + sl - 1, 2 * sl, 2 * sl + 4), slice(4096, 8192)), "f3")

    p40 = slice(0, 40)
    dma("s", hb("GP", 2), V("LZ2"), "gb1")
    for c in FC[1:]:
        dma("s", hb("A0", c), V("LZ%d" % c), "zf%d" % c)
    for i in range(8):
        dma("s", V(("ZI0", "ZI1")[i // 4], slice(8 * (i % 4), 8 * (i % 4) + 8)), V("LH", ALL, slice(16 * i, 16 * i + 16)), "mh")

    def gaps(c):
        tt(hb("A2", c), hb("A0", c), pc(OB, c), AL.subtract)
        act(hb("SS", c), hb("A2", c), AF.Abs)
        act(pb(4 + c % 2, c), hb("A2", c), scale=0.5)
        act(hb("DF", c), hb("SS", c), AF.Exp, scale=-1.0)
        dma("a", hb("ye", c), hb("DF", c), "oe%d" % c)
        if c == FC[0]:
            act(V("P%d" % OB[1]), hb("GP", 2))

    def sign(c):
        return one("P1", c - FC[1], 0, 4, p40) if c > FC[0] else V("P6", p40)

    def votes(c):
        ts(hb("O0", c), hb("SS", c), C("EP", 0, 1), AL.is_le)
        mm(pb(2 + c % 2, c), mat(ONES), hb("O0", c), True, True)
        mm(sign(c), mat(C40, 40), hb("O0", c), True, True)
        tt(pb(4 + c % 2, c), hb("GP", c), pb(4 + c % 2, c), AL.add)
        ts(hb("D2", c), pb(2 + c % 2, c), 8.5, AL.is_ge, 8.0, AL.mult)

    def stores(c):
        tt(hb("D0", c), pb(4 + c % 2, c), hb("D2", c), AL.min)
        dma("a", hb("y", c), hb("D0", c), "oy%d" % c)
        ts(sign(c), sign(c), 8.5, AL.is_ge, 0.5, AL.subtract)

    def flows(c):
        tt(sign(c), hb("ZI1", c, p40), sign(c), AL.mult)
        tt(hb("ZI0", c, p40), hb("ZI0", c, p40), sign(c), AL.add)
        dma("s", hb("yf", c), hb("ZI0", c, p40), "of%d" % c)

    gaps(FC[0])
    votes(FC[0])
    stores(FC[0])
    gaps(FC[1])
    votes(FC[1])
    gaps(FC[2])
    stores(FC[1])
    flows(FC[0])
    votes(FC[2])
    flows(FC[1])
    stores(FC[2])
    flows(FC[2])

    def meets(a, b):
        return a[0] == b[0] and a[2] < b[3] and b[2] < a[3] and not a[1].isdisjoint(b[1])

    def earlier(calls):
        seen, out = {}, []
        for i, o in enumerate(calls):
            dep = set()
            for kind in ("rd", "wr"):
                for r in o[kind]:
                    for j, wj, rj in seen.get(r[0], []):
                        pj = calls[j]
                        clash = (r[4] and pj["q"] != o["q"]) or ((wj or kind == "wr") and meets(r, rj))
                        if clash and not (o["q"] == "p" and pj["q"] == "p") and not (pj["grp"] and pj["grp"] == o["grp"]):
                            dep.add(j)
            out.append(dep)
            for kind in ("rd", "wr"):
                for r in o[kind]:
                    seen.setdefault(r[0], []).append((i, kind == "wr", r))
        return out

    deps, order, done, had, prev = earlier(ops), [], set(), {}, None

    def free_now(j):
        return all(d in done and d != prev and (ops[d]["q"] == "v" or d <= had.get(ops[d]["grp"] or ops[d]["q"], -1)) for d in deps[j])

    for i, o in enumerate(ops):
        if i in done:
            continue
        if o["q"] == "v" and prev in deps[i]:
            for j in [j for j in range(i + 1, min(i + AHEAD, len(ops))) if ops[j]["q"] == "v" and j not in done
                      and ops[j]["wr"][0][3] - ops[j]["wr"][0][2] <= 512 and free_now(j)][:1]:
                order.append(j)
                done.add(j)
        order.append(i)
        done.add(i)
        if o["q"] == "v":
            prev = i
            for d in deps[i]:
                key = ops[d]["grp"] or ops[d]["q"]
                had[key] = max(had.get(key, -1), d)
    ops = [ops[i] for i in order]

    total, semof, free = {}, {}, ["d%d" % i for i in range(95)]
    for o in ops:
        if o["grp"]:
            total[o["grp"]] = total.get(o["grp"], 0) + o["n"]
            if o["grp"] not in semof:
                semof[o["grp"]] = o["grp"] if o["q"] is None else free.pop(0)
    need = set()
    for o, dep in zip(ops, earlier(ops)):
        last = {}
        for j in dep:
            if not ops[j]["grp"]:
                last[ops[j]["q"]] = max(last.get(ops[j]["q"], -1), j)
        o["dep"] = (sorted(set(ops[j]["grp"] for j in dep if ops[j]["grp"])), last)
        if o["q"] is not None:
            need.update(last.values())
    eng = {"v": g.vector, "a": g.scalar, "p": g.tensor, "s": g.sync, "g": g, "r": g}
    cnt, idx, waited = {"v": 0, "a": 0, "p": 0, "g": 0}, {}, {}
    for i, o in enumerate(ops):
        q = o["q"]
        if q is None:
            continue
        qq = "g" if q == "r" else q
        ws = [(semof[n], total[n]) for n in o["dep"][0]] + [("e_" + e, idx[j]) for e, j in sorted(o["dep"][1].items())]
        for s, val in ws:
            if waited.get((qq, s), 0) < val:
                waited[(qq, s)] = val
                eng[q].wait_ge(T.sem[s], val)
        if q == "r":
            o["fn"](T.sem[semof[o["grp"]]])
        elif o["grp"]:
            o["fn"]().then_inc(T.sem[semof[o["grp"]]], 16)
        elif i in need:
            cnt[q] += 1
            idx[i] = cnt[q]
            o["fn"]().then_inc(T.sem["e_" + q], 1)
        else:
            o["fn"]()
    for n in sorted(total):
        if waited.get(("g", semof[n]), 0) < total[n]:
            g.wait_ge(T.sem[semof[n]], total[n])
    for e in cnt:
        if cnt[e]:
            g.wait_ge(T.sem["e_" + e], cnt[e])
